import numpy as np
import ml_dtypes


def mxq(x, axis, fmt="e4m3"):
    dtype, down = {"e4m3": (ml_dtypes.float8_e4m3fn, 7), "e5m2": (ml_dtypes.float8_e5m2, 14)}[fmt]
    v = np.moveaxis(np.asarray(x, np.float32).astype(ml_dtypes.bfloat16).astype(np.float64), axis, -1)
    blocks = v.reshape(v.shape[:-1] + (-1, 32))
    amax = np.abs(blocks).max(-1, keepdims=True)
    byte = np.maximum(np.where(amax > 0, np.frexp(amax)[1] - 1 + 127, 0) - down, 1)
    scale = np.exp2(byte - 127.0)
    codes = (blocks / scale).astype(np.float32).astype(dtype).astype(np.float64)
    return np.moveaxis((codes * scale).reshape(v.shape), -1, axis)


WIDE = False


def mx_kscale(k):
    if not WIDE:
        return np.ones(k)
    levels = np.array([24, -24, 12, -12, 0])
    if k % 512:
        return np.exp2(np.random.permutation(np.resize(levels, k // 32))).repeat(32)
    a = np.empty((k // 512, 16))
    for p in range(k // 512):
        a[p, :8] = np.random.permutation(np.resize(levels, 8))
        for g in range(8):
            far = levels[np.abs(levels - a[p, g]) >= 10]
            a[p, g + 8] = far[np.random.randint(len(far))]
    return np.exp2(a.ravel()).repeat(32)


def f64(x):
    return np.asarray(x).astype(np.float64)


def striped(idx):
    return np.tile(idx.reshape(-1, 16).T, (8, 1)).astype(np.uint16)


def unstriped(offs):
    return offs[:16].T.reshape(-1).astype(np.int64)


E2M1 = np.array([0.0, 0.5, 1.0, 1.5, 2.0, 3.0, 4.0, 6.0, -0.0, -0.5, -1.0, -1.5, -2.0, -3.0, -4.0, -6.0])


def pack_weight(w, fmt):
    k, n = w.shape
    w = f64(np.asarray(w, np.float32).astype(ml_dtypes.bfloat16)).reshape(k // 32, 32, n)
    amax = np.abs(w).max(1)
    if fmt == "e4m3":
        byte = np.frexp(amax)[1] - 1 + 127 - 7
    else:
        mant, ex = np.frexp(amax / 6.0)
        byte = np.where(mant > 0.5, ex, ex - 1) + 127
    byte = np.clip(np.where(amax > 0, byte, 1), 1, 254)
    scaled = (w * np.exp2(127.0 - byte)[:, None, :]).reshape(k, n).astype(np.float32)
    by_word = np.ascontiguousarray(scaled.reshape(k // 512, 128, 4, n).transpose(0, 1, 3, 2))
    if fmt == "e4m3":
        words = by_word.astype(ml_dtypes.float8_e4m3fn).view(np.uint8)
    else:
        c = by_word.astype(ml_dtypes.float4_e2m1fn).view(np.uint8) & 0xF
        words = (c[..., 0::2] | (c[..., 1::2] << 4)).reshape(k // 512, 128, 2 * n)
    return np.ascontiguousarray(words), np.ascontiguousarray(byte.astype(np.uint8).reshape(k // 512, 16, n))


def unpack_weight(words, scales, fmt):
    g, _, n = scales.shape
    words = np.ascontiguousarray(words).reshape(g, 128, n, -1)
    if fmt == "e4m3":
        vals = words.view(ml_dtypes.float8_e4m3fn).astype(np.float64)
    else:
        nib = np.empty((g, 128, n, 4), np.uint8)
        nib[..., 0::2] = words & 0xF
        nib[..., 1::2] = words >> 4
        vals = E2M1[nib]
    vals = vals * np.repeat(np.exp2(scales.astype(np.float64) - 127.0), 8, axis=1)[..., None]
    return vals.transpose(0, 1, 3, 2).reshape(g * 512, n)


K, R, N, T, J = 1024, 1024, 512, 2048, 1024


def setup_inputs():
    n = np.random.standard_normal
    s = mx_kscale(K)[:, None]
    u = mx_kscale(R)[:, None]
    p_tab = pack_weight(n((K, T)) * s, "e4m3")
    p_ws = pack_weight(n((K, R)) / np.sqrt(2 * K) / s * u.T, "e2m1")
    p_wd = pack_weight(n((R, N)) / np.sqrt(R) / u, "e2m1")
    return {
        "tab_words": p_tab[0],
        "tab_scales": p_tab[1],
        "ws_words": p_ws[0],
        "ws_scales": p_ws[1],
        "wt": (n((K, R)) / np.sqrt(2 * K) / s * u.T).astype(np.float32),
        "wd_words": p_wd[0],
        "wd_scales": p_wd[1],
        "wgo": np.tile(np.random.uniform(0.5, 2.0, J), (128, 1)).astype(np.float32),
        "offs": striped(np.random.permutation(T)[:J]),
        "offs2": striped(np.random.permutation(T)[:J]),
    }


def reference(tab_words, tab_scales, ws_words, ws_scales, wt, wd_words, wd_scales, wgo, offs, offs2):
    idx = unstriped(offs)
    idx2 = unstriped(offs2)
    tab_ = unpack_weight(tab_words, tab_scales, "e4m3")[:, idx]
    tabb_ = unpack_weight(tab_words, tab_scales, "e4m3")[:, idx2]
    ws_ = unpack_weight(ws_words, ws_scales, "e2m1")
    wt_ = mxq(f64(wt), 0, "e4m3")
    a = ws_.T @ tab_ + wt_.T @ tabb_
    h = np.maximum(a, 0.0)
    h_ = mxq(h, 0, "e4m3")
    wd_ = unpack_weight(wd_words, wd_scales, "e2m1")
    y = wd_.T @ h_
    out = np.zeros((N, T))
    out[:, idx2] = f64(wgo)[0] * (y)
    return out

@@ -1,0 +1,289 @@
+from contextlib import ExitStack
+
+import concourse.mybir as mybir
+from concourse.masks import make_identity
+
+K, R, N, T, J = 1024, 1024, 512, 2048, 1024
+FLOPS = 2 * (2 * K * R * J + R * N * J)
+
+F32 = mybir.dt.float32
+BF16 = mybir.dt.bfloat16
+I32 = mybir.dt.int32
+U32 = mybir.dt.uint32
+U16 = mybir.dt.uint16
+U8 = mybir.dt.uint8
+FP8X4 = mybir.dt.float8_e4m3fn_x4
+FP4X4 = mybir.dt.float4_e2m1fn_x4
+COPY = mybir.ActivationFunctionType.Copy
+RELU = mybir.ActivationFunctionType.Relu
+MULT = mybir.AluOpType.mult
+
+P = 128
+HALF = 512
+GROUP = 16
+CHUNK = 256
+GATHER_CUTS = [(0, 256), (256, 512), (512, 1024)]
+SCALAR_COLS = {(0, 0): 512, (0, 1): 512, (1, 0): 192, (1, 1): 192}
+
+
+def tile_list_msg_relu_none_kernel(
+    tc, tab_words, tab_scales, ws_words, ws_scales, wt, wd_words, wd_scales, wgo, offs, offs2, out
+):
+    nc = tc.nc
+    with ExitStack() as ctx:
+        lists = ctx.enter_context(tc.tile_pool(name="lists", bufs=1))
+        keep = ctx.enter_context(tc.tile_pool(name="keep", bufs=1))
+        shared = ctx.enter_context(tc.tile_pool(name="shared", bufs=1))
+        psum = ctx.enter_context(tc.psum_pool(name="psum", bufs=1))
+
+        offsets = {"grouped00":0,"src_w0_2":0,"grouped01":4096,"dst_sc_2":4096,"grouped11":8192,"src_sc0_2":8192,"src_sc1_2":8704,"h_in000":12288,"dst_w1_2":12288,"h_in011":14336,"src_w1_2":14336}
+
+        def held(name, shape, dtype):
+            if name in offsets:
+                return shared.tile(shape, dtype, name=name, align_bytes=64, offset=offsets[name])
+            return keep.tile(shape, dtype, name=name, align_bytes=64)
+
+        banks = [psum.tile([P, HALF], F32, name="bank%d" % i) for i in range(8)]
+
+        src_list = lists.tile([P, J // GROUP], U16, name="src_list")
+        dst_list = lists.tile([P, J // GROUP], U16, name="dst_list")
+        nc.sync.dma_start(src_list[:], offs)
+        nc.sync.dma_start(dst_list[:], offs2)
+
+        tab_sc_one = held("tab_sc_one", [P, T], U8)
+        tab_sc_both = held("tab_sc_both", [P, T], U8)
+        nc.vector.memset(tab_sc_both[:].bitcast(I32), 0)
+        nc.vector.memset(tab_sc_one[:].bitcast(I32), 0)
+
+        ident = held("ident", [P, P], F32)
+        make_identity(nc, ident[:])
+        ws_sc = held("ws_sc", [P, 2, R], U8)
+        wd_sc = held("wd_sc", [P, 2, N], U8)
+        nc.vector.memset(ws_sc[:].bitcast(I32), 0)
+        nc.vector.memset(wd_sc[:].bitcast(I32), 0)
+        placed = [held("placed%d" % n, [P, T], F32) for n in range(4)]
+        for n in range(4):
+            for c in range(0, T, 256):
+                nc.gpsimd.memset(placed[n][:, c : c + 256], 0.0)
+
+        wt_raw, tab_w, ws_w = {}, {}, {}
+
+        def load_wt(b, a):
+            wt_raw[b, a] = held("wt_raw%d%d" % (b, a), [P, 4, HALF], F32)
+            rows = wt[a * HALF : (a + 1) * HALF, b * HALF : (b + 1) * HALF]
+            nc.sync.dma_start(wt_raw[b, a][:], rows.rearrange("(p i) c -> p i c", i=4))
+
+        def load_tab(a):
+            tab_w[a] = held("tab_w%d" % a, [P, T], U32)
+            nc.sync.dma_start(tab_w[a][:].bitcast(I32), tab_words[a].rearrange("p t i -> p (t i)").bitcast(I32))
+
+        def load_ws_all():
+            both_halves = held("ws_w", [P, 2, 4 * HALF], U8)
+            nc.sync.dma_start(both_halves[:].bitcast(I32), ws_words.rearrange("a p x -> p a x").bitcast(I32))
+            for b in range(2):
+                ws_w[b] = both_halves[:, :, 2 * HALF * b : 2 * HALF * (b + 1)]
+
+        def load_ws(b):
+            ws_w[b] = held("ws_w%d" % b, [P, 2, 2 * HALF], U8)
+            cols = ws_words[:, :, 2 * HALF * b : 2 * HALF * (b + 1)]
+            nc.sync.dma_start(ws_w[b][:].bitcast(I32), cols.rearrange("a p x -> p a x").bitcast(I32))
+
+        def load_scale_rows(plane, rows):
+            for q in range(4):
+                nc.sync.dma_start(
+                    plane[32 * q : 32 * q + 4, :, :].bitcast(I32),
+                    rows[:, 4 * q : 4 * q + 4, :].rearrange("a r n -> r a n").bitcast(I32),
+                )
+
+        def load_both():
+            for q in range(4):
+                nc.sync.dma_start(
+                    tab_sc_both[32 * q : 32 * q + 8, :].bitcast(I32), tab_scales[:, 4 * q : 4 * q + 4, :].bitcast(I32)
+                )
+
+        def load_one():
+            for q in range(4):
+                nc.sync.dma_start(
+                    tab_sc_one[32 * q : 32 * q + 4, :].bitcast(I32), tab_scales[1, 4 * q : 4 * q + 4, :].bitcast(I32)
+                )
+
+        load_tab(0)
+        load_both()
+        load_wt(0, 0)
+        load_one()
+        load_wt(0, 1)
+        load_tab(1)
+        load_scale_rows(ws_sc, ws_scales)
+        load_ws_all()
+        load_wt(1, 0)
+        load_wt(1, 1)
+        load_scale_rows(wd_sc, wd_scales)
+        wd_w = held("wd_w", [P, 2, 2 * N], U8)
+        nc.sync.dma_start(wd_w[:].bitcast(I32), wd_words.rearrange("a p x -> p a x").bitcast(I32))
+        gain = held("gain", [P, J], F32)
+        nc.sync.dma_start(gain[:], wgo)
+
+        wt_w, wt_sc = {}, {}
+        for b in range(2):
+            for a in range(2):
+                grouped = held("grouped%d%d" % (b, a), [P, HALF, 4], BF16)
+                split = SCALAR_COLS[b, a]
+                nc.scalar.activation(
+                    grouped[:, 0:split, :].rearrange("p (c u) i -> p c i u", u=4),
+                    wt_raw[b, a][:, :, 0:split].rearrange("p i (c u) -> p c i u", u=4),
+                    COPY,
+                )
+                if split < HALF:
+                    nc.vector.tensor_copy(
+                        grouped[:, split:HALF, :].rearrange("p (c u) i -> p c i u", u=4),
+                        wt_raw[b, a][:, :, split:HALF].rearrange("p i (c u) -> p c i u", u=4),
+                    )
+                wt_w[b, a] = held("wt_w%d%d" % (b, a), [P, HALF], U32)
+                wt_sc[b, a] = held("wt_sc%d%d" % (b, a), [P, HALF], U8)
+                nc.vector.quantize_mx(
+                    out=wt_w[b, a][:].bitcast(FP8X4),
+                    scales=wt_sc[b, a][:],
+                    in_=grouped[:].rearrange("p c i -> p (c i)"),
+                )
+
+        picked = {}
+
+        def gather(name, g, window, edge_list, dtype):
+            j0, j1 = GATHER_CUTS[g]
+            picked[name, g] = held("%s_%d" % (name, g), [P, j1 - j0], dtype)
+            nc.vector.tensor_copy(picked[name, g][:], window[:].indirect(edge_list[:, j0 // GROUP : j1 // GROUP]))
+
+        sources = {
+            "dst_w0": (tab_w[0], dst_list, U32),
+            "src_w0": (tab_w[0], src_list, U32),
+            "dst_sc": (tab_sc_both, dst_list, U8),
+            "src_sc0": (tab_sc_both, src_list, U8),
+            "src_sc1": (tab_sc_one, src_list, U8),
+            "dst_w1": (tab_w[1], dst_list, U32),
+            "src_w1": (tab_w[1], src_list, U32),
+        }
+
+        def gather_all(g, names):
+            for name in names:
+                gather(name, g, *sources[name])
+
+        tiles = J // P
+        relu = [held("relu%d" % t, [P, 2, HALF], BF16) for t in range(tiles)]
+        h_w = [held("h_w%d" % c, [P, 2, CHUNK], U32) for c in range(4)]
+        h_sc = [held("h_sc%d" % c, [P, 2, CHUNK], U8) for c in range(4)]
+        msgs = {}
+
+        def first_layer(t, b, bank, on_vector=False):
+            g = [i for i, (j0, j1) in enumerate(GATHER_CUTS) if j0 <= t * P < j1][0]
+            at = t * P - GATHER_CUTS[g][0]
+            cols = slice(at, at + P)
+            acc = banks[bank]
+
+            def target_pass(a):
+                return (picked["dst_w%d" % a, g][:, cols].bitcast(FP8X4), picked["dst_sc", g][4 * a : P, cols],
+                        wt_w[b, a][:].bitcast(FP8X4), wt_sc[b, a][:])
+
+            def source_pass(a):
+                return (picked["src_w%d" % a, g][:, cols].bitcast(FP8X4), picked["src_sc%d" % a, g][:, cols],
+                        ws_w[b][:, a, :].bitcast(FP4X4), ws_sc[:, a, b * HALF : (b + 1) * HALF])
+
+            if b == 0:
+                passes = [target_pass(0), source_pass(0), source_pass(1), target_pass(1)]
+            else:
+                passes = [source_pass(0), source_pass(1), target_pass(0), target_pass(1)]
+            for i, (lhs, lhs_sc, rhs, rhs_sc) in enumerate(passes):
+                nc.tensor.matmul_mx(out=acc[:], lhsT=lhs, lhsT_scale=lhs_sc, rhs=rhs, rhs_scale=rhs_sc,
+                                    start=(i == 0), stop=(i == len(passes) - 1))
+            dst = relu[t][:, b, :].rearrange("p (u m e) -> p u m e", u=2, e=2)
+            sums = acc[:].rearrange("p (m u e) -> p u m e", u=2, e=2)
+            if on_vector:
+                nc.vector.tensor_scalar_max(dst, sums, 0.0)
+            else:
+                nc.scalar.activation(dst, sums, RELU)
+
+        def turn_and_quantise(c, b, bank, t0=0, t1=2):
+            turned = banks[bank]
+            for t in reversed(range(t0, t1)):
+                pairs = relu[2 * c + t][:, b, :].bitcast(F32)
+                for u in range(2):
+                    at = (2 * (t - t0) + u) * P
+                    nc.tensor.transpose(turned[:, at : at + P], pairs[:, u * P : (u + 1) * P], ident[:])
+            h_in = held("h_in%d%d%d" % (c, b, t0), [P, t1 - t0, P, 2], F32)
+            nc.scalar.copy(h_in[:], turned[:, 0 : 2 * P * (t1 - t0)].rearrange("p (t u j) -> p t j u", j=P, u=2))
+            nc.vector.quantize_mx(
+                out=h_w[c][:, b, t0 * P : t1 * P].bitcast(FP8X4),
+                scales=h_sc[c][:, b, t0 * P : t1 * P],
+                in_=h_in[:].rearrange("p t j u -> p (t j u)").bitcast(BF16),
+            )
+
+        def second_layer(units, bank):
+            y = banks[bank]
+            for i, (c, n) in enumerate(units):
+                for t in range(2):
+                    at = i * CHUNK + t * P
+                    for b in (1, 0):
+                        nc.tensor.matmul_mx(
+                            out=y[:, at : at + P],
+                            lhsT=wd_w[:, b, 2 * P * n : 2 * P * (n + 1)].bitcast(FP4X4),
+                            lhsT_scale=wd_sc[:, b, P * n : P * (n + 1)],
+                            rhs=h_w[c][:, b, t * P : (t + 1) * P].bitcast(FP8X4),
+                            rhs_scale=h_sc[c][:, b, t * P : (t + 1) * P],
+                            start=(b == 1),
+                            stop=(b == 0),
+                        )
+            width = len(units) * CHUNK
+            staged = held("msg%d%d" % units[0], [P, width], F32)
+            nc.scalar.copy(staged[:], y[:, 0:width])
+            for i, unit in enumerate(units):
+                msgs[unit] = staged[:, i * CHUNK : (i + 1) * CHUNK]
+
+        everything = list(sources)
+        gather_all(0, everything)
+        first_layer(0, 0, 0)
+        first_layer(1, 0, 1)
+        turn_and_quantise(0, 0, 4)
+        first_layer(0, 1, 6)
+        first_layer(1, 1, 7)
+        turn_and_quantise(0, 1, 5, 0, 1)
+        turn_and_quantise(0, 1, 6, 1, 2)
+        second_layer([(0, 0)], 4)
+        second_layer([(0, 1)], 7)
+        gather_all(1, everything)
+        first_layer(2, 0, 2)
+        first_layer(3, 0, 3)
+        turn_and_quantise(1, 0, 2)
+        first_layer(2, 1, 0)
+        first_layer(3, 1, 1)
+        turn_and_quantise(1, 1, 3)
+        second_layer([(0, 2), (0, 3)], 3)
+        gather_all(2, everything)
+        first_layer(4, 0, 5)
+        first_layer(5, 0, 6)
+        second_layer([(1, 0), (1, 1)], 6)
+        turn_and_quantise(2, 0, 7)
+        first_layer(4, 1, 0)
+        first_layer(5, 1, 1)
+        turn_and_quantise(2, 1, 2)
+        second_layer([(1, 2), (1, 3)], 2)
+        first_layer(6, 0, 4)
+        first_layer(7, 0, 5)
+        second_layer([(2, 0)], 5)
+        turn_and_quantise(3, 0, 3)
+        first_layer(6, 1, 6)
+        first_layer(7, 1, 7)
+        turn_and_quantise(3, 1, 0)
+        second_layer([(2, 1)], 0)
+        second_layer([(3, 0), (2, 2)], 1)
+        second_layer([(3, 1), (3, 2)], 2)
+        second_layer([(2, 3), (3, 3)], 4)
+
+        for c, n in msgs:
+            j0 = c * CHUNK
+            nc.vector.tensor_tensor(
+                placed[n][:].indirect(dst_list[:, j0 // GROUP : (j0 + CHUNK) // GROUP]),
+                msgs[c, n],
+                gain[:, j0 : j0 + CHUNK],
+                MULT,
+            )
+        for n in range(4):
+            nc.sync.dma_start(out[n * P : (n + 1) * P, :], placed[n][:])

@@ -23,7 +23,8 @@ HALF = 512
 GROUP = 16
 CHUNK = 256
 GATHER_CUTS = [(0, 256), (256, 512), (512, 1024)]
-SCALAR_COLS = {(0, 0): 512, (0, 1): 512, (1, 0): 192, (1, 1): 192}
+SCALAR_COLS = {(1, 0): [('scalar', 0, 512)], (1, 1): [('scalar', 0, 128), ('vector', 128, 512)], (0, 0): [('scalar', 0, 512)], (0, 1): [('scalar', 0, 512)]}
+QUANT_CUTS = {(1, 0): [(0, 512)], (1, 1): [(0, 512)], (0, 0): [(0, 512)], (0, 1): [(0, 512)]}
 
 
 def tile_list_msg_relu_none_kernel(
@@ -36,7 +37,7 @@ def tile_list_msg_relu_none_kernel(
         shared = ctx.enter_context(tc.tile_pool(name="shared", bufs=1))
         psum = ctx.enter_context(tc.psum_pool(name="psum", bufs=1))
 
-        offsets = {"grouped00":0,"src_w0_2":0,"grouped01":4096,"dst_sc_2":4096,"grouped11":8192,"src_sc0_2":8192,"src_sc1_2":8704,"h_in000":12288,"dst_w1_2":12288,"h_in011":14336,"src_w1_2":14336}
+        offsets = {"grouped00": 0, "dst_w0_2": 0, "grouped01": 4096, "src_w0_2": 4096, "dst_sc_2": 6144, "grouped11": 8192, "src_sc0_2": 8192, "src_sc1_2": 8704, "dst_w1_2": 9216, "h_in011": 12288, "src_w1_2": 12288}
 
         def held(name, shape, dtype):
             if name in offsets:
@@ -52,7 +53,7 @@ def tile_list_msg_relu_none_kernel(
 
         tab_sc_one = held("tab_sc_one", [P, T], U8)
         tab_sc_both = held("tab_sc_both", [P, T], U8)
-        nc.vector.memset(tab_sc_both[:].bitcast(I32), 0)
+        nc.gpsimd.memset(tab_sc_both[:].bitcast(I32), 0)
         nc.vector.memset(tab_sc_one[:].bitcast(I32), 0)
 
         ident = held("ident", [P, P], F32)
@@ -62,16 +63,17 @@ def tile_list_msg_relu_none_kernel(
         nc.vector.memset(ws_sc[:].bitcast(I32), 0)
         nc.vector.memset(wd_sc[:].bitcast(I32), 0)
         placed = [held("placed%d" % n, [P, T], F32) for n in range(4)]
-        for n in range(4):
-            for c in range(0, T, 256):
-                nc.gpsimd.memset(placed[n][:, c : c + 256], 0.0)
+
+        def zero(n):
+            nc.vector.memset(placed[n][:].bitcast(I32), 0)
 
         wt_raw, tab_w, ws_w = {}, {}, {}
 
-        def load_wt(b, a):
-            wt_raw[b, a] = held("wt_raw%d%d" % (b, a), [P, 4, HALF], F32)
-            rows = wt[a * HALF : (a + 1) * HALF, b * HALF : (b + 1) * HALF]
-            nc.sync.dma_start(wt_raw[b, a][:], rows.rearrange("(p i) c -> p i c", i=4))
+        def load_wt(b, a, c0=0, c1=HALF):
+            if (b, a) not in wt_raw:
+                wt_raw[b, a] = held("wt_raw%d%d" % (b, a), [P, 4, HALF], F32)
+            rows = wt[a * HALF : (a + 1) * HALF, b * HALF + c0 : b * HALF + c1]
+            nc.sync.dma_start(wt_raw[b, a][:, :, c0:c1], rows.rearrange("(p i) c -> p i c", i=4))
 
         def load_tab(a):
             tab_w[a] = held("tab_w%d" % a, [P, T], U32)
@@ -107,9 +109,9 @@ def tile_list_msg_relu_none_kernel(
                     tab_sc_one[32 * q : 32 * q + 4, :].bitcast(I32), tab_scales[1, 4 * q : 4 * q + 4, :].bitcast(I32)
                 )
 
-        load_tab(0)
-        load_both()
         load_wt(0, 0)
+        load_both()
+        load_tab(0)
         load_one()
         load_wt(0, 1)
         load_tab(1)
@@ -124,26 +126,25 @@ def tile_list_msg_relu_none_kernel(
         nc.sync.dma_start(gain[:], wgo)
 
         wt_w, wt_sc = {}, {}
-        for b in range(2):
-            for a in range(2):
-                grouped = held("grouped%d%d" % (b, a), [P, HALF, 4], BF16)
-                split = SCALAR_COLS[b, a]
-                nc.scalar.activation(
-                    grouped[:, 0:split, :].rearrange("p (c u) i -> p c i u", u=4),
-                    wt_raw[b, a][:, :, 0:split].rearrange("p i (c u) -> p c i u", u=4),
-                    COPY,
-                )
-                if split < HALF:
-                    nc.vector.tensor_copy(
-                        grouped[:, split:HALF, :].rearrange("p (c u) i -> p c i u", u=4),
-                        wt_raw[b, a][:, :, split:HALF].rearrange("p i (c u) -> p c i u", u=4),
-                    )
-                wt_w[b, a] = held("wt_w%d%d" % (b, a), [P, HALF], U32)
-                wt_sc[b, a] = held("wt_sc%d%d" % (b, a), [P, HALF], U8)
+
+        def quantise_wt(b, a):
+            grouped = held("grouped%d%d" % (b, a), [P, HALF, 4], BF16)
+            for engine, c0, c1 in SCALAR_COLS[b, a]:
+                dst = grouped[:, c0:c1, :].rearrange("p (c u) i -> p c i u", u=4)
+                raw = wt_raw[b, a][:, :, c0:c1].rearrange("p i (c u) -> p c i u", u=4)
+                if engine == "scalar":
+                    nc.scalar.activation(dst, raw, COPY)
+                elif engine == "vector":
+                    nc.vector.tensor_copy(dst, raw)
+                else:
+                    nc.gpsimd.tensor_scalar(dst, raw, 1.0, 0.0, MULT, mybir.AluOpType.add)
+            wt_w[b, a] = held("wt_w%d%d" % (b, a), [P, HALF], U32)
+            wt_sc[b, a] = held("wt_sc%d%d" % (b, a), [P, HALF], U8)
+            for c0, c1 in QUANT_CUTS[b, a]:
                 nc.vector.quantize_mx(
-                    out=wt_w[b, a][:].bitcast(FP8X4),
-                    scales=wt_sc[b, a][:],
-                    in_=grouped[:].rearrange("p c i -> p (c i)"),
+                    out=wt_w[b, a][:, c0:c1].bitcast(FP8X4),
+                    scales=wt_sc[b, a][:, c0:c1],
+                    in_=grouped[:, c0:c1, :].rearrange("p c i -> p (c i)"),
                 )
 
         picked = {}
@@ -163,9 +164,8 @@ def tile_list_msg_relu_none_kernel(
             "src_w1": (tab_w[1], src_list, U32),
         }
 
-        def gather_all(g, names):
-            for name in names:
-                gather(name, g, *sources[name])
+        def pick(name, g):
+            gather(name, g, *sources[name])
 
         tiles = J // P
         relu = [held("relu%d" % t, [P, 2, HALF], BF16) for t in range(tiles)]
@@ -237,26 +237,51 @@ def tile_list_msg_relu_none_kernel(
             for i, unit in enumerate(units):
                 msgs[unit] = staged[:, i * CHUNK : (i + 1) * CHUNK]
 
-        everything = list(sources)
-        gather_all(0, everything)
+        zero(0)
+        zero(1)
+        zero(2)
+        zero(3)
+        pick("dst_sc", 0)
+        pick("src_sc0", 0)
+        pick("dst_sc", 1)
+        pick("src_sc0", 1)
+        pick("dst_w0", 0)
+        pick("src_w0", 0)
+        pick("dst_w0", 1)
+        pick("src_w0", 1)
+        quantise_wt(0, 0)
+        pick("src_sc1", 0)
+        pick("src_sc1", 1)
+        pick("dst_w0", 2)
+        quantise_wt(0, 1)
+        pick("src_w1", 0)
+        pick("dst_w1", 0)
+        pick("dst_w1", 1)
+        pick("src_w1", 1)
         first_layer(0, 0, 0)
         first_layer(1, 0, 1)
         turn_and_quantise(0, 0, 4)
+        pick("src_w0", 2)
+        pick("dst_sc", 2)
+        quantise_wt(1, 0)
+        quantise_wt(1, 1)
         first_layer(0, 1, 6)
         first_layer(1, 1, 7)
         turn_and_quantise(0, 1, 5, 0, 1)
         turn_and_quantise(0, 1, 6, 1, 2)
         second_layer([(0, 0)], 4)
         second_layer([(0, 1)], 7)
-        gather_all(1, everything)
         first_layer(2, 0, 2)
         first_layer(3, 0, 3)
-        turn_and_quantise(1, 0, 2)
         first_layer(2, 1, 0)
         first_layer(3, 1, 1)
         turn_and_quantise(1, 1, 3)
+        turn_and_quantise(1, 0, 2)
         second_layer([(0, 2), (0, 3)], 3)
-        gather_all(2, everything)
+        pick("src_sc0", 2)
+        pick("src_sc1", 2)
+        pick("dst_w1", 2)
+        pick("src_w1", 2)
         first_layer(4, 0, 5)
         first_layer(5, 0, 6)
         second_layer([(1, 0), (1, 1)], 6)
@@ -264,16 +289,17 @@ def tile_list_msg_relu_none_kernel(
         first_layer(4, 1, 0)
         first_layer(5, 1, 1)
         turn_and_quantise(2, 1, 2)
-        second_layer([(1, 2), (1, 3)], 2)
-        first_layer(6, 0, 4)
-        first_layer(7, 0, 5)
         second_layer([(2, 0)], 5)
+        first_layer(6, 0, 4)
+        second_layer([(1, 2), (1, 3)], 4)
+        first_layer(7, 0, 5)
         turn_and_quantise(3, 0, 3)
         first_layer(6, 1, 6)
         first_layer(7, 1, 7)
         turn_and_quantise(3, 1, 0)
         second_layer([(2, 1)], 0)
-        second_layer([(3, 0), (2, 2)], 1)
+        second_layer([(3, 0)], 1)
+        second_layer([(2, 2)], 7)
         second_layer([(3, 1), (3, 2)], 2)
         second_layer([(2, 3), (3, 3)], 4)
 

@@ -22,9 +22,9 @@ P = 128
 HALF = 512
 GROUP = 16
 CHUNK = 256
-GATHER_CUTS = [(0, 256), (256, 512), (512, 1024)]
-SCALAR_COLS = {(1, 0): [('scalar', 0, 512)], (1, 1): [('scalar', 0, 128), ('vector', 128, 512)], (0, 0): [('scalar', 0, 512)], (0, 1): [('scalar', 0, 512)]}
-QUANT_CUTS = {(1, 0): [(0, 512)], (1, 1): [(0, 512)], (0, 0): [(0, 512)], (0, 1): [(0, 512)]}
+GATHER_CUTS = [(0, 256), (256, 512), (512, 1024), (0, 512)]
+SCALAR_COLS = {(1, 0): [('scalar', 0, 320), ('vector', 320, 512)], (1, 1): [('scalar', 0, 256), ('vector', 256, 512)], (0, 0): [('scalar', 0, 512)], (0, 1): [('scalar', 0, 512)]}
+QUANT_CUTS = {(1, 0): [(0, 512)], (1, 1): [(0, 256), (256, 512)], (0, 0): [(0, 512)], (0, 1): [(0, 512)]}
 
 
 def tile_list_msg_relu_none_kernel(
@@ -37,7 +37,7 @@ def tile_list_msg_relu_none_kernel(
         shared = ctx.enter_context(tc.tile_pool(name="shared", bufs=1))
         psum = ctx.enter_context(tc.psum_pool(name="psum", bufs=1))
 
-        offsets = {"grouped00": 0, "dst_w0_2": 0, "grouped01": 4096, "src_w0_2": 4096, "dst_sc_2": 6144, "grouped11": 8192, "src_sc0_2": 8192, "src_sc1_2": 8704, "dst_w1_2": 9216, "h_in011": 12288, "src_w1_2": 12288}
+        offsets = {"grouped11": 0, "dst_sc_2": 0, "dst_w1_2": 512, "grouped01": 4096, "src_sc0_2": 4096, "h_in011": 8192, "src_w1_2": 8192}
 
         def held(name, shape, dtype):
             if name in offsets:
@@ -56,6 +56,8 @@ def tile_list_msg_relu_none_kernel(
         nc.gpsimd.memset(tab_sc_both[:].bitcast(I32), 0)
         nc.vector.memset(tab_sc_one[:].bitcast(I32), 0)
 
+        moved_sc = held("moved_sc", [P, HALF], U8)
+        nc.vector.memset(moved_sc[:].bitcast(I32), 0)
         ident = held("ident", [P, P], F32)
         make_identity(nc, ident[:])
         ws_sc = held("ws_sc", [P, 2, R], U8)
@@ -63,9 +65,9 @@ def tile_list_msg_relu_none_kernel(
         nc.vector.memset(ws_sc[:].bitcast(I32), 0)
         nc.vector.memset(wd_sc[:].bitcast(I32), 0)
         placed = [held("placed%d" % n, [P, T], F32) for n in range(4)]
-
-        def zero(n):
-            nc.vector.memset(placed[n][:].bitcast(I32), 0)
+        for n in range(4):
+            for c in range(0, T, 256):
+                nc.gpsimd.memset(placed[n][:, c : c + 256], 0.0)
 
         wt_raw, tab_w, ws_w = {}, {}, {}
 
@@ -109,9 +111,9 @@ def tile_list_msg_relu_none_kernel(
                     tab_sc_one[32 * q : 32 * q + 4, :].bitcast(I32), tab_scales[1, 4 * q : 4 * q + 4, :].bitcast(I32)
                 )
 
+        load_tab(0)
         load_wt(0, 0)
         load_both()
-        load_tab(0)
         load_one()
         load_wt(0, 1)
         load_tab(1)
@@ -165,7 +167,15 @@ def tile_list_msg_relu_none_kernel(
         }
 
         def pick(name, g):
-            gather(name, g, *sources[name])
+            if (name, g) == ("src_sc1", 2):
+                picked[name, g] = moved_sc
+                for q in range(4):
+                    nc.sync.dma_start(
+                        moved_sc[32 * q : 32 * q + 4, :].bitcast(I32),
+                        picked["src_sc0", g][32 * q + 4 : 32 * q + 8, :].bitcast(I32),
+                    )
+            else:
+                gather(name, g, *sources[name])
 
         tiles = J // P
         relu = [held("relu%d" % t, [P, 2, HALF], BF16) for t in range(tiles)]
@@ -174,17 +184,19 @@ def tile_list_msg_relu_none_kernel(
         msgs = {}
 
         def first_layer(t, b, bank, on_vector=False):
-            g = [i for i, (j0, j1) in enumerate(GATHER_CUTS) if j0 <= t * P < j1][0]
-            at = t * P - GATHER_CUTS[g][0]
-            cols = slice(at, at + P)
             acc = banks[bank]
 
+            def edge_cols(name, row=0):
+                g = [g for (nm, g) in picked if nm == name and GATHER_CUTS[g][0] <= t * P < GATHER_CUTS[g][1]][0]
+                at = t * P - GATHER_CUTS[g][0]
+                return picked[name, g][row:P, at : at + P]
+
             def target_pass(a):
-                return (picked["dst_w%d" % a, g][:, cols].bitcast(FP8X4), picked["dst_sc", g][4 * a : P, cols],
+                return (edge_cols("dst_w%d" % a).bitcast(FP8X4), edge_cols("dst_sc", 4 * a),
                         wt_w[b, a][:].bitcast(FP8X4), wt_sc[b, a][:])
 
             def source_pass(a):
-                return (picked["src_w%d" % a, g][:, cols].bitcast(FP8X4), picked["src_sc%d" % a, g][:, cols],
+                return (edge_cols("src_w%d" % a).bitcast(FP8X4), edge_cols("src_sc%d" % a),
                         ws_w[b][:, a, :].bitcast(FP4X4), ws_sc[:, a, b * HALF : (b + 1) * HALF])
 
             if b == 0:
@@ -237,32 +249,24 @@ def tile_list_msg_relu_none_kernel(
             for i, unit in enumerate(units):
                 msgs[unit] = staged[:, i * CHUNK : (i + 1) * CHUNK]
 
-        zero(0)
-        zero(1)
-        zero(2)
-        zero(3)
-        pick("dst_sc", 0)
-        pick("src_sc0", 0)
-        pick("dst_sc", 1)
-        pick("src_sc0", 1)
-        pick("dst_w0", 0)
-        pick("src_w0", 0)
-        pick("dst_w0", 1)
-        pick("src_w0", 1)
+        pick("dst_w0", 3)
+        pick("src_w0", 3)
+        pick("dst_sc", 3)
         quantise_wt(0, 0)
-        pick("src_sc1", 0)
-        pick("src_sc1", 1)
+        pick("src_sc1", 3)
         pick("dst_w0", 2)
+        pick("src_sc0", 3)
         quantise_wt(0, 1)
-        pick("src_w1", 0)
         pick("dst_w1", 0)
+        pick("src_w1", 0)
         pick("dst_w1", 1)
         pick("src_w1", 1)
         first_layer(0, 0, 0)
-        first_layer(1, 0, 1)
+        first_layer(1, 0, 0)
         turn_and_quantise(0, 0, 4)
         pick("src_w0", 2)
-        pick("dst_sc", 2)
+        pick("src_sc0", 2)
+        pick("src_sc1", 2)
         quantise_wt(1, 0)
         quantise_wt(1, 1)
         first_layer(0, 1, 6)
@@ -277,9 +281,8 @@ def tile_list_msg_relu_none_kernel(
         first_layer(3, 1, 1)
         turn_and_quantise(1, 1, 3)
         turn_and_quantise(1, 0, 2)
-        second_layer([(0, 2), (0, 3)], 3)
-        pick("src_sc0", 2)
-        pick("src_sc1", 2)
+        second_layer([(0, 2), (0, 3)], 2)
+        pick("dst_sc", 2)
         pick("dst_w1", 2)
         pick("src_w1", 2)
         first_layer(4, 0, 5)
@@ -290,15 +293,15 @@ def tile_list_msg_relu_none_kernel(
         first_layer(5, 1, 1)
         turn_and_quantise(2, 1, 2)
         second_layer([(2, 0)], 5)
-        first_layer(6, 0, 4)
+        first_layer(6, 0, 7)
         second_layer([(1, 2), (1, 3)], 4)
         first_layer(7, 0, 5)
         turn_and_quantise(3, 0, 3)
         first_layer(6, 1, 6)
+        second_layer([(2, 1)], 0)
         first_layer(7, 1, 7)
         turn_and_quantise(3, 1, 0)
-        second_layer([(2, 1)], 0)
-        second_layer([(3, 0)], 1)
+        second_layer([(3, 0)], 6)
         second_layer([(2, 2)], 7)
         second_layer([(3, 1), (3, 2)], 2)
         second_layer([(2, 3), (3, 3)], 4)

@@ -22,9 +22,9 @@ P = 128
 HALF = 512
 GROUP = 16
 CHUNK = 256
-GATHER_CUTS = [(0, 256), (256, 512), (512, 1024), (0, 512)]
-SCALAR_COLS = {(1, 0): [('scalar', 0, 320), ('vector', 320, 512)], (1, 1): [('scalar', 0, 256), ('vector', 256, 512)], (0, 0): [('scalar', 0, 512)], (0, 1): [('scalar', 0, 512)]}
-QUANT_CUTS = {(1, 0): [(0, 512)], (1, 1): [(0, 256), (256, 512)], (0, 0): [(0, 512)], (0, 1): [(0, 512)]}
+CHUNKS = J // CHUNK
+BANKS = 8
+STAGE_BYTES = 2 * 4 * HALF
 
 
 def tile_list_msg_relu_none_kernel(
@@ -37,282 +37,217 @@ def tile_list_msg_relu_none_kernel(
         shared = ctx.enter_context(tc.tile_pool(name="shared", bufs=1))
         psum = ctx.enter_context(tc.psum_pool(name="psum", bufs=1))
 
-        offsets = {"grouped11": 0, "dst_sc_2": 0, "dst_w1_2": 512, "grouped01": 4096, "src_sc0_2": 4096, "h_in011": 8192, "src_w1_2": 8192}
+        def held(name, shape, dtype, offset=None):
+            if offset is None:
+                return keep.tile(shape, dtype, name=name, align_bytes=64)
+            return shared.tile(shape, dtype, name=name, align_bytes=64, offset=offset)
 
-        def held(name, shape, dtype):
-            if name in offsets:
-                return shared.tile(shape, dtype, name=name, align_bytes=64, offset=offsets[name])
-            return keep.tile(shape, dtype, name=name, align_bytes=64)
+        banks = [psum.tile([P, HALF], F32, name="bank%d" % i) for i in range(BANKS)]
+        uses = []
 
-        banks = [psum.tile([P, HALF], F32, name="bank%d" % i) for i in range(8)]
+        def next_bank():
+            uses.append(len(uses))
+            return banks[uses[-1] % BANKS]
 
-        src_list = lists.tile([P, J // GROUP], U16, name="src_list")
-        dst_list = lists.tile([P, J // GROUP], U16, name="dst_list")
-        nc.sync.dma_start(src_list[:], offs)
-        nc.sync.dma_start(dst_list[:], offs2)
-
-        tab_sc_one = held("tab_sc_one", [P, T], U8)
-        tab_sc_both = held("tab_sc_both", [P, T], U8)
-        nc.gpsimd.memset(tab_sc_both[:].bitcast(I32), 0)
-        nc.vector.memset(tab_sc_one[:].bitcast(I32), 0)
-
-        moved_sc = held("moved_sc", [P, HALF], U8)
-        nc.vector.memset(moved_sc[:].bitcast(I32), 0)
-        ident = held("ident", [P, P], F32)
-        make_identity(nc, ident[:])
+        tab_sc = held("tab_sc", [P, T], U8)
         ws_sc = held("ws_sc", [P, 2, R], U8)
         wd_sc = held("wd_sc", [P, 2, N], U8)
-        nc.vector.memset(ws_sc[:].bitcast(I32), 0)
-        nc.vector.memset(wd_sc[:].bitcast(I32), 0)
-        placed = [held("placed%d" % n, [P, T], F32) for n in range(4)]
-        for n in range(4):
-            for c in range(0, T, 256):
-                nc.gpsimd.memset(placed[n][:, c : c + 256], 0.0)
-
-        wt_raw, tab_w, ws_w = {}, {}, {}
-
-        def load_wt(b, a, c0=0, c1=HALF):
-            if (b, a) not in wt_raw:
-                wt_raw[b, a] = held("wt_raw%d%d" % (b, a), [P, 4, HALF], F32)
-            rows = wt[a * HALF : (a + 1) * HALF, b * HALF + c0 : b * HALF + c1]
-            nc.sync.dma_start(wt_raw[b, a][:, :, c0:c1], rows.rearrange("(p i) c -> p i c", i=4))
+        moved_sc = held("moved_sc", [P, J], U8)
+        for plane in (tab_sc, ws_sc, wd_sc, moved_sc):
+            nc.vector.memset(plane[:].bitcast(I32), 0)
 
         def load_tab(a):
-            tab_w[a] = held("tab_w%d" % a, [P, T], U32)
-            nc.sync.dma_start(tab_w[a][:].bitcast(I32), tab_words[a].rearrange("p t i -> p (t i)").bitcast(I32))
+            words = held("tab_w%d" % a, [P, T], U32)
+            nc.sync.dma_start(words[:].bitcast(I32), tab_words[a].rearrange("p t i -> p (t i)").bitcast(I32))
+            return words
 
-        def load_ws_all():
-            both_halves = held("ws_w", [P, 2, 4 * HALF], U8)
-            nc.sync.dma_start(both_halves[:].bitcast(I32), ws_words.rearrange("a p x -> p a x").bitcast(I32))
-            for b in range(2):
-                ws_w[b] = both_halves[:, :, 2 * HALF * b : 2 * HALF * (b + 1)]
+        def load_wt(a, c0, c1):
+            raw = held("wt_raw%d_%d" % (a, c0), [P, 4, c1 - c0], F32)
+            nc.sync.dma_start(raw[:], wt[a * HALF : (a + 1) * HALF, c0:c1].rearrange("(p i) c -> p i c", i=4))
+            return raw
 
-        def load_ws(b):
-            ws_w[b] = held("ws_w%d" % b, [P, 2, 2 * HALF], U8)
-            cols = ws_words[:, :, 2 * HALF * b : 2 * HALF * (b + 1)]
-            nc.sync.dma_start(ws_w[b][:].bitcast(I32), cols.rearrange("a p x -> p a x").bitcast(I32))
-
-        def load_scale_rows(plane, rows):
+        def load_packed(name, words, plane, rows):
             for q in range(4):
                 nc.sync.dma_start(
                     plane[32 * q : 32 * q + 4, :, :].bitcast(I32),
                     rows[:, 4 * q : 4 * q + 4, :].rearrange("a r n -> r a n").bitcast(I32),
                 )
+            codes = held(name, [P, 2, words.shape[2]], U8)
+            nc.sync.dma_start(codes[:].bitcast(I32), words.rearrange("a p x -> p a x").bitcast(I32))
+            return codes
 
-        def load_both():
-            for q in range(4):
-                nc.sync.dma_start(
-                    tab_sc_both[32 * q : 32 * q + 8, :].bitcast(I32), tab_scales[:, 4 * q : 4 * q + 4, :].bitcast(I32)
-                )
-
-        def load_one():
-            for q in range(4):
-                nc.sync.dma_start(
-                    tab_sc_one[32 * q : 32 * q + 4, :].bitcast(I32), tab_scales[1, 4 * q : 4 * q + 4, :].bitcast(I32)
-                )
-
-        load_tab(0)
-        load_wt(0, 0)
-        load_both()
-        load_one()
-        load_wt(0, 1)
-        load_tab(1)
-        load_scale_rows(ws_sc, ws_scales)
-        load_ws_all()
-        load_wt(1, 0)
-        load_wt(1, 1)
-        load_scale_rows(wd_sc, wd_scales)
-        wd_w = held("wd_w", [P, 2, 2 * N], U8)
-        nc.sync.dma_start(wd_w[:].bitcast(I32), wd_words.rearrange("a p x -> p a x").bitcast(I32))
+        src_list = lists.tile([P, J // GROUP], U16, name="src_list")
+        dst_list = lists.tile([P, J // GROUP], U16, name="dst_list")
+        nc.sync.dma_start(src_list[:], offs)
+        nc.sync.dma_start(dst_list[:], offs2)
+        for q in range(4):
+            nc.sync.dma_start(
+                tab_sc[32 * q : 32 * q + 8, :].bitcast(I32), tab_scales[:, 4 * q : 4 * q + 4, :].bitcast(I32)
+            )
+        tab_w = [load_tab(0)]
+        quarters = [(0, 0), (0, 1), (1, 0), (1, 1)]
+        raws = [[load_wt(a, b * HALF, (b + 1) * HALF)] for a, b in quarters[:3]]
+        ws_w = load_packed("ws_w", ws_words, ws_sc, ws_scales)
+        tab_w.append(load_tab(1))
+        raws.append([load_wt(1, HALF, HALF + CHUNK), load_wt(1, HALF + CHUNK, R)])
+        wd_w = load_packed("wd_w", wd_words, wd_sc, wd_scales)
         gain = held("gain", [P, J], F32)
         nc.sync.dma_start(gain[:], wgo)
 
         wt_w, wt_sc = {}, {}
 
-        def quantise_wt(b, a):
-            grouped = held("grouped%d%d" % (b, a), [P, HALF, 4], BF16)
-            for engine, c0, c1 in SCALAR_COLS[b, a]:
-                dst = grouped[:, c0:c1, :].rearrange("p (c u) i -> p c i u", u=4)
-                raw = wt_raw[b, a][:, :, c0:c1].rearrange("p i (c u) -> p c i u", u=4)
-                if engine == "scalar":
-                    nc.scalar.activation(dst, raw, COPY)
-                elif engine == "vector":
-                    nc.vector.tensor_copy(dst, raw)
+        def quantise_wt(i):
+            grouped = held("grouped%d" % i, [P, HALF, 4], BF16, i * STAGE_BYTES)
+            codes = held("wt_w%d" % i, [P, HALF], U32)
+            plane = held("wt_sc%d" % i, [P, HALF], U8)
+            width = HALF // len(raws[i])
+            for piece, raw in enumerate(raws[i]):
+                cols = slice(piece * width, (piece + 1) * width)
+                dst = grouped[:, cols, :].rearrange("p (c u) i -> p c i u", u=4)
+                src = raw[:].rearrange("p i (c u) -> p c i u", u=4)
+                if piece == 0:
+                    nc.scalar.activation(dst, src, COPY)
                 else:
-                    nc.gpsimd.tensor_scalar(dst, raw, 1.0, 0.0, MULT, mybir.AluOpType.add)
-            wt_w[b, a] = held("wt_w%d%d" % (b, a), [P, HALF], U32)
-            wt_sc[b, a] = held("wt_sc%d%d" % (b, a), [P, HALF], U8)
-            for c0, c1 in QUANT_CUTS[b, a]:
+                    nc.vector.tensor_copy(dst, src)
                 nc.vector.quantize_mx(
-                    out=wt_w[b, a][:, c0:c1].bitcast(FP8X4),
-                    scales=wt_sc[b, a][:, c0:c1],
-                    in_=grouped[:, c0:c1, :].rearrange("p c i -> p (c i)"),
+                    out=codes[:, cols].bitcast(FP8X4),
+                    scales=plane[:, cols],
+                    in_=grouped[:, cols, :].rearrange("p c i -> p (c i)"),
                 )
+            wt_w[quarters[i]], wt_sc[quarters[i]] = codes, plane
 
         picked = {}
 
-        def gather(name, g, window, edge_list, dtype):
-            j0, j1 = GATHER_CUTS[g]
-            picked[name, g] = held("%s_%d" % (name, g), [P, j1 - j0], dtype)
-            nc.vector.tensor_copy(picked[name, g][:], window[:].indirect(edge_list[:, j0 // GROUP : j1 // GROUP]))
+        def gather(name, window, edge_list, dtype, j0, j1, offset=None):
+            got = held("%s_%d" % (name, j0), [P, j1 - j0], dtype, offset)
+            nc.vector.tensor_copy(got[:], window[:].indirect(edge_list[:, j0 // GROUP : j1 // GROUP]))
+            for t in range(j0 // P, j1 // P):
+                picked[name, t] = (got, t * P - j0)
+            return got
 
-        sources = {
-            "dst_w0": (tab_w[0], dst_list, U32),
-            "src_w0": (tab_w[0], src_list, U32),
-            "dst_sc": (tab_sc_both, dst_list, U8),
-            "src_sc0": (tab_sc_both, src_list, U8),
-            "src_sc1": (tab_sc_one, src_list, U8),
-            "dst_w1": (tab_w[1], dst_list, U32),
-            "src_w1": (tab_w[1], src_list, U32),
-        }
+        src_sc = gather("src_sc0", tab_sc, src_list, U8, 0, J)
+        for q in range(4):
+            nc.gpsimd.dma_start(
+                moved_sc[32 * q : 32 * q + 4, :].bitcast(I32), src_sc[32 * q + 4 : 32 * q + 8, :].bitcast(I32)
+            )
+        for t in range(J // P):
+            picked["src_sc1", t] = (moved_sc, t * P)
+        gather("dst_sc", tab_sc, dst_list, U8, 0, HALF)
+        gather("dst_w0", tab_w[0], dst_list, U32, 0, HALF)
+        gather("src_w0", tab_w[0], src_list, U32, 0, HALF)
+        quantise_wt(0)
+        gather("dst_w0", tab_w[0], dst_list, U32, HALF, J, 0)
+        gather("src_w0", tab_w[0], src_list, U32, HALF, J, 4 * HALF)
+        quantise_wt(1)
+        gather("dst_sc", tab_sc, dst_list, U8, HALF, J, STAGE_BYTES)
+        quantise_wt(2)
+        for c in range(2):
+            at = 2 * STAGE_BYTES + 8 * CHUNK * c
+            gather("dst_w1", tab_w[1], dst_list, U32, c * CHUNK, (c + 1) * CHUNK, at)
+            gather("src_w1", tab_w[1], src_list, U32, c * CHUNK, (c + 1) * CHUNK, at + 4 * CHUNK)
+        quantise_wt(3)
+        gather("dst_w1", tab_w[1], dst_list, U32, HALF, J, 3 * STAGE_BYTES)
+        gather("src_w1", tab_w[1], src_list, U32, HALF, J, 3 * STAGE_BYTES + 4 * HALF)
 
-        def pick(name, g):
-            if (name, g) == ("src_sc1", 2):
-                picked[name, g] = moved_sc
-                for q in range(4):
-                    nc.sync.dma_start(
-                        moved_sc[32 * q : 32 * q + 4, :].bitcast(I32),
-                        picked["src_sc0", g][32 * q + 4 : 32 * q + 8, :].bitcast(I32),
-                    )
-            else:
-                gather(name, g, *sources[name])
+        ident = held("ident", [P, P], F32)
+        make_identity(nc, ident[:])
+        placed = [held("placed%d" % n, [P, T], F32) for n in range(N // P)]
+        for page in placed:
+            for c0 in range(0, T, CHUNK):
+                nc.gpsimd.memset(page[:, c0 : c0 + CHUNK], 0.0)
 
-        tiles = J // P
-        relu = [held("relu%d" % t, [P, 2, HALF], BF16) for t in range(tiles)]
-        h_w = [held("h_w%d" % c, [P, 2, CHUNK], U32) for c in range(4)]
-        h_sc = [held("h_sc%d" % c, [P, 2, CHUNK], U8) for c in range(4)]
-        msgs = {}
+        relu = [[held("relu%d%d" % (s, t), [P, HALF], BF16) for t in range(2)] for s in range(2)]
+        h_w = [held("h_w%d" % c, [P, 2, CHUNK], U32) for c in range(CHUNKS)]
+        h_sc = [held("h_sc%d" % c, [P, 2, CHUNK], U8) for c in range(CHUNKS)]
+        sums = {}
 
-        def first_layer(t, b, bank, on_vector=False):
-            acc = banks[bank]
+        def edge_cols(name, t, row=0):
+            got, at = picked[name, t]
+            return got[row:P, at : at + P]
 
-            def edge_cols(name, row=0):
-                g = [g for (nm, g) in picked if nm == name and GATHER_CUTS[g][0] <= t * P < GATHER_CUTS[g][1]][0]
-                at = t * P - GATHER_CUTS[g][0]
-                return picked[name, g][row:P, at : at + P]
+        def first_layer(c):
+            for b in range(2):
+                for t in (2 * c, 2 * c + 1):
+                    target = [
+                        (edge_cols("dst_w%d" % a, t).bitcast(FP8X4), edge_cols("dst_sc", t, 4 * a),
+                         wt_w[a, b][:].bitcast(FP8X4), wt_sc[a, b][:])
+                        for a in range(2)
+                    ]
+                    source = [
+                        (edge_cols("src_w%d" % a, t).bitcast(FP8X4), edge_cols("src_sc%d" % a, t),
+                         ws_w[:, a, 2 * HALF * b : 2 * HALF * (b + 1)].bitcast(FP4X4),
+                         ws_sc[:, a, b * HALF : (b + 1) * HALF])
+                        for a in range(2)
+                    ]
+                    passes = [target[0], source[0]] + ([target[1], source[1]] if b == 0 else [source[1], target[1]])
+                    acc = next_bank()
+                    for i, (lhs, lhs_sc, rhs, rhs_sc) in enumerate(passes):
+                        nc.tensor.matmul_mx(out=acc[:], lhsT=lhs, lhsT_scale=lhs_sc, rhs=rhs, rhs_scale=rhs_sc,
+                                            start=(i == 0), stop=(i == len(passes) - 1))
+                    sums[t, b] = acc
 
-            def target_pass(a):
-                return (edge_cols("dst_w%d" % a).bitcast(FP8X4), edge_cols("dst_sc", 4 * a),
-                        wt_w[b, a][:].bitcast(FP8X4), wt_sc[b, a][:])
-
-            def source_pass(a):
-                return (edge_cols("src_w%d" % a).bitcast(FP8X4), edge_cols("src_sc%d" % a),
-                        ws_w[b][:, a, :].bitcast(FP4X4), ws_sc[:, a, b * HALF : (b + 1) * HALF])
-
-            if b == 0:
-                passes = [target_pass(0), source_pass(0), source_pass(1), target_pass(1)]
-            else:
-                passes = [source_pass(0), source_pass(1), target_pass(0), target_pass(1)]
-            for i, (lhs, lhs_sc, rhs, rhs_sc) in enumerate(passes):
-                nc.tensor.matmul_mx(out=acc[:], lhsT=lhs, lhsT_scale=lhs_sc, rhs=rhs, rhs_scale=rhs_sc,
-                                    start=(i == 0), stop=(i == len(passes) - 1))
-            dst = relu[t][:, b, :].rearrange("p (u m e) -> p u m e", u=2, e=2)
-            sums = acc[:].rearrange("p (m u e) -> p u m e", u=2, e=2)
-            if on_vector:
-                nc.vector.tensor_scalar_max(dst, sums, 0.0)
-            else:
-                nc.scalar.activation(dst, sums, RELU)
-
-        def turn_and_quantise(c, b, bank, t0=0, t1=2):
-            turned = banks[bank]
-            for t in reversed(range(t0, t1)):
-                pairs = relu[2 * c + t][:, b, :].bitcast(F32)
+        def turn_and_quantise(c, b):
+            rows = relu[(c + b) % 2]
+            for t in range(2):
+                nc.scalar.activation(
+                    rows[t][:].rearrange("p (u m e) -> p u m e", u=2, e=2),
+                    sums[2 * c + t, b][:].rearrange("p (m u e) -> p u m e", u=2, e=2),
+                    RELU,
+                )
+            turned = next_bank()
+            for t in range(2):
+                pairs = rows[t][:].bitcast(F32)
                 for u in range(2):
-                    at = (2 * (t - t0) + u) * P
+                    at = (2 * t + u) * P
                     nc.tensor.transpose(turned[:, at : at + P], pairs[:, u * P : (u + 1) * P], ident[:])
-            h_in = held("h_in%d%d%d" % (c, b, t0), [P, t1 - t0, P, 2], F32)
-            nc.scalar.copy(h_in[:], turned[:, 0 : 2 * P * (t1 - t0)].rearrange("p (t u j) -> p t j u", j=P, u=2))
+            h_in = held("h_in%d%d" % (c, b), [P, 2, P, 2], F32)
+            nc.scalar.copy(h_in[:], turned[:].rearrange("p (t u j) -> p t j u", j=P, u=2))
             nc.vector.quantize_mx(
-                out=h_w[c][:, b, t0 * P : t1 * P].bitcast(FP8X4),
-                scales=h_sc[c][:, b, t0 * P : t1 * P],
+                out=h_w[c][:, b, :].bitcast(FP8X4),
+                scales=h_sc[c][:, b, :],
                 in_=h_in[:].rearrange("p t j u -> p (t j u)").bitcast(BF16),
             )
 
-        def second_layer(units, bank):
-            y = banks[bank]
-            for i, (c, n) in enumerate(units):
-                for t in range(2):
-                    at = i * CHUNK + t * P
-                    for b in (1, 0):
-                        nc.tensor.matmul_mx(
-                            out=y[:, at : at + P],
-                            lhsT=wd_w[:, b, 2 * P * n : 2 * P * (n + 1)].bitcast(FP4X4),
-                            lhsT_scale=wd_sc[:, b, P * n : P * (n + 1)],
-                            rhs=h_w[c][:, b, t * P : (t + 1) * P].bitcast(FP8X4),
-                            rhs_scale=h_sc[c][:, b, t * P : (t + 1) * P],
-                            start=(b == 1),
-                            stop=(b == 0),
-                        )
-            width = len(units) * CHUNK
-            staged = held("msg%d%d" % units[0], [P, width], F32)
-            nc.scalar.copy(staged[:], y[:, 0:width])
-            for i, unit in enumerate(units):
-                msgs[unit] = staged[:, i * CHUNK : (i + 1) * CHUNK]
-
-        pick("dst_w0", 3)
-        pick("src_w0", 3)
-        pick("dst_sc", 3)
-        quantise_wt(0, 0)
-        pick("src_sc1", 3)
-        pick("dst_w0", 2)
-        pick("src_sc0", 3)
-        quantise_wt(0, 1)
-        pick("dst_w1", 0)
-        pick("src_w1", 0)
-        pick("dst_w1", 1)
-        pick("src_w1", 1)
-        first_layer(0, 0, 0)
-        first_layer(1, 0, 0)
-        turn_and_quantise(0, 0, 4)
-        pick("src_w0", 2)
-        pick("src_sc0", 2)
-        pick("src_sc1", 2)
-        quantise_wt(1, 0)
-        quantise_wt(1, 1)
-        first_layer(0, 1, 6)
-        first_layer(1, 1, 7)
-        turn_and_quantise(0, 1, 5, 0, 1)
-        turn_and_quantise(0, 1, 6, 1, 2)
-        second_layer([(0, 0)], 4)
-        second_layer([(0, 1)], 7)
-        first_layer(2, 0, 2)
-        first_layer(3, 0, 3)
-        first_layer(2, 1, 0)
-        first_layer(3, 1, 1)
-        turn_and_quantise(1, 1, 3)
-        turn_and_quantise(1, 0, 2)
-        second_layer([(0, 2), (0, 3)], 2)
-        pick("dst_sc", 2)
-        pick("dst_w1", 2)
-        pick("src_w1", 2)
-        first_layer(4, 0, 5)
-        first_layer(5, 0, 6)
-        second_layer([(1, 0), (1, 1)], 6)
-        turn_and_quantise(2, 0, 7)
-        first_layer(4, 1, 0)
-        first_layer(5, 1, 1)
-        turn_and_quantise(2, 1, 2)
-        second_layer([(2, 0)], 5)
-        first_layer(6, 0, 7)
-        second_layer([(1, 2), (1, 3)], 4)
-        first_layer(7, 0, 5)
-        turn_and_quantise(3, 0, 3)
-        first_layer(6, 1, 6)
-        second_layer([(2, 1)], 0)
-        first_layer(7, 1, 7)
-        turn_and_quantise(3, 1, 0)
-        second_layer([(3, 0)], 6)
-        second_layer([(2, 2)], 7)
-        second_layer([(3, 1), (3, 2)], 2)
-        second_layer([(2, 3), (3, 3)], 4)
-
-        for c, n in msgs:
+        def send(c, n, y=None):
+            if y is None:
+                y = next_bank()
+            for t in range(2):
+                for b in range(2):
+                    nc.tensor.matmul_mx(
+                        out=y[:, t * P : (t + 1) * P],
+                        lhsT=wd_w[:, b, 2 * P * n : 2 * P * (n + 1)].bitcast(FP4X4),
+                        lhsT_scale=wd_sc[:, b, P * n : P * (n + 1)],
+                        rhs=h_w[c][:, b, t * P : (t + 1) * P].bitcast(FP8X4),
+                        rhs_scale=h_sc[c][:, b, t * P : (t + 1) * P],
+                        start=(b == 0),
+                        stop=(b == 1),
+                    )
+            msg = held("msg%d%d" % (c, n), [P, CHUNK], F32)
+            nc.scalar.copy(msg[:], y[:, 0:CHUNK])
             j0 = c * CHUNK
             nc.vector.tensor_tensor(
                 placed[n][:].indirect(dst_list[:, j0 // GROUP : (j0 + CHUNK) // GROUP]),
-                msgs[c, n],
+                msg[:],
                 gain[:, j0 : j0 + CHUNK],
                 MULT,
             )
-        for n in range(4):
-            nc.sync.dma_start(out[n * P : (n + 1) * P, :], placed[n][:])
+            return y
+
+        first_layer(0)
+        first_layer(1)
+        turn_and_quantise(0, 0)
+        turn_and_quantise(0, 1)
+        for c in range(CHUNKS - 1):
+            send(c, 0)
+            send(c, 1)
+            turn_and_quantise(c + 1, 0)
+            turn_and_quantise(c + 1, 1)
+            send(c, 2)
+            if c + 2 < CHUNKS:
+                send(c, 3)
+                first_layer(c + 2)
+        last = [send(CHUNKS - 1, n) for n in range(3)]
+        send(CHUNKS - 2, 3, last[1])
+        send(CHUNKS - 1, 3, last[2])
+        for n, page in enumerate(placed):
+            nc.sync.dma_start(out[n * P : (n + 1) * P, :], page[:])

@@ -61,19 +61,22 @@ def tile_list_msg_relu_none_kernel(
             nc.sync.dma_start(words[:].bitcast(I32), tab_words[a].rearrange("p t i -> p (t i)").bitcast(I32))
             return words
 
-        def load_wt(a, c0, c1):
-            raw = held("wt_raw%d_%d" % (a, c0), [P, 4, c1 - c0], F32)
-            nc.sync.dma_start(raw[:], wt[a * HALF : (a + 1) * HALF, c0:c1].rearrange("(p i) c -> p i c", i=4))
+        def load_wt(a, b):
+            raw = held("wt_raw%d%d" % (a, b), [P, 4, HALF], F32)
+            rows = wt[a * HALF : (a + 1) * HALF, b * HALF : (b + 1) * HALF]
+            nc.sync.dma_start(raw[:], rows.rearrange("(p i) c -> p i c", i=4))
             return raw
 
-        def load_packed(name, words, plane, rows):
+        def load_rows(plane, rows):
             for q in range(4):
                 nc.sync.dma_start(
                     plane[32 * q : 32 * q + 4, :, :].bitcast(I32),
                     rows[:, 4 * q : 4 * q + 4, :].rearrange("a r n -> r a n").bitcast(I32),
                 )
-            codes = held(name, [P, 2, words.shape[2]], U8)
-            nc.sync.dma_start(codes[:].bitcast(I32), words.rearrange("a p x -> p a x").bitcast(I32))
+
+        def load_words(name, words):
+            codes = held(name, [P, words.shape[1]], U8)
+            nc.sync.dma_start(codes[:].bitcast(I32), words.bitcast(I32))
             return codes
 
         src_list = lists.tile([P, J // GROUP], U16, name="src_list")
@@ -84,38 +87,6 @@ def tile_list_msg_relu_none_kernel(
             nc.sync.dma_start(
                 tab_sc[32 * q : 32 * q + 8, :].bitcast(I32), tab_scales[:, 4 * q : 4 * q + 4, :].bitcast(I32)
             )
-        tab_w = [load_tab(0)]
-        quarters = [(0, 0), (0, 1), (1, 0), (1, 1)]
-        raws = [[load_wt(a, b * HALF, (b + 1) * HALF)] for a, b in quarters[:3]]
-        ws_w = load_packed("ws_w", ws_words, ws_sc, ws_scales)
-        tab_w.append(load_tab(1))
-        raws.append([load_wt(1, HALF, HALF + CHUNK), load_wt(1, HALF + CHUNK, R)])
-        wd_w = load_packed("wd_w", wd_words, wd_sc, wd_scales)
-        gain = held("gain", [P, J], F32)
-        nc.sync.dma_start(gain[:], wgo)
-
-        wt_w, wt_sc = {}, {}
-
-        def quantise_wt(i):
-            grouped = held("grouped%d" % i, [P, HALF, 4], BF16, i * STAGE_BYTES)
-            codes = held("wt_w%d" % i, [P, HALF], U32)
-            plane = held("wt_sc%d" % i, [P, HALF], U8)
-            width = HALF // len(raws[i])
-            for piece, raw in enumerate(raws[i]):
-                cols = slice(piece * width, (piece + 1) * width)
-                dst = grouped[:, cols, :].rearrange("p (c u) i -> p c i u", u=4)
-                src = raw[:].rearrange("p i (c u) -> p c i u", u=4)
-                if piece == 0:
-                    nc.scalar.activation(dst, src, COPY)
-                else:
-                    nc.vector.tensor_copy(dst, src)
-                nc.vector.quantize_mx(
-                    out=codes[:, cols].bitcast(FP8X4),
-                    scales=plane[:, cols],
-                    in_=grouped[:, cols, :].rearrange("p c i -> p (c i)"),
-                )
-            wt_w[quarters[i]], wt_sc[quarters[i]] = codes, plane
-
         picked = {}
 
         def gather(name, window, edge_list, dtype, j0, j1, offset=None):
@@ -125,29 +96,60 @@ def tile_list_msg_relu_none_kernel(
                 picked[name, t] = (got, t * P - j0)
             return got
 
+        raw = {(0, 0): load_wt(0, 0)}
+        tab_w = [load_tab(0)]
+        raw[0, 1] = load_wt(0, 1)
+        raw[1, 0] = load_wt(1, 0)
+        load_rows(ws_sc, ws_scales)
+        ws_w = [load_words("ws_w0", ws_words[0])]
+        raw[1, 1] = load_wt(1, 1)
         src_sc = gather("src_sc0", tab_sc, src_list, U8, 0, J)
         for q in range(4):
-            nc.gpsimd.dma_start(
+            nc.sync.dma_start(
                 moved_sc[32 * q : 32 * q + 4, :].bitcast(I32), src_sc[32 * q + 4 : 32 * q + 8, :].bitcast(I32)
             )
         for t in range(J // P):
             picked["src_sc1", t] = (moved_sc, t * P)
-        gather("dst_sc", tab_sc, dst_list, U8, 0, HALF)
-        gather("dst_w0", tab_w[0], dst_list, U32, 0, HALF)
+        tab_w.append(load_tab(1))
+        ws_w.append(load_words("ws_w1", ws_words[1]))
+        load_rows(wd_sc, wd_scales)
+        wd_w = held("wd_w", [P, 2, 2 * N], U8)
+        nc.sync.dma_start(wd_w[:].bitcast(I32), wd_words.rearrange("a p x -> p a x").bitcast(I32))
+        gain = held("gain", [P, J], F32)
+        nc.sync.dma_start(gain[:], wgo)
+
+        wt_w, wt_sc = {}, {}
+
+        def quantise_wt(a, b, pieces=1, offset=None):
+            grouped = held("grouped%d%d" % (a, b), [P, HALF, 4], BF16, offset)
+            wt_w[a, b] = held("wt_w%d%d" % (a, b), [P, HALF], U32)
+            wt_sc[a, b] = held("wt_sc%d%d" % (a, b), [P, HALF], U8)
+            width = HALF // pieces
+            for c0 in range(0, HALF, width):
+                cols = slice(c0, c0 + width)
+                nc.scalar.activation(
+                    grouped[:, cols, :].rearrange("p (c u) i -> p c i u", u=4),
+                    raw[a, b][:, :, cols].rearrange("p i (c u) -> p c i u", u=4),
+                    COPY,
+                )
+                nc.vector.quantize_mx(
+                    out=wt_w[a, b][:, cols].bitcast(FP8X4),
+                    scales=wt_sc[a, b][:, cols],
+                    in_=grouped[:, cols, :].rearrange("p c i -> p (c i)"),
+                )
+
+        gather("dst_sc", tab_sc, dst_list, U8, 0, J)
+        quantise_wt(0, 0)
+        gather("dst_w0", tab_w[0], dst_list, U32, 0, J)
         gather("src_w0", tab_w[0], src_list, U32, 0, HALF)
-        quantise_wt(0)
-        gather("dst_w0", tab_w[0], dst_list, U32, HALF, J, 0)
-        gather("src_w0", tab_w[0], src_list, U32, HALF, J, 4 * HALF)
-        quantise_wt(1)
-        gather("dst_sc", tab_sc, dst_list, U8, HALF, J, STAGE_BYTES)
-        quantise_wt(2)
-        for c in range(2):
-            at = 2 * STAGE_BYTES + 8 * CHUNK * c
-            gather("dst_w1", tab_w[1], dst_list, U32, c * CHUNK, (c + 1) * CHUNK, at)
-            gather("src_w1", tab_w[1], src_list, U32, c * CHUNK, (c + 1) * CHUNK, at + 4 * CHUNK)
-        quantise_wt(3)
-        gather("dst_w1", tab_w[1], dst_list, U32, HALF, J, 3 * STAGE_BYTES)
-        gather("src_w1", tab_w[1], src_list, U32, HALF, J, 3 * STAGE_BYTES + 4 * HALF)
+        quantise_wt(0, 1, 1, 0)
+        gather("src_w0", tab_w[0], src_list, U32, HALF, J, 0)
+        quantise_wt(1, 0)
+        quantise_wt(1, 1, 2)
+        for j0 in (0, CHUNK):
+            gather("dst_w1", tab_w[1], dst_list, U32, j0, j0 + CHUNK)
+            gather("src_w1", tab_w[1], src_list, U32, j0, j0 + CHUNK)
+        gather("src_w1", tab_w[1], src_list, U32, HALF, J)
 
         ident = held("ident", [P, P], F32)
         make_identity(nc, ident[:])
@@ -156,7 +158,6 @@ def tile_list_msg_relu_none_kernel(
             for c0 in range(0, T, CHUNK):
                 nc.gpsimd.memset(page[:, c0 : c0 + CHUNK], 0.0)
 
-        relu = [[held("relu%d%d" % (s, t), [P, HALF], BF16) for t in range(2)] for s in range(2)]
         h_w = [held("h_w%d" % c, [P, 2, CHUNK], U32) for c in range(CHUNKS)]
         h_sc = [held("h_sc%d" % c, [P, 2, CHUNK], U8) for c in range(CHUNKS)]
         sums = {}
@@ -165,42 +166,47 @@ def tile_list_msg_relu_none_kernel(
             got, at = picked[name, t]
             return got[row:P, at : at + P]
 
-        def first_layer(c):
+        def first_layer(c, steps):
             for b in range(2):
                 for t in (2 * c, 2 * c + 1):
-                    target = [
-                        (edge_cols("dst_w%d" % a, t).bitcast(FP8X4), edge_cols("dst_sc", t, 4 * a),
-                         wt_w[a, b][:].bitcast(FP8X4), wt_sc[a, b][:])
-                        for a in range(2)
-                    ]
-                    source = [
-                        (edge_cols("src_w%d" % a, t).bitcast(FP8X4), edge_cols("src_sc%d" % a, t),
-                         ws_w[:, a, 2 * HALF * b : 2 * HALF * (b + 1)].bitcast(FP4X4),
-                         ws_sc[:, a, b * HALF : (b + 1) * HALF])
-                        for a in range(2)
-                    ]
-                    passes = [target[0], source[0]] + ([target[1], source[1]] if b == 0 else [source[1], target[1]])
-                    acc = next_bank()
-                    for i, (lhs, lhs_sc, rhs, rhs_sc) in enumerate(passes):
-                        nc.tensor.matmul_mx(out=acc[:], lhsT=lhs, lhsT_scale=lhs_sc, rhs=rhs, rhs_scale=rhs_sc,
-                                            start=(i == 0), stop=(i == len(passes) - 1))
-                    sums[t, b] = acc
+                    for a in steps:
+                        if a == 0:
+                            sums[t, b] = next_bank()
+                        nc.tensor.matmul_mx(
+                            out=sums[t, b][:],
+                            lhsT=edge_cols("dst_w%d" % a, t).bitcast(FP8X4),
+                            lhsT_scale=edge_cols("dst_sc", t, 4 * a),
+                            rhs=wt_w[a, b][:].bitcast(FP8X4),
+                            rhs_scale=wt_sc[a, b][:],
+                            start=(a == 0),
+                            stop=False,
+                        )
+                        nc.tensor.matmul_mx(
+                            out=sums[t, b][:],
+                            lhsT=edge_cols("src_w%d" % a, t).bitcast(FP8X4),
+                            lhsT_scale=edge_cols("src_sc%d" % a, t),
+                            rhs=ws_w[a][:, 2 * HALF * b : 2 * HALF * (b + 1)].bitcast(FP4X4),
+                            rhs_scale=ws_sc[:, a, b * HALF : (b + 1) * HALF],
+                            start=False,
+                            stop=(a == 1),
+                        )
 
-        def turn_and_quantise(c, b):
-            rows = relu[(c + b) % 2]
+        def rectify(c, b, rows):
             for t in range(2):
                 nc.scalar.activation(
                     rows[t][:].rearrange("p (u m e) -> p u m e", u=2, e=2),
                     sums[2 * c + t, b][:].rearrange("p (m u e) -> p u m e", u=2, e=2),
                     RELU,
                 )
+
+        def turn_and_quantise(c, b, rows, offset=None):
             turned = next_bank()
+            h_in = held("h_in%d%d" % (c, b), [P, 2, P, 2], F32, offset)
             for t in range(2):
                 pairs = rows[t][:].bitcast(F32)
                 for u in range(2):
                     at = (2 * t + u) * P
                     nc.tensor.transpose(turned[:, at : at + P], pairs[:, u * P : (u + 1) * P], ident[:])
-            h_in = held("h_in%d%d" % (c, b), [P, 2, P, 2], F32)
             nc.scalar.copy(h_in[:], turned[:].rearrange("p (t u j) -> p t j u", j=P, u=2))
             nc.vector.quantize_mx(
                 out=h_w[c][:, b, :].bitcast(FP8X4),
@@ -233,19 +239,29 @@ def tile_list_msg_relu_none_kernel(
             )
             return y
 
-        first_layer(0)
-        first_layer(1)
-        turn_and_quantise(0, 0)
-        turn_and_quantise(0, 1)
+        first_layer(0, (0,))
+        first_layer(1, (0,))
+        first_layer(0, (1,))
+        relu = [[held("relu%d%d" % (b, t), [P, HALF], BF16) for t in range(2)] for b in range(2)]
+        after = STAGE_BYTES
+        rectify(0, 0, relu[0])
+        rectify(0, 1, relu[1])
+        turn_and_quantise(0, 0, relu[0])
+        turn_and_quantise(0, 1, relu[1], after + 4 * HALF - 64)
+        gather("dst_w1", tab_w[1], dst_list, U32, HALF, J, after)
+        relu[1] = [held("relu2%d" % t, [P, HALF], BF16, after + 4 * HALF + 2 * HALF * t) for t in range(2)]
         for c in range(CHUNKS - 1):
             send(c, 0)
+            if c == 0:
+                first_layer(1, (1,))
             send(c, 1)
-            turn_and_quantise(c + 1, 0)
-            turn_and_quantise(c + 1, 1)
+            for b in range(2):
+                rectify(c + 1, b, relu[(c + 1 + b) % 2])
+                turn_and_quantise(c + 1, b, relu[(c + 1 + b) % 2])
             send(c, 2)
             if c + 2 < CHUNKS:
                 send(c, 3)
-                first_layer(c + 2)
+                first_layer(c + 2, (0, 1))
         last = [send(CHUNKS - 1, n) for n in range(3)]
         send(CHUNKS - 2, 3, last[1])
         send(CHUNKS - 1, 3, last[2])

@@ -25,6 +25,7 @@ CHUNK = 256
 CHUNKS = J // CHUNK
 BANKS = 8
 STAGE_BYTES = 2 * 4 * HALF
+STEPS = ((("dst", 0), ("src", 0), ("dst", 1), ("src", 1)), (("dst", 0), ("src", 0), ("src", 1), ("dst", 1)))
 
 
 def tile_list_msg_relu_none_kernel(
@@ -53,7 +54,8 @@ def tile_list_msg_relu_none_kernel(
         ws_sc = held("ws_sc", [P, 2, R], U8)
         wd_sc = held("wd_sc", [P, 2, N], U8)
         moved_sc = held("moved_sc", [P, J], U8)
-        for plane in (tab_sc, ws_sc, wd_sc, moved_sc):
+        nc.gpsimd.memset(tab_sc[:].bitcast(I32), 0)
+        for plane in (ws_sc, wd_sc, moved_sc):
             nc.vector.memset(plane[:].bitcast(I32), 0)
 
         def load_tab(a):
@@ -61,17 +63,16 @@ def tile_list_msg_relu_none_kernel(
             nc.sync.dma_start(words[:].bitcast(I32), tab_words[a].rearrange("p t i -> p (t i)").bitcast(I32))
             return words
 
-        def load_wt(a, b):
-            raw = held("wt_raw%d%d" % (a, b), [P, 4, HALF], F32)
-            rows = wt[a * HALF : (a + 1) * HALF, b * HALF : (b + 1) * HALF]
-            nc.sync.dma_start(raw[:], rows.rearrange("(p i) c -> p i c", i=4))
+        def load_wt(a, c0, width, queue=nc.sync):
+            raw = held("wt_raw%d_%d" % (a, c0), [P, 4, width], F32)
+            rows = wt[a * HALF : (a + 1) * HALF, c0 : c0 + width]
+            queue.dma_start(raw[:], rows.rearrange("(p i) c -> p i c", i=4))
             return raw
 
         def load_rows(plane, rows):
-            for q in range(4):
+            for r in range(4):
                 nc.sync.dma_start(
-                    plane[32 * q : 32 * q + 4, :, :].bitcast(I32),
-                    rows[:, 4 * q : 4 * q + 4, :].rearrange("a r n -> r a n").bitcast(I32),
+                    plane[r:P:32, :, :].bitcast(I32), rows[:, r:16:4, :].rearrange("a q n -> q a n").bitcast(I32)
                 )
 
         def load_words(name, words):
@@ -96,21 +97,20 @@ def tile_list_msg_relu_none_kernel(
                 picked[name, t] = (got, t * P - j0)
             return got
 
-        raw = {(0, 0): load_wt(0, 0)}
+        raw = {(0, 0): [load_wt(0, 0, HALF, nc.scalar)]}
         tab_w = [load_tab(0)]
-        raw[0, 1] = load_wt(0, 1)
-        raw[1, 0] = load_wt(1, 0)
         load_rows(ws_sc, ws_scales)
+        raw[0, 1] = [load_wt(0, HALF, HALF)]
+        raw[1, 0] = [load_wt(1, 0, HALF)]
         ws_w = [load_words("ws_w0", ws_words[0])]
-        raw[1, 1] = load_wt(1, 1)
+        raw[1, 1] = [load_wt(1, HALF, CHUNK)]
         src_sc = gather("src_sc0", tab_sc, src_list, U8, 0, J)
-        for q in range(4):
-            nc.sync.dma_start(
-                moved_sc[32 * q : 32 * q + 4, :].bitcast(I32), src_sc[32 * q + 4 : 32 * q + 8, :].bitcast(I32)
-            )
+        for r in range(4):
+            nc.sync.dma_start(moved_sc[r:P:32, :].bitcast(I32), src_sc[4 + r : P : 32, :].bitcast(I32))
         for t in range(J // P):
             picked["src_sc1", t] = (moved_sc, t * P)
         tab_w.append(load_tab(1))
+        raw[1, 1].append(load_wt(1, HALF + CHUNK, CHUNK))
         ws_w.append(load_words("ws_w1", ws_words[1]))
         load_rows(wd_sc, wd_scales)
         wd_w = held("wd_w", [P, 2, 2 * N], U8)
@@ -120,18 +120,19 @@ def tile_list_msg_relu_none_kernel(
 
         wt_w, wt_sc = {}, {}
 
-        def quantise_wt(a, b, pieces=1, offset=None):
+        def quantise_wt(a, b, offset=None):
             grouped = held("grouped%d%d" % (a, b), [P, HALF, 4], BF16, offset)
             wt_w[a, b] = held("wt_w%d%d" % (a, b), [P, HALF], U32)
             wt_sc[a, b] = held("wt_sc%d%d" % (a, b), [P, HALF], U8)
-            width = HALF // pieces
-            for c0 in range(0, HALF, width):
-                cols = slice(c0, c0 + width)
-                nc.scalar.activation(
-                    grouped[:, cols, :].rearrange("p (c u) i -> p c i u", u=4),
-                    raw[a, b][:, :, cols].rearrange("p i (c u) -> p c i u", u=4),
-                    COPY,
-                )
+            width = HALF // len(raw[a, b])
+            for i, piece in enumerate(raw[a, b]):
+                cols = slice(i * width, (i + 1) * width)
+                dst = grouped[:, cols, :].rearrange("p (c u) i -> p c i u", u=4)
+                src = piece[:].rearrange("p i (c u) -> p c i u", u=4)
+                if i == 0:
+                    nc.scalar.activation(dst, src, COPY)
+                else:
+                    nc.vector.tensor_copy(dst, src)
                 nc.vector.quantize_mx(
                     out=wt_w[a, b][:, cols].bitcast(FP8X4),
                     scales=wt_sc[a, b][:, cols],
@@ -142,14 +143,15 @@ def tile_list_msg_relu_none_kernel(
         quantise_wt(0, 0)
         gather("dst_w0", tab_w[0], dst_list, U32, 0, J)
         gather("src_w0", tab_w[0], src_list, U32, 0, HALF)
-        quantise_wt(0, 1, 1, 0)
+        quantise_wt(0, 1, 0)
         gather("src_w0", tab_w[0], src_list, U32, HALF, J, 0)
         quantise_wt(1, 0)
-        quantise_wt(1, 1, 2)
-        for j0 in (0, CHUNK):
-            gather("dst_w1", tab_w[1], dst_list, U32, j0, j0 + CHUNK)
-            gather("src_w1", tab_w[1], src_list, U32, j0, j0 + CHUNK)
-        gather("src_w1", tab_w[1], src_list, U32, HALF, J)
+        quantise_wt(1, 1, 3 * STAGE_BYTES)
+        gather("dst_w1", tab_w[1], dst_list, U32, 0, CHUNK)
+        gather("src_w1", tab_w[1], src_list, U32, 0, CHUNK)
+        gather("dst_w1", tab_w[1], dst_list, U32, CHUNK, HALF, 3 * STAGE_BYTES)
+        gather("src_w1", tab_w[1], src_list, U32, CHUNK, HALF, 3 * STAGE_BYTES + 4 * CHUNK)
+        gather("src_w1", tab_w[1], src_list, U32, HALF, J, 3 * STAGE_BYTES + 4 * HALF)
 
         ident = held("ident", [P, P], F32)
         make_identity(nc, ident[:])
@@ -166,29 +168,28 @@ def tile_list_msg_relu_none_kernel(
             got, at = picked[name, t]
             return got[row:P, at : at + P]
 
-        def first_layer(c, steps):
-            for b in range(2):
-                for t in (2 * c, 2 * c + 1):
-                    for a in steps:
-                        if a == 0:
+        def first_layer(c, first, last, groups=range(4)):
+            for g in groups:
+                for b, t in ((g // 2, 2 * c + g % 2),):
+                    for i in range(first, last):
+                        side, a = STEPS[b][i]
+                        if i == 0:
                             sums[t, b] = next_bank()
+                        if side == "dst":
+                            lhs_sc = edge_cols("dst_sc", t, 4 * a)
+                            rhs, rhs_sc = wt_w[a, b][:].bitcast(FP8X4), wt_sc[a, b][:]
+                        else:
+                            lhs_sc = edge_cols("src_sc%d" % a, t)
+                            rhs = ws_w[a][:, 2 * HALF * b : 2 * HALF * (b + 1)].bitcast(FP4X4)
+                            rhs_sc = ws_sc[:, a, b * HALF : (b + 1) * HALF]
                         nc.tensor.matmul_mx(
                             out=sums[t, b][:],
-                            lhsT=edge_cols("dst_w%d" % a, t).bitcast(FP8X4),
-                            lhsT_scale=edge_cols("dst_sc", t, 4 * a),
-                            rhs=wt_w[a, b][:].bitcast(FP8X4),
-                            rhs_scale=wt_sc[a, b][:],
-                            start=(a == 0),
-                            stop=False,
-                        )
-                        nc.tensor.matmul_mx(
-                            out=sums[t, b][:],
-                            lhsT=edge_cols("src_w%d" % a, t).bitcast(FP8X4),
-                            lhsT_scale=edge_cols("src_sc%d" % a, t),
-                            rhs=ws_w[a][:, 2 * HALF * b : 2 * HALF * (b + 1)].bitcast(FP4X4),
-                            rhs_scale=ws_sc[:, a, b * HALF : (b + 1) * HALF],
-                            start=False,
-                            stop=(a == 1),
+                            lhsT=edge_cols("%s_w%d" % (side, a), t).bitcast(FP8X4),
+                            lhsT_scale=lhs_sc,
+                            rhs=rhs,
+                            rhs_scale=rhs_sc,
+                            start=(i == 0),
+                            stop=(i == 3),
                         )
 
         def rectify(c, b, rows):
@@ -213,20 +214,21 @@ def tile_list_msg_relu_none_kernel(
                 scales=h_sc[c][:, b, :],
                 in_=h_in[:].rearrange("p t j u -> p (t j u)").bitcast(BF16),
             )
+            return turned
 
         def send(c, n, y=None):
             if y is None:
                 y = next_bank()
             for t in range(2):
-                for b in range(2):
+                for b in (1, 0):
                     nc.tensor.matmul_mx(
                         out=y[:, t * P : (t + 1) * P],
                         lhsT=wd_w[:, b, 2 * P * n : 2 * P * (n + 1)].bitcast(FP4X4),
                         lhsT_scale=wd_sc[:, b, P * n : P * (n + 1)],
                         rhs=h_w[c][:, b, t * P : (t + 1) * P].bitcast(FP8X4),
                         rhs_scale=h_sc[c][:, b, t * P : (t + 1) * P],
-                        start=(b == 0),
-                        stop=(b == 1),
+                        start=(b == 1),
+                        stop=(b == 0),
                     )
             msg = held("msg%d%d" % (c, n), [P, CHUNK], F32)
             nc.scalar.copy(msg[:], y[:, 0:CHUNK])
@@ -239,9 +241,9 @@ def tile_list_msg_relu_none_kernel(
             )
             return y
 
-        first_layer(0, (0,))
-        first_layer(1, (0,))
-        first_layer(0, (1,))
+        first_layer(0, 0, 2)
+        first_layer(1, 0, 2)
+        first_layer(0, 2, 4)
         relu = [[held("relu%d%d" % (b, t), [P, HALF], BF16) for t in range(2)] for b in range(2)]
         after = STAGE_BYTES
         rectify(0, 0, relu[0])
@@ -250,20 +252,30 @@ def tile_list_msg_relu_none_kernel(
         turn_and_quantise(0, 1, relu[1], after + 4 * HALF - 64)
         gather("dst_w1", tab_w[1], dst_list, U32, HALF, J, after)
         relu[1] = [held("relu2%d" % t, [P, HALF], BF16, after + 4 * HALF + 2 * HALF * t) for t in range(2)]
-        for c in range(CHUNKS - 1):
+
+        def finish_hidden(c):
+            for b in range(2):
+                rectify(c, b, relu[(c + b) % 2])
+                turned = turn_and_quantise(c, b, relu[(c + b) % 2])
+            return turned
+
+        for c in range(CHUNKS - 2):
             send(c, 0)
             if c == 0:
-                first_layer(1, (1,))
+                first_layer(1, 2, 4)
             send(c, 1)
-            for b in range(2):
-                rectify(c + 1, b, relu[(c + 1 + b) % 2])
-                turn_and_quantise(c + 1, b, relu[(c + 1 + b) % 2])
+            if c > 0:
+                first_layer(c + 1, 0, 4, range(3, 4))
+            finish_hidden(c + 1)
             send(c, 2)
-            if c + 2 < CHUNKS:
-                send(c, 3)
-                first_layer(c + 2, (0, 1))
-        last = [send(CHUNKS - 1, n) for n in range(3)]
-        send(CHUNKS - 2, 3, last[1])
-        send(CHUNKS - 1, 3, last[2])
+            send(c, 3)
+            first_layer(c + 2, 0, 4, range(3))
+        send(2, 0)
+        send(2, 1)
+        first_layer(3, 0, 4, range(3, 4))
+        send(2, 2, finish_hidden(3))
+        last = [send(3, n) for n in range(3)]
+        send(2, 3, last[1])
+        send(3, 3, last[2])
         for n, page in enumerate(placed):
             nc.sync.dma_start(out[n * P : (n + 1) * P, :], page[:])

@@ -157,8 +157,7 @@ def tile_list_msg_relu_none_kernel(
         make_identity(nc, ident[:])
         placed = [held("placed%d" % n, [P, T], F32) for n in range(N // P)]
         for page in placed:
-            for c0 in range(0, T, CHUNK):
-                nc.gpsimd.memset(page[:, c0 : c0 + CHUNK], 0.0)
+            nc.gpsimd.memset(page[:], 0.0)
 
         h_w = [held("h_w%d" % c, [P, 2, CHUNK], U32) for c in range(CHUNKS)]
         h_sc = [held("h_sc%d" % c, [P, 2, CHUNK], U8) for c in range(CHUNKS)]

@@ -25,6 +25,8 @@ CHUNK = 256
 CHUNKS = J // CHUNK
 BANKS = 8
 STAGE_BYTES = 2 * 4 * HALF
+PLANE_AT = 4 * STAGE_BYTES
+RAW_AT = 5 * STAGE_BYTES
 STEPS = ((("dst", 0), ("src", 0), ("dst", 1), ("src", 1)), (("dst", 0), ("src", 0), ("src", 1), ("dst", 1)))
 
 
@@ -50,21 +52,16 @@ def tile_list_msg_relu_none_kernel(
             uses.append(len(uses))
             return banks[uses[-1] % BANKS]
 
-        tab_sc = held("tab_sc", [P, T], U8)
-        ws_sc = held("ws_sc", [P, 2, R], U8)
-        wd_sc = held("wd_sc", [P, 2, N], U8)
-        moved_sc = held("moved_sc", [P, J], U8)
+        tab_sc = held("tab_sc", [P, T], U8, PLANE_AT)
         nc.gpsimd.memset(tab_sc[:].bitcast(I32), 0)
-        for plane in (ws_sc, wd_sc, moved_sc):
-            nc.vector.memset(plane[:].bitcast(I32), 0)
 
         def load_tab(a):
             words = held("tab_w%d" % a, [P, T], U32)
             nc.sync.dma_start(words[:].bitcast(I32), tab_words[a].rearrange("p t i -> p (t i)").bitcast(I32))
             return words
 
-        def load_wt(a, c0, width, queue=nc.sync):
-            raw = held("wt_raw%d_%d" % (a, c0), [P, 4, width], F32)
+        def load_wt(a, c0, width, queue=nc.sync, offset=None):
+            raw = held("wt_raw%d_%d" % (a, c0), [P, 4, width], F32, offset)
             rows = wt[a * HALF : (a + 1) * HALF, c0 : c0 + width]
             queue.dma_start(raw[:], rows.rearrange("(p i) c -> p i c", i=4))
             return raw
@@ -97,27 +94,6 @@ def tile_list_msg_relu_none_kernel(
                 picked[name, t] = (got, t * P - j0)
             return got
 
-        raw = {(0, 0): [load_wt(0, 0, HALF, nc.scalar)]}
-        tab_w = [load_tab(0)]
-        load_rows(ws_sc, ws_scales)
-        raw[0, 1] = [load_wt(0, HALF, HALF)]
-        raw[1, 0] = [load_wt(1, 0, HALF)]
-        ws_w = [load_words("ws_w0", ws_words[0])]
-        raw[1, 1] = [load_wt(1, HALF, CHUNK)]
-        src_sc = gather("src_sc0", tab_sc, src_list, U8, 0, J)
-        for r in range(4):
-            nc.sync.dma_start(moved_sc[r:P:32, :].bitcast(I32), src_sc[4 + r : P : 32, :].bitcast(I32))
-        for t in range(J // P):
-            picked["src_sc1", t] = (moved_sc, t * P)
-        tab_w.append(load_tab(1))
-        raw[1, 1].append(load_wt(1, HALF + CHUNK, CHUNK))
-        ws_w.append(load_words("ws_w1", ws_words[1]))
-        load_rows(wd_sc, wd_scales)
-        wd_w = held("wd_w", [P, 2, 2 * N], U8)
-        nc.sync.dma_start(wd_w[:].bitcast(I32), wd_words.rearrange("a p x -> p a x").bitcast(I32))
-        gain = held("gain", [P, J], F32)
-        nc.sync.dma_start(gain[:], wgo)
-
         wt_w, wt_sc = {}, {}
 
         def quantise_wt(a, b, offset=None):
@@ -139,8 +115,32 @@ def tile_list_msg_relu_none_kernel(
                     in_=grouped[:, cols, :].rearrange("p c i -> p (c i)"),
                 )
 
-        gather("dst_sc", tab_sc, dst_list, U8, 0, J)
+        raw = {(0, 0): [load_wt(0, 0, HALF, nc.scalar, RAW_AT)]}
+        tab_w = [load_tab(0)]
+        raw[0, 1] = [load_wt(0, HALF, HALF)]
+        raw[1, 0] = [load_wt(1, 0, HALF)]
         quantise_wt(0, 0)
+        ws_sc = held("ws_sc", [P, 2, R], U8, RAW_AT)
+        load_rows(ws_sc, ws_scales)
+        ws_w = [load_words("ws_w0", ws_words[0])]
+        raw[1, 1] = [load_wt(1, HALF, CHUNK)]
+        src_sc = gather("src_sc0", tab_sc, src_list, U8, 0, J)
+        gather("dst_sc", tab_sc, dst_list, U8, 0, J)
+        moved_sc = held("moved_sc", [P, J], U8, PLANE_AT)
+        wd_sc = held("wd_sc", [P, 2, N], U8, PLANE_AT + J)
+        for r in range(4):
+            nc.sync.dma_start(moved_sc[r:P:32, :].bitcast(I32), src_sc[4 + r : P : 32, :].bitcast(I32))
+        for t in range(J // P):
+            picked["src_sc1", t] = (moved_sc, t * P)
+        tab_w.append(load_tab(1))
+        raw[1, 1].append(load_wt(1, HALF + CHUNK, CHUNK))
+        ws_w.append(load_words("ws_w1", ws_words[1]))
+        load_rows(wd_sc, wd_scales)
+        wd_w = held("wd_w", [P, 2, 2 * N], U8)
+        nc.sync.dma_start(wd_w[:].bitcast(I32), wd_words.rearrange("a p x -> p a x").bitcast(I32))
+        gain = held("gain", [P, J], F32)
+        nc.sync.dma_start(gain[:], wgo)
+
         gather("dst_w0", tab_w[0], dst_list, U32, 0, J)
         gather("src_w0", tab_w[0], src_list, U32, 0, HALF)
         quantise_wt(0, 1, 0)

@@ -24,10 +24,15 @@ GROUP = 16
 CHUNK = 256
 CHUNKS = J // CHUNK
 BANKS = 8
-STAGE_BYTES = 2 * 4 * HALF
-PLANE_AT = 4 * STAGE_BYTES
-RAW_AT = 5 * STAGE_BYTES
+ALIGN = 64
+WORD = 4
 STEPS = ((("dst", 0), ("src", 0), ("dst", 1), ("src", 1)), (("dst", 0), ("src", 0), ("src", 1), ("dst", 1)))
+EARLY_GROUPS = 3
+STAGE_BYTES = 2 * 4 * HALF
+SECOND_AT = 0
+TURNED_AT = STAGE_BYTES
+LAST_AT = 3 * STAGE_BYTES
+FIRST_AT = 5 * STAGE_BYTES
 
 
 def tile_list_msg_relu_none_kernel(
@@ -42,8 +47,8 @@ def tile_list_msg_relu_none_kernel(
 
         def held(name, shape, dtype, offset=None):
             if offset is None:
-                return keep.tile(shape, dtype, name=name, align_bytes=64)
-            return shared.tile(shape, dtype, name=name, align_bytes=64, offset=offset)
+                return keep.tile(shape, dtype, name=name, align_bytes=ALIGN)
+            return shared.tile(shape, dtype, name=name, align_bytes=ALIGN, offset=offset)
 
         banks = [psum.tile([P, HALF], F32, name="bank%d" % i) for i in range(BANKS)]
         uses = []
@@ -52,7 +57,7 @@ def tile_list_msg_relu_none_kernel(
             uses.append(len(uses))
             return banks[uses[-1] % BANKS]
 
-        tab_sc = held("tab_sc", [P, T], U8, PLANE_AT)
+        tab_sc = held("tab_sc", [P, T], U8)
         nc.gpsimd.memset(tab_sc[:].bitcast(I32), 0)
 
         def load_tab(a):
@@ -60,16 +65,16 @@ def tile_list_msg_relu_none_kernel(
             nc.sync.dma_start(words[:].bitcast(I32), tab_words[a].rearrange("p t i -> p (t i)").bitcast(I32))
             return words
 
-        def load_wt(a, c0, width, queue=nc.sync, offset=None):
-            raw = held("wt_raw%d_%d" % (a, c0), [P, 4, width], F32, offset)
+        def load_wt(a, c0, width, queue=nc.sync):
+            piece = held("wt_raw%d_%d" % (a, c0), [P, 4, width], F32)
             rows = wt[a * HALF : (a + 1) * HALF, c0 : c0 + width]
-            queue.dma_start(raw[:], rows.rearrange("(p i) c -> p i c", i=4))
-            return raw
+            queue.dma_start(piece[:], rows.rearrange("(p i) c -> p i c", i=4))
+            return piece
 
-        def load_rows(plane, rows):
+        def load_rows(planes, rows):
             for r in range(4):
                 nc.sync.dma_start(
-                    plane[r:P:32, :, :].bitcast(I32), rows[:, r:16:4, :].rearrange("a q n -> q a n").bitcast(I32)
+                    planes[r:P:32, :, :].bitcast(I32), rows[:, r:16:4, :].rearrange("a q n -> q a n").bitcast(I32)
                 )
 
         def load_words(name, words):
@@ -115,25 +120,25 @@ def tile_list_msg_relu_none_kernel(
                     in_=grouped[:, cols, :].rearrange("p c i -> p (c i)"),
                 )
 
-        raw = {(0, 0): [load_wt(0, 0, HALF, nc.scalar, RAW_AT)]}
+        raw = {(0, 0): [load_wt(0, 0, HALF, nc.scalar)]}
         tab_w = [load_tab(0)]
         raw[0, 1] = [load_wt(0, HALF, HALF)]
         raw[1, 0] = [load_wt(1, 0, HALF)]
-        quantise_wt(0, 0)
-        ws_sc = held("ws_sc", [P, 2, R], U8, RAW_AT)
+        quantise_wt(0, 0, FIRST_AT)
+        ws_sc = held("ws_sc", [P, 2, R], U8)
         load_rows(ws_sc, ws_scales)
         ws_w = [load_words("ws_w0", ws_words[0])]
-        raw[1, 1] = [load_wt(1, HALF, CHUNK)]
+        raw[1, 1] = [load_wt(1, HALF, HALF // 2)]
         src_sc = gather("src_sc0", tab_sc, src_list, U8, 0, J)
         gather("dst_sc", tab_sc, dst_list, U8, 0, J)
-        moved_sc = held("moved_sc", [P, J], U8, PLANE_AT)
-        wd_sc = held("wd_sc", [P, 2, N], U8, PLANE_AT + J)
+        moved_sc = held("moved_sc", [P, J], U8)
+        wd_sc = held("wd_sc", [P, 2, N], U8)
         for r in range(4):
             nc.sync.dma_start(moved_sc[r:P:32, :].bitcast(I32), src_sc[4 + r : P : 32, :].bitcast(I32))
         for t in range(J // P):
             picked["src_sc1", t] = (moved_sc, t * P)
         tab_w.append(load_tab(1))
-        raw[1, 1].append(load_wt(1, HALF + CHUNK, CHUNK))
+        raw[1, 1].append(load_wt(1, HALF + HALF // 2, HALF // 2))
         ws_w.append(load_words("ws_w1", ws_words[1]))
         load_rows(wd_sc, wd_scales)
         wd_w = held("wd_w", [P, 2, 2 * N], U8)
@@ -141,17 +146,18 @@ def tile_list_msg_relu_none_kernel(
         gain = held("gain", [P, J], F32)
         nc.sync.dma_start(gain[:], wgo)
 
-        gather("dst_w0", tab_w[0], dst_list, U32, 0, J)
-        gather("src_w0", tab_w[0], src_list, U32, 0, HALF)
-        quantise_wt(0, 1, 0)
-        gather("src_w0", tab_w[0], src_list, U32, HALF, J, 0)
+        gather("dst_w0", tab_w[0], dst_list, U32, 0, 2 * CHUNK)
+        gather("src_w0", tab_w[0], src_list, U32, 0, 2 * CHUNK, FIRST_AT)
+        quantise_wt(0, 1, SECOND_AT)
+        gather("dst_w0", tab_w[0], dst_list, U32, 2 * CHUNK, J, SECOND_AT)
         quantise_wt(1, 0)
-        quantise_wt(1, 1, 3 * STAGE_BYTES)
+        quantise_wt(1, 1, LAST_AT)
         gather("dst_w1", tab_w[1], dst_list, U32, 0, CHUNK)
         gather("src_w1", tab_w[1], src_list, U32, 0, CHUNK)
-        gather("dst_w1", tab_w[1], dst_list, U32, CHUNK, HALF, 3 * STAGE_BYTES)
-        gather("src_w1", tab_w[1], src_list, U32, CHUNK, HALF, 3 * STAGE_BYTES + 4 * CHUNK)
-        gather("src_w1", tab_w[1], src_list, U32, HALF, J, 3 * STAGE_BYTES + 4 * HALF)
+        gather("dst_w1", tab_w[1], dst_list, U32, CHUNK, 2 * CHUNK, LAST_AT + ALIGN)
+        gather("src_w1", tab_w[1], src_list, U32, CHUNK, 2 * CHUNK, LAST_AT + ALIGN + WORD * CHUNK)
+        gather("src_w1", tab_w[1], src_list, U32, 2 * CHUNK, J, LAST_AT + ALIGN + WORD * 2 * CHUNK)
+        gather("src_w0", tab_w[0], src_list, U32, 2 * CHUNK, J, LAST_AT + ALIGN - WORD * 2 * CHUNK)
 
         ident = held("ident", [P, P], F32)
         make_identity(nc, ident[:])
@@ -169,27 +175,27 @@ def tile_list_msg_relu_none_kernel(
 
         def first_layer(c, first, last, groups=range(4)):
             for g in groups:
-                for b, t in ((g // 2, 2 * c + g % 2),):
-                    for i in range(first, last):
-                        side, a = STEPS[b][i]
-                        if i == 0:
-                            sums[t, b] = next_bank()
-                        if side == "dst":
-                            lhs_sc = edge_cols("dst_sc", t, 4 * a)
-                            rhs, rhs_sc = wt_w[a, b][:].bitcast(FP8X4), wt_sc[a, b][:]
-                        else:
-                            lhs_sc = edge_cols("src_sc%d" % a, t)
-                            rhs = ws_w[a][:, 2 * HALF * b : 2 * HALF * (b + 1)].bitcast(FP4X4)
-                            rhs_sc = ws_sc[:, a, b * HALF : (b + 1) * HALF]
-                        nc.tensor.matmul_mx(
-                            out=sums[t, b][:],
-                            lhsT=edge_cols("%s_w%d" % (side, a), t).bitcast(FP8X4),
-                            lhsT_scale=lhs_sc,
-                            rhs=rhs,
-                            rhs_scale=rhs_sc,
-                            start=(i == 0),
-                            stop=(i == 3),
-                        )
+                b, t = g // 2, 2 * c + g % 2
+                for i in range(first, last):
+                    side, a = STEPS[b][i]
+                    if i == 0:
+                        sums[t, b] = next_bank()
+                    if side == "dst":
+                        lhs_sc = edge_cols("dst_sc", t, 4 * a)
+                        rhs, rhs_sc = wt_w[a, b][:].bitcast(FP8X4), wt_sc[a, b][:]
+                    else:
+                        lhs_sc = edge_cols("src_sc%d" % a, t)
+                        rhs = ws_w[a][:, 2 * HALF * b : 2 * HALF * (b + 1)].bitcast(FP4X4)
+                        rhs_sc = ws_sc[:, a, b * HALF : (b + 1) * HALF]
+                    nc.tensor.matmul_mx(
+                        out=sums[t, b][:],
+                        lhsT=edge_cols("%s_w%d" % (side, a), t).bitcast(FP8X4),
+                        lhsT_scale=lhs_sc,
+                        rhs=rhs,
+                        rhs_scale=rhs_sc,
+                        start=(i == 0),
+                        stop=(i == 3),
+                    )
 
         def rectify(c, b, rows):
             for t in range(2):
@@ -199,43 +205,48 @@ def tile_list_msg_relu_none_kernel(
                     RELU,
                 )
 
-        def turn_and_quantise(c, b, rows, offset=None):
+        def turn(rows, h_in):
             turned = next_bank()
-            h_in = held("h_in%d%d" % (c, b), [P, 2, P, 2], F32, offset)
             for t in range(2):
                 pairs = rows[t][:].bitcast(F32)
                 for u in range(2):
                     at = (2 * t + u) * P
                     nc.tensor.transpose(turned[:, at : at + P], pairs[:, u * P : (u + 1) * P], ident[:])
-            nc.scalar.copy(h_in[:], turned[:].rearrange("p (t u j) -> p t j u", j=P, u=2))
+            nc.scalar.copy(h_in, turned[:].rearrange("p (t u j) -> p t j u", j=P, u=2))
+            return turned
+
+        def turn_and_quantise(c, b, rows, offset=None):
+            h_in = held("h_in%d%d" % (c, b), [P, 2, P, 2], F32, offset)
+            turn(rows, h_in[:])
             nc.vector.quantize_mx(
                 out=h_w[c][:, b, :].bitcast(FP8X4),
                 scales=h_sc[c][:, b, :],
                 in_=h_in[:].rearrange("p t j u -> p (t j u)").bitcast(BF16),
             )
-            return turned
 
-        def send(c, n, y=None):
+        def send(c, n, y=None, chunks=1):
             if y is None:
                 y = next_bank()
-            for t in range(2):
+            width = chunks * CHUNK
+            for t in range(width // P):
                 for b in (1, 0):
+                    cols = slice(t % 2 * P, (t % 2 + 1) * P)
                     nc.tensor.matmul_mx(
                         out=y[:, t * P : (t + 1) * P],
                         lhsT=wd_w[:, b, 2 * P * n : 2 * P * (n + 1)].bitcast(FP4X4),
                         lhsT_scale=wd_sc[:, b, P * n : P * (n + 1)],
-                        rhs=h_w[c][:, b, t * P : (t + 1) * P].bitcast(FP8X4),
-                        rhs_scale=h_sc[c][:, b, t * P : (t + 1) * P],
+                        rhs=h_w[c + t // 2][:, b, cols].bitcast(FP8X4),
+                        rhs_scale=h_sc[c + t // 2][:, b, cols],
                         start=(b == 1),
                         stop=(b == 0),
                     )
-            msg = held("msg%d%d" % (c, n), [P, CHUNK], F32)
-            nc.scalar.copy(msg[:], y[:, 0:CHUNK])
+            msg = held("msg%d%d" % (c, n), [P, width], F32)
+            nc.scalar.copy(msg[:], y[:, 0:width])
             j0 = c * CHUNK
             nc.vector.tensor_tensor(
-                placed[n][:].indirect(dst_list[:, j0 // GROUP : (j0 + CHUNK) // GROUP]),
+                placed[n][:].indirect(dst_list[:, j0 // GROUP : (j0 + width) // GROUP]),
                 msg[:],
-                gain[:, j0 : j0 + CHUNK],
+                gain[:, j0 : j0 + width],
                 MULT,
             )
             return y
@@ -244,18 +255,24 @@ def tile_list_msg_relu_none_kernel(
         first_layer(1, 0, 2)
         first_layer(0, 2, 4)
         relu = [[held("relu%d%d" % (b, t), [P, HALF], BF16) for t in range(2)] for b in range(2)]
-        after = STAGE_BYTES
         rectify(0, 0, relu[0])
         rectify(0, 1, relu[1])
         turn_and_quantise(0, 0, relu[0])
-        turn_and_quantise(0, 1, relu[1], after + 4 * HALF - 64)
-        gather("dst_w1", tab_w[1], dst_list, U32, HALF, J, after)
-        relu[1] = [held("relu2%d" % t, [P, HALF], BF16, after + 4 * HALF + 2 * HALF * t) for t in range(2)]
+        gathered_end = TURNED_AT + WORD * 2 * CHUNK
+        turn_and_quantise(0, 1, relu[1], gathered_end - ALIGN)
+        gather("dst_w1", tab_w[1], dst_list, U32, 2 * CHUNK, J, TURNED_AT)
+        relu[1] = [held("relu2%d" % t, [P, HALF], BF16, gathered_end + 2 * HALF * t) for t in range(2)]
 
         def finish_hidden(c):
+            h_in = held("h_in%d" % c, [P, 2, 2, P, 2], F32)
             for b in range(2):
                 rectify(c, b, relu[(c + b) % 2])
-                turned = turn_and_quantise(c, b, relu[(c + b) % 2])
+                turned = turn(relu[(c + b) % 2], h_in[:, b])
+            nc.vector.quantize_mx(
+                out=h_w[c][:].rearrange("p b j -> p (b j)").bitcast(FP8X4),
+                scales=h_sc[c][:].rearrange("p b j -> p (b j)"),
+                in_=h_in[:].rearrange("p b t j u -> p (b t j u)").bitcast(BF16),
+            )
             return turned
 
         for c in range(CHUNKS - 2):
@@ -264,17 +281,17 @@ def tile_list_msg_relu_none_kernel(
                 first_layer(1, 2, 4)
             send(c, 1)
             if c > 0:
-                first_layer(c + 1, 0, 4, range(3, 4))
+                first_layer(c + 1, 0, 4, range(EARLY_GROUPS, 4))
             finish_hidden(c + 1)
             send(c, 2)
             send(c, 3)
-            first_layer(c + 2, 0, 4, range(3))
-        send(2, 0)
-        send(2, 1)
-        first_layer(3, 0, 4, range(3, 4))
-        send(2, 2, finish_hidden(3))
-        last = [send(3, n) for n in range(3)]
-        send(2, 3, last[1])
-        send(3, 3, last[2])
+            first_layer(c + 2, 0, 4, range(EARLY_GROUPS))
+        before_last, last = CHUNKS - 2, CHUNKS - 1
+        send(before_last, 0)
+        send(before_last, 1)
+        first_layer(last, 0, 4, range(EARLY_GROUPS, 4))
+        send(before_last, 2, finish_hidden(last))
+        last_banks = [send(last, n) for n in range(3)]
+        send(before_last, 3, last_banks[1], 2)
         for n, page in enumerate(placed):
             nc.sync.dma_start(out[n * P : (n + 1) * P, :], page[:])

@@ -228,15 +228,14 @@ def tile_list_msg_relu_none_kernel(
             if y is None:
                 y = next_bank()
             width = chunks * CHUNK
-            for t in range(width // P):
+            for t in range(chunks):
                 for b in (1, 0):
-                    cols = slice(t % 2 * P, (t % 2 + 1) * P)
                     nc.tensor.matmul_mx(
-                        out=y[:, t * P : (t + 1) * P],
+                        out=y[:, t * CHUNK : (t + 1) * CHUNK],
                         lhsT=wd_w[:, b, 2 * P * n : 2 * P * (n + 1)].bitcast(FP4X4),
                         lhsT_scale=wd_sc[:, b, P * n : P * (n + 1)],
-                        rhs=h_w[c + t // 2][:, b, cols].bitcast(FP8X4),
-                        rhs_scale=h_sc[c + t // 2][:, b, cols],
+                        rhs=h_w[c + t][:, b, :].bitcast(FP8X4),
+                        rhs_scale=h_sc[c + t][:, b, :],
                         start=(b == 1),
                         stop=(b == 0),
                     )

@@ -1,7 +1,6 @@
 from contextlib import ExitStack
 
 import concourse.mybir as mybir
-from concourse.masks import make_identity
 
 K, R, N, T, J = 1024, 1024, 512, 2048, 1024
 FLOPS = 2 * (2 * K * R * J + R * N * J)
@@ -26,13 +25,12 @@ CHUNKS = J // CHUNK
 BANKS = 8
 ALIGN = 64
 WORD = 4
-STEPS = ((("dst", 0), ("src", 0), ("dst", 1), ("src", 1)), (("dst", 0), ("src", 0), ("src", 1), ("dst", 1)))
-EARLY_GROUPS = 3
-STAGE_BYTES = 2 * 4 * HALF
-SECOND_AT = 0
-TURNED_AT = STAGE_BYTES
-LAST_AT = 3 * STAGE_BYTES
-FIRST_AT = 5 * STAGE_BYTES
+STEPS = ((("dst", 0), ("src", 0), ("dst", 1), ("src", 1)), (("src", 0), ("dst", 0), ("src", 1), ("dst", 1)))
+RAW_BYTES = 4 * 4 * HALF
+FIRST_AT = 0
+SECOND_AT = RAW_BYTES
+LAST_AT = 2 * RAW_BYTES
+THIRD_AT = 3 * RAW_BYTES
 
 
 def tile_list_msg_relu_none_kernel(
@@ -51,24 +49,21 @@ def tile_list_msg_relu_none_kernel(
             return shared.tile(shape, dtype, name=name, align_bytes=ALIGN, offset=offset)
 
         banks = [psum.tile([P, HALF], F32, name="bank%d" % i) for i in range(BANKS)]
-        uses = []
-
-        def next_bank():
-            uses.append(len(uses))
-            return banks[uses[-1] % BANKS]
 
         tab_sc = held("tab_sc", [P, T], U8)
         nc.gpsimd.memset(tab_sc[:].bitcast(I32), 0)
+        ws_sc_raw = held("ws_sc_raw", [P, 2, R], U8)
+        nc.gpsimd.memset(ws_sc_raw[:].rearrange("p a r -> p (a r)").bitcast(I32), 0)
 
         def load_tab(a):
             words = held("tab_w%d" % a, [P, T], U32)
             nc.sync.dma_start(words[:].bitcast(I32), tab_words[a].rearrange("p t i -> p (t i)").bitcast(I32))
             return words
 
-        def load_wt(a, c0, width, queue=nc.sync):
-            piece = held("wt_raw%d_%d" % (a, c0), [P, 4, width], F32)
+        def load_wt(a, c0, width, offset=None):
+            piece = held("wt_raw%d_%d" % (a, c0), [P, 4, width], F32, offset)
             rows = wt[a * HALF : (a + 1) * HALF, c0 : c0 + width]
-            queue.dma_start(piece[:], rows.rearrange("(p i) c -> p i c", i=4))
+            nc.sync.dma_start(piece[:], rows.rearrange("(p i) c -> p i c", i=4))
             return piece
 
         def load_rows(planes, rows):
@@ -77,165 +72,153 @@ def tile_list_msg_relu_none_kernel(
                     planes[r:P:32, :, :].bitcast(I32), rows[:, r:16:4, :].rearrange("a q n -> q a n").bitcast(I32)
                 )
 
-        def load_words(name, words):
-            codes = held(name, [P, words.shape[1]], U8)
-            nc.sync.dma_start(codes[:].bitcast(I32), words.bitcast(I32))
-            return codes
-
         src_list = lists.tile([P, J // GROUP], U16, name="src_list")
         dst_list = lists.tile([P, J // GROUP], U16, name="dst_list")
-        nc.sync.dma_start(src_list[:], offs)
         nc.sync.dma_start(dst_list[:], offs2)
+        nc.sync.dma_start(src_list[:], offs)
         for q in range(4):
             nc.sync.dma_start(
                 tab_sc[32 * q : 32 * q + 8, :].bitcast(I32), tab_scales[:, 4 * q : 4 * q + 4, :].bitcast(I32)
             )
         picked = {}
 
-        def gather(name, window, edge_list, dtype, j0, j1, offset=None):
-            got = held("%s_%d" % (name, j0), [P, j1 - j0], dtype, offset)
-            nc.vector.tensor_copy(got[:], window[:].indirect(edge_list[:, j0 // GROUP : j1 // GROUP]))
+        def gather(name, window, edge_list, dtype, j0, j1, got=None, at=0):
+            if got is None:
+                got = held("%s_%d" % (name, j0), [P, j1 - j0], dtype)
+            nc.vector.tensor_copy(
+                got[:, at : at + j1 - j0], window[:].indirect(edge_list[:, j0 // GROUP : j1 // GROUP])
+            )
             for t in range(j0 // P, j1 // P):
-                picked[name, t] = (got, t * P - j0)
+                picked[name, t] = (got, at + t * P - j0)
             return got
 
         wt_w, wt_sc = {}, {}
 
-        def quantise_wt(a, b, offset=None):
-            grouped = held("grouped%d%d" % (a, b), [P, HALF, 4], BF16, offset)
+        def quantise_wt(a, b, parts=1, offset=None):
+            grouped = held("grouped%d%d" % (a, b), [P, 4, P, 4], BF16, offset)
             wt_w[a, b] = held("wt_w%d%d" % (a, b), [P, HALF], U32)
             wt_sc[a, b] = held("wt_sc%d%d" % (a, b), [P, HALF], U8)
-            width = HALF // len(raw[a, b])
-            for i, piece in enumerate(raw[a, b]):
-                cols = slice(i * width, (i + 1) * width)
-                dst = grouped[:, cols, :].rearrange("p (c u) i -> p c i u", u=4)
-                src = piece[:].rearrange("p i (c u) -> p c i u", u=4)
-                if i == 0:
-                    nc.scalar.activation(dst, src, COPY)
-                else:
-                    nc.vector.tensor_copy(dst, src)
+            width = P // len(raw[a, b])
+            for u, piece in enumerate(raw[a, b]):
+                nc.scalar.activation(
+                    grouped[:, :, u * width : (u + 1) * width, :].rearrange("p t m i -> p m i t"),
+                    piece[:].rearrange("p i (m t) -> p m i t", t=4),
+                    COPY,
+                )
+            flat = grouped[:].rearrange("p t m i -> p (t m i)")
+            width = HALF // parts
+            for u in range(parts):
+                cols = slice(u * width, (u + 1) * width)
                 nc.vector.quantize_mx(
                     out=wt_w[a, b][:, cols].bitcast(FP8X4),
                     scales=wt_sc[a, b][:, cols],
-                    in_=grouped[:, cols, :].rearrange("p c i -> p (c i)"),
+                    in_=flat[:, 4 * u * width : 4 * (u + 1) * width],
                 )
 
-        raw = {(0, 0): [load_wt(0, 0, HALF, nc.scalar)]}
+        raw = {(0, 0): [load_wt(0, 0, HALF, FIRST_AT)]}
         tab_w = [load_tab(0)]
+        ws_raw = held("ws_raw", [P, 2, R], U16)
+        nc.sync.dma_start(ws_raw[:].bitcast(I32), ws_words.rearrange("a p x -> p a x").bitcast(I32))
+        load_rows(ws_sc_raw, ws_scales)
+        raw[1, 0] = [load_wt(1, 0, HALF, SECOND_AT)]
         raw[0, 1] = [load_wt(0, HALF, HALF)]
-        raw[1, 0] = [load_wt(1, 0, HALF)]
-        quantise_wt(0, 0, FIRST_AT)
-        ws_sc = held("ws_sc", [P, 2, R], U8)
-        load_rows(ws_sc, ws_scales)
-        ws_w = [load_words("ws_w0", ws_words[0])]
-        raw[1, 1] = [load_wt(1, HALF, HALF // 2)]
-        src_sc = gather("src_sc0", tab_sc, src_list, U8, 0, J)
+        tab_w.append(load_tab(1))
+
         gather("dst_sc", tab_sc, dst_list, U8, 0, J)
+        src_sc = gather("src_sc0", tab_sc, src_list, U8, 0, J)
         moved_sc = held("moved_sc", [P, J], U8)
-        wd_sc = held("wd_sc", [P, 2, N], U8)
         for r in range(4):
             nc.sync.dma_start(moved_sc[r:P:32, :].bitcast(I32), src_sc[4 + r : P : 32, :].bitcast(I32))
         for t in range(J // P):
             picked["src_sc1", t] = (moved_sc, t * P)
-        tab_w.append(load_tab(1))
-        raw[1, 1].append(load_wt(1, HALF + HALF // 2, HALF // 2))
-        ws_w.append(load_words("ws_w1", ws_words[1]))
+        raw[1, 1] = [load_wt(1, HALF, HALF // 2), load_wt(1, HALF + HALF // 2, HALF // 2, THIRD_AT)]
+        wd_sc = held("wd_sc", [P, 2, N], U8)
         load_rows(wd_sc, wd_scales)
         wd_w = held("wd_w", [P, 2, 2 * N], U8)
         nc.sync.dma_start(wd_w[:].bitcast(I32), wd_words.rearrange("a p x -> p a x").bitcast(I32))
         gain = held("gain", [P, J], F32)
         nc.sync.dma_start(gain[:], wgo)
 
-        gather("dst_w0", tab_w[0], dst_list, U32, 0, 2 * CHUNK)
-        gather("src_w0", tab_w[0], src_list, U32, 0, 2 * CHUNK, FIRST_AT)
-        quantise_wt(0, 1, SECOND_AT)
-        gather("dst_w0", tab_w[0], dst_list, U32, 2 * CHUNK, J, SECOND_AT)
+        quantise_wt(0, 0)
+        ws_w = held("ws_w", [P, 4, 4, P], U16)
+        nc.scalar.copy(ws_w[:], ws_raw[:].rearrange("p a (b m t) -> p (a b) t m", b=2, t=4))
+        on_first = held("on_first", [P, 6 * CHUNK], U32, FIRST_AT)
+        gather("dst_w0", tab_w[0], dst_list, U32, 0, 2 * CHUNK, on_first)
+        ws_sc = held("ws_sc", [P, 4, 4, P], U8)
+        nc.vector.tensor_copy(ws_sc[:], ws_sc_raw[:].rearrange("p a (b m t) -> p (a b) t m", b=2, t=4))
+        gather("src_w0", tab_w[0], src_list, U32, 0, 2 * CHUNK, on_first, 2 * CHUNK)
+        gather("dst_w0", tab_w[0], dst_list, U32, 2 * CHUNK, J, on_first, 4 * CHUNK)
         quantise_wt(1, 0)
-        quantise_wt(1, 1, LAST_AT)
+        gather("src_w0", tab_w[0], src_list, U32, 2 * CHUNK, J, held("on_second", [P, 2 * CHUNK], U32, SECOND_AT))
         gather("dst_w1", tab_w[1], dst_list, U32, 0, CHUNK)
         gather("src_w1", tab_w[1], src_list, U32, 0, CHUNK)
-        gather("dst_w1", tab_w[1], dst_list, U32, CHUNK, 2 * CHUNK, LAST_AT + ALIGN)
-        gather("src_w1", tab_w[1], src_list, U32, CHUNK, 2 * CHUNK, LAST_AT + ALIGN + WORD * CHUNK)
-        gather("src_w1", tab_w[1], src_list, U32, 2 * CHUNK, J, LAST_AT + ALIGN + WORD * 2 * CHUNK)
-        gather("src_w0", tab_w[0], src_list, U32, 2 * CHUNK, J, LAST_AT + ALIGN - WORD * 2 * CHUNK)
+        quantise_wt(0, 1)
+        gather("dst_w1", tab_w[1], dst_list, U32, 2 * CHUNK, J)
+        quantise_wt(1, 1, 4, LAST_AT)
+        on_last = held("on_last", [P, 2 * CHUNK], U32, LAST_AT)
+        gather("dst_w1", tab_w[1], dst_list, U32, CHUNK, 2 * CHUNK, on_last)
+        gather("src_w1", tab_w[1], src_list, U32, CHUNK, 2 * CHUNK, on_last, CHUNK)
 
-        ident = held("ident", [P, P], F32)
-        make_identity(nc, ident[:])
         placed = [held("placed%d" % n, [P, T], F32) for n in range(N // P)]
         for page in placed:
             nc.gpsimd.memset(page[:], 0.0)
 
+        h_in = [held("h_in%d" % c, [P, 2, 2, P, 4], BF16, None if c else THIRD_AT) for c in range(CHUNKS)]
         h_w = [held("h_w%d" % c, [P, 2, CHUNK], U32) for c in range(CHUNKS)]
         h_sc = [held("h_sc%d" % c, [P, 2, CHUNK], U8) for c in range(CHUNKS)]
-        sums = {}
+        sum_banks = ((0, 1, 2, 3), (4, 5, 6, 7), (2, 3, 0, 1), (6, 7, 4, 5))
 
-        def edge_cols(name, t, row=0):
-            got, at = picked[name, t]
+        def edge_cols(name, tile, row=0):
+            got, at = picked[name, tile]
             return got[row:P, at : at + P]
 
-        def first_layer(c, first, last, groups=range(4)):
-            for g in groups:
-                b, t = g // 2, 2 * c + g % 2
-                for i in range(first, last):
-                    side, a = STEPS[b][i]
-                    if i == 0:
-                        sums[t, b] = next_bank()
-                    if side == "dst":
-                        lhs_sc = edge_cols("dst_sc", t, 4 * a)
-                        rhs, rhs_sc = wt_w[a, b][:].bitcast(FP8X4), wt_sc[a, b][:]
-                    else:
-                        lhs_sc = edge_cols("src_sc%d" % a, t)
-                        rhs = ws_w[a][:, 2 * HALF * b : 2 * HALF * (b + 1)].bitcast(FP4X4)
-                        rhs_sc = ws_sc[:, a, b * HALF : (b + 1) * HALF]
-                    nc.tensor.matmul_mx(
-                        out=sums[t, b][:],
-                        lhsT=edge_cols("%s_w%d" % (side, a), t).bitcast(FP8X4),
-                        lhsT_scale=lhs_sc,
-                        rhs=rhs,
-                        rhs_scale=rhs_sc,
-                        start=(i == 0),
-                        stop=(i == 3),
-                    )
+        def first_layer(c, groups, steps):
+            for i in steps:
+                for t in range(4):
+                    for g in groups:
+                        b, tile = g // 2, 2 * c + g % 2
+                        side, a = STEPS[b][i]
+                        cols = slice(t * P, (t + 1) * P)
+                        if side == "dst":
+                            lhs, lhs_sc = wt_w[a, b][:, cols].bitcast(FP8X4), wt_sc[a, b][:, cols]
+                            rhs_sc = edge_cols("dst_sc", tile, 4 * a)
+                        else:
+                            lhs, lhs_sc = ws_w[:, 2 * a + b, t, :].bitcast(FP4X4), ws_sc[:, 2 * a + b, t, :]
+                            rhs_sc = edge_cols("src_sc%d" % a, tile)
+                        nc.tensor.matmul_mx(
+                            out=banks[sum_banks[c][g]][:, cols],
+                            lhsT=lhs,
+                            lhsT_scale=lhs_sc,
+                            rhs=edge_cols("%s_w%d" % (side, a), tile).bitcast(FP8X4),
+                            rhs_scale=rhs_sc,
+                            start=(i == 0 and t == 0),
+                            stop=(i == 3 and t == 3),
+                        )
 
-        def rectify(c, b, rows):
-            for t in range(2):
+        def rectify(c, groups):
+            for g in groups:
                 nc.scalar.activation(
-                    rows[t][:].rearrange("p (u m e) -> p u m e", u=2, e=2),
-                    sums[2 * c + t, b][:].rearrange("p (m u e) -> p u m e", u=2, e=2),
-                    RELU,
+                    h_in[c][:, g // 2, g % 2], banks[sum_banks[c][g]][:].rearrange("p (t j) -> p j t", t=4), RELU
                 )
 
-        def turn(rows, h_in):
-            turned = next_bank()
-            for t in range(2):
-                pairs = rows[t][:].bitcast(F32)
-                for u in range(2):
-                    at = (2 * t + u) * P
-                    nc.tensor.transpose(turned[:, at : at + P], pairs[:, u * P : (u + 1) * P], ident[:])
-            nc.scalar.copy(h_in, turned[:].rearrange("p (t u j) -> p t j u", j=P, u=2))
-            return turned
-
-        def turn_and_quantise(c, b, rows, offset=None):
-            h_in = held("h_in%d%d" % (c, b), [P, 2, P, 2], F32, offset)
-            turn(rows, h_in[:])
+        def quantise_h(c, b0, b1):
             nc.vector.quantize_mx(
-                out=h_w[c][:, b, :].bitcast(FP8X4),
-                scales=h_sc[c][:, b, :],
-                in_=h_in[:].rearrange("p t j u -> p (t j u)").bitcast(BF16),
+                out=h_w[c][:, b0:b1, :].rearrange("p b j -> p (b j)").bitcast(FP8X4),
+                scales=h_sc[c][:, b0:b1, :].rearrange("p b j -> p (b j)"),
+                in_=h_in[c][:, b0:b1].rearrange("p b e j t -> p (b e j t)"),
             )
 
-        def send(c, n, y=None, chunks=1):
-            if y is None:
-                y = next_bank()
+        def send(c, n, bank, chunks=1):
+            y = banks[bank]
             width = chunks * CHUNK
-            for t in range(chunks):
+            for u in range(chunks):
                 for b in (1, 0):
                     nc.tensor.matmul_mx(
-                        out=y[:, t * CHUNK : (t + 1) * CHUNK],
+                        out=y[:, u * CHUNK : (u + 1) * CHUNK],
                         lhsT=wd_w[:, b, 2 * P * n : 2 * P * (n + 1)].bitcast(FP4X4),
                         lhsT_scale=wd_sc[:, b, P * n : P * (n + 1)],
-                        rhs=h_w[c + t][:, b, :].bitcast(FP8X4),
-                        rhs_scale=h_sc[c + t][:, b, :],
+                        rhs=h_w[c + u][:, b, :].bitcast(FP8X4),
+                        rhs_scale=h_sc[c + u][:, b, :],
                         start=(b == 1),
                         stop=(b == 0),
                     )
@@ -248,49 +231,38 @@ def tile_list_msg_relu_none_kernel(
                 gain[:, j0 : j0 + width],
                 MULT,
             )
-            return y
 
-        first_layer(0, 0, 2)
-        first_layer(1, 0, 2)
-        first_layer(0, 2, 4)
-        relu = [[held("relu%d%d" % (b, t), [P, HALF], BF16) for t in range(2)] for b in range(2)]
-        rectify(0, 0, relu[0])
-        rectify(0, 1, relu[1])
-        turn_and_quantise(0, 0, relu[0])
-        gathered_end = TURNED_AT + WORD * 2 * CHUNK
-        turn_and_quantise(0, 1, relu[1], gathered_end - ALIGN)
-        gather("dst_w1", tab_w[1], dst_list, U32, 2 * CHUNK, J, TURNED_AT)
-        relu[1] = [held("relu2%d" % t, [P, HALF], BF16, gathered_end + 2 * HALF * t) for t in range(2)]
-
-        def finish_hidden(c):
-            h_in = held("h_in%d" % c, [P, 2, 2, P, 2], F32)
-            for b in range(2):
-                rectify(c, b, relu[(c + b) % 2])
-                turned = turn(relu[(c + b) % 2], h_in[:, b])
-            nc.vector.quantize_mx(
-                out=h_w[c][:].rearrange("p b j -> p (b j)").bitcast(FP8X4),
-                scales=h_sc[c][:].rearrange("p b j -> p (b j)"),
-                in_=h_in[:].rearrange("p b t j u -> p (b t j u)").bitcast(BF16),
-            )
-            return turned
-
-        for c in range(CHUNKS - 2):
-            send(c, 0)
-            if c == 0:
-                first_layer(1, 2, 4)
-            send(c, 1)
-            if c > 0:
-                first_layer(c + 1, 0, 4, range(EARLY_GROUPS, 4))
-            finish_hidden(c + 1)
-            send(c, 2)
-            send(c, 3)
-            first_layer(c + 2, 0, 4, range(EARLY_GROUPS))
-        before_last, last = CHUNKS - 2, CHUNKS - 1
-        send(before_last, 0)
-        send(before_last, 1)
-        first_layer(last, 0, 4, range(EARLY_GROUPS, 4))
-        send(before_last, 2, finish_hidden(last))
-        last_banks = [send(last, n) for n in range(3)]
-        send(before_last, 3, last_banks[1], 2)
+        for i in range(2):
+            for c in range(2):
+                first_layer(c, (0, 1), (i,))
+        for i in range(2):
+            for c in range(2):
+                first_layer(c, (2, 3), (i,))
+        first_layer(0, (0, 1), (2, 3))
+        rectify(0, (0, 1))
+        quantise_h(0, 0, 1)
+        first_layer(0, (2, 3), (2, 3))
+        rectify(0, (2, 3))
+        quantise_h(0, 1, 2)
+        gather("src_w1", tab_w[1], src_list, U32, 2 * CHUNK, J, held("on_third", [P, 2 * CHUNK], U32, THIRD_AT))
+        send(0, 0, 0)
+        first_layer(1, (0, 1), (2, 3))
+        send(0, 1, 1)
+        first_layer(1, (2, 3), (2, 3))
+        for c in range(1, CHUNKS):
+            rectify(c, range(4))
+            quantise_h(c, 0, 2)
+            send(c - 1, 2, sum_banks[c][3])
+            if c + 1 < CHUNKS:
+                send(c - 1, 3, sum_banks[c][2])
+                for g in range(2):
+                    first_layer(c + 1, (g,), range(4))
+            for n in range(2):
+                send(c, n, sum_banks[c][n])
+            if c + 1 < CHUNKS:
+                for g in range(2, 4):
+                    first_layer(c + 1, (g,), range(4))
+        send(3, 2, sum_banks[3][2])
+        send(2, 3, sum_banks[3][1], 2)
         for n, page in enumerate(placed):
             nc.sync.dma_start(out[n * P : (n + 1) * P, :], page[:])

@@ -25,7 +25,8 @@ CHUNKS = J // CHUNK
 BANKS = 8
 ALIGN = 64
 WORD = 4
-STEPS = ((("dst", 0), ("src", 0), ("dst", 1), ("src", 1)), (("src", 0), ("dst", 0), ("src", 1), ("dst", 1)))
+LATER_HIGH = (("src", 0), ("dst", 0), ("src", 1), ("dst", 1))
+STEPS = ((("dst", 0), ("src", 0), ("dst", 1), ("src", 1)), (("src", 0), ("src", 1), ("dst", 0), ("dst", 1)))
 RAW_BYTES = 4 * 4 * HALF
 FIRST_AT = 0
 SECOND_AT = RAW_BYTES
@@ -100,11 +101,12 @@ def tile_list_msg_relu_none_kernel(
             wt_sc[a, b] = held("wt_sc%d%d" % (a, b), [P, HALF], U8)
             width = P // len(raw[a, b])
             for u, piece in enumerate(raw[a, b]):
-                nc.scalar.activation(
-                    grouped[:, :, u * width : (u + 1) * width, :].rearrange("p t m i -> p m i t"),
-                    piece[:].rearrange("p i (m t) -> p m i t", t=4),
-                    COPY,
-                )
+                dst = grouped[:, :, u * width : (u + 1) * width, :].rearrange("p t m i -> p m i t")
+                src = piece[:].rearrange("p i (m t) -> p m i t", t=4)
+                if piece is not raw[1, 1][1]:
+                    nc.scalar.activation(dst, src, COPY)
+                else:
+                    nc.vector.tensor_copy(dst, src)
             flat = grouped[:].rearrange("p t m i -> p (t m i)")
             width = HALF // parts
             for u in range(parts):
@@ -121,7 +123,6 @@ def tile_list_msg_relu_none_kernel(
         nc.sync.dma_start(ws_raw[:].bitcast(I32), ws_words.rearrange("a p x -> p a x").bitcast(I32))
         load_rows(ws_sc_raw, ws_scales)
         raw[1, 0] = [load_wt(1, 0, HALF, SECOND_AT)]
-        raw[0, 1] = [load_wt(0, HALF, HALF)]
         tab_w.append(load_tab(1))
 
         gather("dst_sc", tab_sc, dst_list, U8, 0, J)
@@ -131,7 +132,8 @@ def tile_list_msg_relu_none_kernel(
             nc.sync.dma_start(moved_sc[r:P:32, :].bitcast(I32), src_sc[4 + r : P : 32, :].bitcast(I32))
         for t in range(J // P):
             picked["src_sc1", t] = (moved_sc, t * P)
-        raw[1, 1] = [load_wt(1, HALF, HALF // 2), load_wt(1, HALF + HALF // 2, HALF // 2, THIRD_AT)]
+        raw[0, 1] = [load_wt(0, HALF, HALF // 2), load_wt(0, HALF + HALF // 2, HALF // 2)]
+        raw[1, 1] = [load_wt(1, HALF, HALF // 2, THIRD_AT), load_wt(1, HALF + HALF // 2, HALF // 2)]
         wd_sc = held("wd_sc", [P, 2, N], U8)
         load_rows(wd_sc, wd_scales)
         wd_w = held("wd_w", [P, 2, 2 * N], U8)
@@ -152,12 +154,12 @@ def tile_list_msg_relu_none_kernel(
         gather("src_w0", tab_w[0], src_list, U32, 2 * CHUNK, J, held("on_second", [P, 2 * CHUNK], U32, SECOND_AT))
         gather("dst_w1", tab_w[1], dst_list, U32, 0, CHUNK)
         gather("src_w1", tab_w[1], src_list, U32, 0, CHUNK)
-        quantise_wt(0, 1)
         gather("dst_w1", tab_w[1], dst_list, U32, 2 * CHUNK, J)
+        quantise_wt(0, 1)
         quantise_wt(1, 1, 4, LAST_AT)
         on_last = held("on_last", [P, 2 * CHUNK], U32, LAST_AT)
         gather("dst_w1", tab_w[1], dst_list, U32, CHUNK, 2 * CHUNK, on_last)
-        gather("src_w1", tab_w[1], src_list, U32, CHUNK, 2 * CHUNK, on_last, CHUNK)
+        gather("src_w1", tab_w[1], src_list, U32, 2 * CHUNK, 3 * CHUNK, on_last, CHUNK)
 
         placed = [held("placed%d" % n, [P, T], F32) for n in range(N // P)]
         for page in placed:
@@ -177,7 +179,7 @@ def tile_list_msg_relu_none_kernel(
                 for t in range(4):
                     for g in groups:
                         b, tile = g // 2, 2 * c + g % 2
-                        side, a = STEPS[b][i]
+                        side, a = (LATER_HIGH if b and c else STEPS[b])[i]
                         cols = slice(t * P, (t + 1) * P)
                         if side == "dst":
                             lhs, lhs_sc = wt_w[a, b][:, cols].bitcast(FP8X4), wt_sc[a, b][:, cols]
@@ -235,16 +237,19 @@ def tile_list_msg_relu_none_kernel(
         for i in range(2):
             for c in range(2):
                 first_layer(c, (0, 1), (i,))
-        for i in range(2):
-            for c in range(2):
-                first_layer(c, (2, 3), (i,))
+        for c in range(2):
+            first_layer(c, (2, 3), (0,))
         first_layer(0, (0, 1), (2, 3))
         rectify(0, (0, 1))
         quantise_h(0, 0, 1)
-        first_layer(0, (2, 3), (2, 3))
+        first_layer(0, (2, 3), (1, 2))
+        first_layer(1, (2, 3), (1,))
+        first_layer(0, (2, 3), (3,))
         rectify(0, (2, 3))
         quantise_h(0, 1, 2)
-        gather("src_w1", tab_w[1], src_list, U32, 2 * CHUNK, J, held("on_third", [P, 2 * CHUNK], U32, THIRD_AT))
+        on_third = held("on_third", [P, 2 * CHUNK], U32, THIRD_AT)
+        gather("src_w1", tab_w[1], src_list, U32, CHUNK, 2 * CHUNK, on_third)
+        gather("src_w1", tab_w[1], src_list, U32, 3 * CHUNK, J, on_third, CHUNK)
         send(0, 0, 0)
         first_layer(1, (0, 1), (2, 3))
         send(0, 1, 1)

@@ -25,13 +25,14 @@ CHUNKS = J // CHUNK
 BANKS = 8
 ALIGN = 64
 WORD = 4
-LATER_HIGH = (("src", 0), ("dst", 0), ("src", 1), ("dst", 1))
-STEPS = ((("dst", 0), ("src", 0), ("dst", 1), ("src", 1)), (("src", 0), ("src", 1), ("dst", 0), ("dst", 1)))
+STEPS = ((("dst", 0), ("src", 0), ("dst", 1), ("src", 1)), (("src", 0), ("dst", 0), ("src", 1), ("dst", 1)))
 RAW_BYTES = 4 * 4 * HALF
 FIRST_AT = 0
 SECOND_AT = RAW_BYTES
 LAST_AT = 2 * RAW_BYTES
 THIRD_AT = 3 * RAW_BYTES
+FOURTH_AT = 4 * RAW_BYTES
+FIFTH_AT = 5 * RAW_BYTES
 
 
 def tile_list_msg_relu_none_kernel(
@@ -53,8 +54,12 @@ def tile_list_msg_relu_none_kernel(
 
         tab_sc = held("tab_sc", [P, T], U8)
         nc.gpsimd.memset(tab_sc[:].bitcast(I32), 0)
-        ws_sc_raw = held("ws_sc_raw", [P, 2, R], U8)
-        nc.gpsimd.memset(ws_sc_raw[:].rearrange("p a r -> p (a r)").bitcast(I32), 0)
+        ws_sc_raw = held("ws_sc_raw", [P, 2, R], U8, FOURTH_AT)
+        nc.vector.memset(ws_sc_raw[:].rearrange("p a r -> p (a r)").bitcast(I32), 0)
+
+        placed = [held("placed%d" % n, [P, T], F32) for n in range(N // P - 1)]
+        for page in placed:
+            nc.vector.memset(page[:].bitcast(I32), 0)
 
         def load_tab(a):
             words = held("tab_w%d" % a, [P, T], U32)
@@ -103,10 +108,7 @@ def tile_list_msg_relu_none_kernel(
             for u, piece in enumerate(raw[a, b]):
                 dst = grouped[:, :, u * width : (u + 1) * width, :].rearrange("p t m i -> p m i t")
                 src = piece[:].rearrange("p i (m t) -> p m i t", t=4)
-                if piece is not raw[1, 1][1]:
-                    nc.scalar.activation(dst, src, COPY)
-                else:
-                    nc.vector.tensor_copy(dst, src)
+                nc.scalar.activation(dst, src, COPY)
             flat = grouped[:].rearrange("p t m i -> p (t m i)")
             width = HALF // parts
             for u in range(parts):
@@ -118,11 +120,12 @@ def tile_list_msg_relu_none_kernel(
                 )
 
         raw = {(0, 0): [load_wt(0, 0, HALF, FIRST_AT)]}
+        load_rows(ws_sc_raw, ws_scales)
         tab_w = [load_tab(0)]
         ws_raw = held("ws_raw", [P, 2, R], U16)
         nc.sync.dma_start(ws_raw[:].bitcast(I32), ws_words.rearrange("a p x -> p a x").bitcast(I32))
-        load_rows(ws_sc_raw, ws_scales)
-        raw[1, 0] = [load_wt(1, 0, HALF, SECOND_AT)]
+        raw[0, 1] = [load_wt(0, HALF, HALF, SECOND_AT)]
+        raw[1, 0] = [load_wt(1, 0, HALF, FIFTH_AT)]
         tab_w.append(load_tab(1))
 
         gather("dst_sc", tab_sc, dst_list, U8, 0, J)
@@ -132,8 +135,7 @@ def tile_list_msg_relu_none_kernel(
             nc.sync.dma_start(moved_sc[r:P:32, :].bitcast(I32), src_sc[4 + r : P : 32, :].bitcast(I32))
         for t in range(J // P):
             picked["src_sc1", t] = (moved_sc, t * P)
-        raw[0, 1] = [load_wt(0, HALF, HALF // 2), load_wt(0, HALF + HALF // 2, HALF // 2)]
-        raw[1, 1] = [load_wt(1, HALF, HALF // 2, THIRD_AT), load_wt(1, HALF + HALF // 2, HALF // 2)]
+        raw[1, 1] = [load_wt(1, HALF, HALF // 2), load_wt(1, HALF + HALF // 2, HALF // 2, THIRD_AT)]
         wd_sc = held("wd_sc", [P, 2, N], U8)
         load_rows(wd_sc, wd_scales)
         wd_w = held("wd_w", [P, 2, 2 * N], U8)
@@ -141,29 +143,26 @@ def tile_list_msg_relu_none_kernel(
         gain = held("gain", [P, J], F32)
         nc.sync.dma_start(gain[:], wgo)
 
+        gather("dst_w0", tab_w[0], dst_list, U32, 0, 2 * CHUNK)
+        gather("src_w0", tab_w[0], src_list, U32, 0, 2 * CHUNK)
         quantise_wt(0, 0)
         ws_w = held("ws_w", [P, 4, 4, P], U16)
         nc.scalar.copy(ws_w[:], ws_raw[:].rearrange("p a (b m t) -> p (a b) t m", b=2, t=4))
-        on_first = held("on_first", [P, 6 * CHUNK], U32, FIRST_AT)
-        gather("dst_w0", tab_w[0], dst_list, U32, 0, 2 * CHUNK, on_first)
         ws_sc = held("ws_sc", [P, 4, 4, P], U8)
-        nc.vector.tensor_copy(ws_sc[:], ws_sc_raw[:].rearrange("p a (b m t) -> p (a b) t m", b=2, t=4))
-        gather("src_w0", tab_w[0], src_list, U32, 0, 2 * CHUNK, on_first, 2 * CHUNK)
-        gather("dst_w0", tab_w[0], dst_list, U32, 2 * CHUNK, J, on_first, 4 * CHUNK)
-        quantise_wt(1, 0)
-        gather("src_w0", tab_w[0], src_list, U32, 2 * CHUNK, J, held("on_second", [P, 2 * CHUNK], U32, SECOND_AT))
-        gather("dst_w1", tab_w[1], dst_list, U32, 0, CHUNK)
-        gather("src_w1", tab_w[1], src_list, U32, 0, CHUNK)
-        gather("dst_w1", tab_w[1], dst_list, U32, 2 * CHUNK, J)
+        nc.gpsimd.tensor_copy(ws_sc[:], ws_sc_raw[:].rearrange("p a (b m t) -> p (a b) t m", b=2, t=4))
+        gather("dst_w0", tab_w[0], dst_list, U32, 2 * CHUNK, J, held("on_first", [P, 2 * CHUNK], U32, FIRST_AT))
         quantise_wt(0, 1)
+        gather("src_w0", tab_w[0], src_list, U32, 2 * CHUNK, J, held("on_second", [P, 2 * CHUNK], U32, SECOND_AT))
+        quantise_wt(1, 0)
+        on_fifth = held("on_fifth", [P, 5 * CHUNK], U32, FIFTH_AT)
+        gather("dst_w1", tab_w[1], dst_list, U32, 0, CHUNK, on_fifth)
+        gather("src_w1", tab_w[1], src_list, U32, 0, CHUNK, on_fifth, CHUNK)
+        gather("dst_w1", tab_w[1], dst_list, U32, 2 * CHUNK, J, on_fifth, 2 * CHUNK)
+        gather("src_w1", tab_w[1], src_list, U32, 2 * CHUNK, 3 * CHUNK, on_fifth, 4 * CHUNK)
         quantise_wt(1, 1, 4, LAST_AT)
-        on_last = held("on_last", [P, 2 * CHUNK], U32, LAST_AT)
+        on_last = held("on_last", [P, CHUNK], U32, LAST_AT)
         gather("dst_w1", tab_w[1], dst_list, U32, CHUNK, 2 * CHUNK, on_last)
-        gather("src_w1", tab_w[1], src_list, U32, 2 * CHUNK, 3 * CHUNK, on_last, CHUNK)
 
-        placed = [held("placed%d" % n, [P, T], F32) for n in range(N // P)]
-        for page in placed:
-            nc.gpsimd.memset(page[:], 0.0)
 
         h_in = [held("h_in%d" % c, [P, 2, 2, P, 4], BF16, None if c else THIRD_AT) for c in range(CHUNKS)]
         h_w = [held("h_w%d" % c, [P, 2, CHUNK], U32) for c in range(CHUNKS)]
@@ -179,7 +178,7 @@ def tile_list_msg_relu_none_kernel(
                 for t in range(4):
                     for g in groups:
                         b, tile = g // 2, 2 * c + g % 2
-                        side, a = (LATER_HIGH if b and c else STEPS[b])[i]
+                        side, a = STEPS[b][i]
                         cols = slice(t * P, (t + 1) * P)
                         if side == "dst":
                             lhs, lhs_sc = wt_w[a, b][:, cols].bitcast(FP8X4), wt_sc[a, b][:, cols]
@@ -234,19 +233,18 @@ def tile_list_msg_relu_none_kernel(
                 MULT,
             )
 
-        for i in range(2):
-            for c in range(2):
-                first_layer(c, (0, 1), (i,))
-        for c in range(2):
-            first_layer(c, (2, 3), (0,))
+        for b in range(2):
+            for i in range(2):
+                for c in range(2):
+                    first_layer(c, (2 * b, 2 * b + 1), (i,))
         first_layer(0, (0, 1), (2, 3))
         rectify(0, (0, 1))
         quantise_h(0, 0, 1)
-        first_layer(0, (2, 3), (1, 2))
-        first_layer(1, (2, 3), (1,))
-        first_layer(0, (2, 3), (3,))
+        first_layer(0, (2, 3), (2, 3))
         rectify(0, (2, 3))
         quantise_h(0, 1, 2)
+        placed.append(held("placed3", [P, T], F32, THIRD_AT + WORD * 2 * CHUNK))
+        nc.gpsimd.memset(placed[3][:], 0.0)
         on_third = held("on_third", [P, 2 * CHUNK], U32, THIRD_AT)
         gather("src_w1", tab_w[1], src_list, U32, CHUNK, 2 * CHUNK, on_third)
         gather("src_w1", tab_w[1], src_list, U32, 3 * CHUNK, J, on_third, CHUNK)

@@ -54,12 +54,12 @@ def tile_list_msg_relu_none_kernel(
 
         tab_sc = held("tab_sc", [P, T], U8)
         nc.gpsimd.memset(tab_sc[:].bitcast(I32), 0)
-        ws_sc_raw = held("ws_sc_raw", [P, 2, R], U8, FOURTH_AT)
-        nc.vector.memset(ws_sc_raw[:].rearrange("p a r -> p (a r)").bitcast(I32), 0)
+        ws_sc_raw = held("ws_sc_raw", [P, R], U8)
+        nc.gpsimd.memset(ws_sc_raw[:].bitcast(I32), 0)
 
-        placed = [held("placed%d" % n, [P, T], F32) for n in range(N // P - 1)]
+        placed = [held("placed%d" % n, [P, T], F32) for n in range(N // P)]
         for page in placed:
-            nc.vector.memset(page[:].bitcast(I32), 0)
+            nc.gpsimd.memset(page[:], 0.0)
 
         def load_tab(a):
             words = held("tab_w%d" % a, [P, T], U32)
@@ -78,14 +78,21 @@ def tile_list_msg_relu_none_kernel(
                     planes[r:P:32, :, :].bitcast(I32), rows[:, r:16:4, :].rearrange("a q n -> q a n").bitcast(I32)
                 )
 
+        def load_both(planes, rows):
+            for r in range(4):
+                nc.sync.dma_start(
+                    planes[r:P:16, :].bitcast(I32), rows[:, r:16:4, :].rearrange("a q n -> q a n").bitcast(I32)
+                )
+
+        def move_up(dst, src):
+            for r in range(4):
+                nc.sync.dma_start(dst[r:P:32, :].bitcast(I32), src[16 + r : P : 32, :].bitcast(I32))
+
         src_list = lists.tile([P, J // GROUP], U16, name="src_list")
         dst_list = lists.tile([P, J // GROUP], U16, name="dst_list")
         nc.sync.dma_start(dst_list[:], offs2)
         nc.sync.dma_start(src_list[:], offs)
-        for q in range(4):
-            nc.sync.dma_start(
-                tab_sc[32 * q : 32 * q + 8, :].bitcast(I32), tab_scales[:, 4 * q : 4 * q + 4, :].bitcast(I32)
-            )
+        load_both(tab_sc, tab_scales)
         picked = {}
 
         def gather(name, window, edge_list, dtype, j0, j1, got=None, at=0):
@@ -120,21 +127,36 @@ def tile_list_msg_relu_none_kernel(
                 )
 
         raw = {(0, 0): [load_wt(0, 0, HALF, FIRST_AT)]}
-        load_rows(ws_sc_raw, ws_scales)
         tab_w = [load_tab(0)]
         ws_raw = held("ws_raw", [P, 2, R], U16)
         nc.sync.dma_start(ws_raw[:].bitcast(I32), ws_words.rearrange("a p x -> p a x").bitcast(I32))
+        load_both(ws_sc_raw, ws_scales)
         raw[0, 1] = [load_wt(0, HALF, HALF, SECOND_AT)]
         raw[1, 0] = [load_wt(1, 0, HALF, FIFTH_AT)]
-        tab_w.append(load_tab(1))
 
-        gather("dst_sc", tab_sc, dst_list, U8, 0, J)
-        src_sc = gather("src_sc0", tab_sc, src_list, U8, 0, J)
-        moved_sc = held("moved_sc", [P, J], U8)
-        for r in range(4):
-            nc.sync.dma_start(moved_sc[r:P:32, :].bitcast(I32), src_sc[4 + r : P : 32, :].bitcast(I32))
+        edge_sc = held("edge_sc", [P, 2 * J], U8)
+        moved_sc = held("moved_sc", [P, 2 * J], U8)
+        gather("dst_sc0", tab_sc, dst_list, U8, 0, J, edge_sc)
+        gather("src_sc0", tab_sc, src_list, U8, 0, J, edge_sc, J)
         for t in range(J // P):
-            picked["src_sc1", t] = (moved_sc, t * P)
+            picked["dst_sc1", t] = (moved_sc, t * P)
+            picked["src_sc1", t] = (moved_sc, J + t * P)
+
+        quantise_wt(0, 0)
+        ws_w = held("ws_w", [P, 4, 4, P], U16)
+        nc.scalar.copy(ws_w[:], ws_raw[:].rearrange("p a (b m t) -> p (a b) t m", b=2, t=4))
+        on_first = held("on_first", [P, 6 * CHUNK], U32, FIRST_AT)
+        gather("dst_w0", tab_w[0], dst_list, U32, 0, 2 * CHUNK, on_first)
+        ws_sc = [held("ws_sc%d" % a, [P, 2, 4, P], U8) for a in range(2)]
+        nc.vector.tensor_copy(ws_sc[0][:], ws_sc_raw[:].rearrange("p (b m t) -> p b t m", b=2, t=4))
+        gather("src_w0", tab_w[0], src_list, U32, 0, 2 * CHUNK, on_first, 2 * CHUNK)
+        gather("dst_w0", tab_w[0], dst_list, U32, 2 * CHUNK, J, on_first, 4 * CHUNK)
+        quantise_wt(0, 1)
+        gather("src_w0", tab_w[0], src_list, U32, 2 * CHUNK, J, held("on_second", [P, 2 * CHUNK], U32, SECOND_AT))
+        quantise_wt(1, 0)
+        move_up(moved_sc[:], edge_sc[:])
+        tab_w.append(load_tab(1))
+        move_up(ws_sc[1][:].rearrange("p b t m -> p (b t m)"), ws_sc[0][:].rearrange("p b t m -> p (b t m)"))
         raw[1, 1] = [load_wt(1, HALF, HALF // 2), load_wt(1, HALF + HALF // 2, HALF // 2, THIRD_AT)]
         wd_sc = held("wd_sc", [P, 2, N], U8)
         load_rows(wd_sc, wd_scales)
@@ -142,27 +164,13 @@ def tile_list_msg_relu_none_kernel(
         nc.sync.dma_start(wd_w[:].bitcast(I32), wd_words.rearrange("a p x -> p a x").bitcast(I32))
         gain = held("gain", [P, J], F32)
         nc.sync.dma_start(gain[:], wgo)
-
-        gather("dst_w0", tab_w[0], dst_list, U32, 0, 2 * CHUNK)
-        gather("src_w0", tab_w[0], src_list, U32, 0, 2 * CHUNK)
-        quantise_wt(0, 0)
-        ws_w = held("ws_w", [P, 4, 4, P], U16)
-        nc.scalar.copy(ws_w[:], ws_raw[:].rearrange("p a (b m t) -> p (a b) t m", b=2, t=4))
-        ws_sc = held("ws_sc", [P, 4, 4, P], U8)
-        nc.gpsimd.tensor_copy(ws_sc[:], ws_sc_raw[:].rearrange("p a (b m t) -> p (a b) t m", b=2, t=4))
-        gather("dst_w0", tab_w[0], dst_list, U32, 2 * CHUNK, J, held("on_first", [P, 2 * CHUNK], U32, FIRST_AT))
-        quantise_wt(0, 1)
-        gather("src_w0", tab_w[0], src_list, U32, 2 * CHUNK, J, held("on_second", [P, 2 * CHUNK], U32, SECOND_AT))
-        quantise_wt(1, 0)
         on_fifth = held("on_fifth", [P, 5 * CHUNK], U32, FIFTH_AT)
         gather("dst_w1", tab_w[1], dst_list, U32, 0, CHUNK, on_fifth)
         gather("src_w1", tab_w[1], src_list, U32, 0, CHUNK, on_fifth, CHUNK)
         gather("dst_w1", tab_w[1], dst_list, U32, 2 * CHUNK, J, on_fifth, 2 * CHUNK)
         gather("src_w1", tab_w[1], src_list, U32, 2 * CHUNK, 3 * CHUNK, on_fifth, 4 * CHUNK)
         quantise_wt(1, 1, 4, LAST_AT)
-        on_last = held("on_last", [P, CHUNK], U32, LAST_AT)
-        gather("dst_w1", tab_w[1], dst_list, U32, CHUNK, 2 * CHUNK, on_last)
-
+        gather("dst_w1", tab_w[1], dst_list, U32, CHUNK, 2 * CHUNK, held("on_last", [P, CHUNK], U32, LAST_AT))
 
         h_in = [held("h_in%d" % c, [P, 2, 2, P, 4], BF16, None if c else THIRD_AT) for c in range(CHUNKS)]
         h_w = [held("h_w%d" % c, [P, 2, CHUNK], U32) for c in range(CHUNKS)]
@@ -182,9 +190,9 @@ def tile_list_msg_relu_none_kernel(
                         cols = slice(t * P, (t + 1) * P)
                         if side == "dst":
                             lhs, lhs_sc = wt_w[a, b][:, cols].bitcast(FP8X4), wt_sc[a, b][:, cols]
-                            rhs_sc = edge_cols("dst_sc", tile, 4 * a)
+                            rhs_sc = edge_cols("dst_sc%d" % a, tile)
                         else:
-                            lhs, lhs_sc = ws_w[:, 2 * a + b, t, :].bitcast(FP4X4), ws_sc[:, 2 * a + b, t, :]
+                            lhs, lhs_sc = ws_w[:, 2 * a + b, t, :].bitcast(FP4X4), ws_sc[a][:, b, t, :]
                             rhs_sc = edge_cols("src_sc%d" % a, tile)
                         nc.tensor.matmul_mx(
                             out=banks[sum_banks[c][g]][:, cols],
@@ -243,8 +251,6 @@ def tile_list_msg_relu_none_kernel(
         first_layer(0, (2, 3), (2, 3))
         rectify(0, (2, 3))
         quantise_h(0, 1, 2)
-        placed.append(held("placed3", [P, T], F32, THIRD_AT + WORD * 2 * CHUNK))
-        nc.gpsimd.memset(placed[3][:], 0.0)
         on_third = held("on_third", [P, 2 * CHUNK], U32, THIRD_AT)
         gather("src_w1", tab_w[1], src_list, U32, CHUNK, 2 * CHUNK, on_third)
         gather("src_w1", tab_w[1], src_list, U32, 3 * CHUNK, J, on_third, CHUNK)

@@ -54,8 +54,8 @@ def tile_list_msg_relu_none_kernel(
 
         tab_sc = held("tab_sc", [P, T], U8)
         nc.gpsimd.memset(tab_sc[:].bitcast(I32), 0)
-        ws_sc_raw = held("ws_sc_raw", [P, R], U8)
-        nc.gpsimd.memset(ws_sc_raw[:].bitcast(I32), 0)
+        ws_sc_raw = held("ws_sc_raw", [P, 2, R], U8)
+        nc.gpsimd.memset(ws_sc_raw[:].rearrange("p a r -> p (a r)").bitcast(I32), 0)
 
         placed = [held("placed%d" % n, [P, T], F32) for n in range(N // P)]
         for page in placed:
@@ -115,7 +115,10 @@ def tile_list_msg_relu_none_kernel(
             for u, piece in enumerate(raw[a, b]):
                 dst = grouped[:, :, u * width : (u + 1) * width, :].rearrange("p t m i -> p m i t")
                 src = piece[:].rearrange("p i (m t) -> p m i t", t=4)
-                nc.scalar.activation(dst, src, COPY)
+                if u == 0:
+                    nc.scalar.activation(dst, src, COPY)
+                else:
+                    nc.vector.tensor_copy(dst, src)
             flat = grouped[:].rearrange("p t m i -> p (t m i)")
             width = HALF // parts
             for u in range(parts):
@@ -130,7 +133,7 @@ def tile_list_msg_relu_none_kernel(
         tab_w = [load_tab(0)]
         ws_raw = held("ws_raw", [P, 2, R], U16)
         nc.sync.dma_start(ws_raw[:].bitcast(I32), ws_words.rearrange("a p x -> p a x").bitcast(I32))
-        load_both(ws_sc_raw, ws_scales)
+        load_rows(ws_sc_raw, ws_scales)
         raw[0, 1] = [load_wt(0, HALF, HALF, SECOND_AT)]
         raw[1, 0] = [load_wt(1, 0, HALF, FIFTH_AT)]
 
@@ -142,35 +145,34 @@ def tile_list_msg_relu_none_kernel(
             picked["dst_sc1", t] = (moved_sc, t * P)
             picked["src_sc1", t] = (moved_sc, J + t * P)
 
+        gather("dst_w0", tab_w[0], dst_list, U32, 0, 2 * CHUNK)
+        gather("src_w0", tab_w[0], src_list, U32, 0, 2 * CHUNK)
         quantise_wt(0, 0)
         ws_w = held("ws_w", [P, 4, 4, P], U16)
         nc.scalar.copy(ws_w[:], ws_raw[:].rearrange("p a (b m t) -> p (a b) t m", b=2, t=4))
-        on_first = held("on_first", [P, 6 * CHUNK], U32, FIRST_AT)
-        gather("dst_w0", tab_w[0], dst_list, U32, 0, 2 * CHUNK, on_first)
-        ws_sc = [held("ws_sc%d" % a, [P, 2, 4, P], U8) for a in range(2)]
-        nc.vector.tensor_copy(ws_sc[0][:], ws_sc_raw[:].rearrange("p (b m t) -> p b t m", b=2, t=4))
-        gather("src_w0", tab_w[0], src_list, U32, 0, 2 * CHUNK, on_first, 2 * CHUNK)
-        gather("dst_w0", tab_w[0], dst_list, U32, 2 * CHUNK, J, on_first, 4 * CHUNK)
+        ws_sc = held("ws_sc", [P, 4, 4, P], U8, FIRST_AT + WORD * 2 * CHUNK)
+        nc.vector.tensor_copy(ws_sc[:], ws_sc_raw[:].rearrange("p a (b m t) -> p (a b) t m", b=2, t=4))
+        gather("dst_w0", tab_w[0], dst_list, U32, 2 * CHUNK, J, held("on_first", [P, 2 * CHUNK], U32, FIRST_AT))
         quantise_wt(0, 1)
         gather("src_w0", tab_w[0], src_list, U32, 2 * CHUNK, J, held("on_second", [P, 2 * CHUNK], U32, SECOND_AT))
         quantise_wt(1, 0)
-        move_up(moved_sc[:], edge_sc[:])
         tab_w.append(load_tab(1))
-        move_up(ws_sc[1][:].rearrange("p b t m -> p (b t m)"), ws_sc[0][:].rearrange("p b t m -> p (b t m)"))
-        raw[1, 1] = [load_wt(1, HALF, HALF // 2), load_wt(1, HALF + HALF // 2, HALF // 2, THIRD_AT)]
+        move_up(moved_sc[:], edge_sc[:])
+        raw[1, 1] = [load_wt(1, HALF, HALF // 2, THIRD_AT), load_wt(1, HALF + HALF // 2, HALF // 2)]
         wd_sc = held("wd_sc", [P, 2, N], U8)
         load_rows(wd_sc, wd_scales)
         wd_w = held("wd_w", [P, 2, 2 * N], U8)
         nc.sync.dma_start(wd_w[:].bitcast(I32), wd_words.rearrange("a p x -> p a x").bitcast(I32))
         gain = held("gain", [P, J], F32)
         nc.sync.dma_start(gain[:], wgo)
-        on_fifth = held("on_fifth", [P, 5 * CHUNK], U32, FIFTH_AT)
+        on_fifth = held("on_fifth", [P, 4 * CHUNK], U32, FIFTH_AT)
         gather("dst_w1", tab_w[1], dst_list, U32, 0, CHUNK, on_fifth)
         gather("src_w1", tab_w[1], src_list, U32, 0, CHUNK, on_fifth, CHUNK)
-        gather("dst_w1", tab_w[1], dst_list, U32, 2 * CHUNK, J, on_fifth, 2 * CHUNK)
-        gather("src_w1", tab_w[1], src_list, U32, 2 * CHUNK, 3 * CHUNK, on_fifth, 4 * CHUNK)
+        gather("dst_w1", tab_w[1], dst_list, U32, CHUNK, 3 * CHUNK, on_fifth, 2 * CHUNK)
         quantise_wt(1, 1, 4, LAST_AT)
-        gather("dst_w1", tab_w[1], dst_list, U32, CHUNK, 2 * CHUNK, held("on_last", [P, CHUNK], U32, LAST_AT))
+        on_last = held("on_last", [P, 2 * CHUNK], U32, LAST_AT)
+        gather("src_w1", tab_w[1], src_list, U32, CHUNK, 2 * CHUNK, on_last)
+        gather("dst_w1", tab_w[1], dst_list, U32, 3 * CHUNK, J, on_last, CHUNK)
 
         h_in = [held("h_in%d" % c, [P, 2, 2, P, 4], BF16, None if c else THIRD_AT) for c in range(CHUNKS)]
         h_w = [held("h_w%d" % c, [P, 2, CHUNK], U32) for c in range(CHUNKS)]
@@ -192,7 +194,7 @@ def tile_list_msg_relu_none_kernel(
                             lhs, lhs_sc = wt_w[a, b][:, cols].bitcast(FP8X4), wt_sc[a, b][:, cols]
                             rhs_sc = edge_cols("dst_sc%d" % a, tile)
                         else:
-                            lhs, lhs_sc = ws_w[:, 2 * a + b, t, :].bitcast(FP4X4), ws_sc[a][:, b, t, :]
+                            lhs, lhs_sc = ws_w[:, 2 * a + b, t, :].bitcast(FP4X4), ws_sc[:, 2 * a + b, t, :]
                             rhs_sc = edge_cols("src_sc%d" % a, tile)
                         nc.tensor.matmul_mx(
                             out=banks[sum_banks[c][g]][:, cols],
@@ -251,9 +253,7 @@ def tile_list_msg_relu_none_kernel(
         first_layer(0, (2, 3), (2, 3))
         rectify(0, (2, 3))
         quantise_h(0, 1, 2)
-        on_third = held("on_third", [P, 2 * CHUNK], U32, THIRD_AT)
-        gather("src_w1", tab_w[1], src_list, U32, CHUNK, 2 * CHUNK, on_third)
-        gather("src_w1", tab_w[1], src_list, U32, 3 * CHUNK, J, on_third, CHUNK)
+        gather("src_w1", tab_w[1], src_list, U32, 2 * CHUNK, J, held("on_third", [P, 2 * CHUNK], U32, THIRD_AT))
         send(0, 0, 0)
         first_layer(1, (0, 1), (2, 3))
         send(0, 1, 1)

@@ -25,6 +25,7 @@ CHUNKS = J // CHUNK
 BANKS = 8
 ALIGN = 64
 WORD = 4
+FIRST_LOW = (("dst", 0), ("src", 0), ("src", 1), ("dst", 1))
 STEPS = ((("dst", 0), ("src", 0), ("dst", 1), ("src", 1)), (("src", 0), ("dst", 0), ("src", 1), ("dst", 1)))
 RAW_BYTES = 4 * 4 * HALF
 FIRST_AT = 0
@@ -91,8 +92,8 @@ def tile_list_msg_relu_none_kernel(
         src_list = lists.tile([P, J // GROUP], U16, name="src_list")
         dst_list = lists.tile([P, J // GROUP], U16, name="dst_list")
         nc.sync.dma_start(dst_list[:], offs2)
-        nc.sync.dma_start(src_list[:], offs)
         load_both(tab_sc, tab_scales)
+        nc.sync.dma_start(src_list[:], offs)
         picked = {}
 
         def gather(name, window, edge_list, dtype, j0, j1, got=None, at=0):
@@ -155,21 +156,21 @@ def tile_list_msg_relu_none_kernel(
         gather("dst_w0", tab_w[0], dst_list, U32, 2 * CHUNK, J, held("on_first", [P, 2 * CHUNK], U32, FIRST_AT))
         quantise_wt(0, 1)
         gather("src_w0", tab_w[0], src_list, U32, 2 * CHUNK, J, held("on_second", [P, 2 * CHUNK], U32, SECOND_AT))
-        quantise_wt(1, 0)
         tab_w.append(load_tab(1))
         move_up(moved_sc[:], edge_sc[:])
-        raw[1, 1] = [load_wt(1, HALF, HALF // 2, THIRD_AT), load_wt(1, HALF + HALF // 2, HALF // 2)]
+        raw[1, 1] = [load_wt(1, HALF, HALF // 2, THIRD_AT), load_wt(1, HALF + HALF // 2, HALF // 2, LAST_AT)]
         wd_sc = held("wd_sc", [P, 2, N], U8)
         load_rows(wd_sc, wd_scales)
         wd_w = held("wd_w", [P, 2, 2 * N], U8)
         nc.sync.dma_start(wd_w[:].bitcast(I32), wd_words.rearrange("a p x -> p a x").bitcast(I32))
         gain = held("gain", [P, J], F32)
         nc.sync.dma_start(gain[:], wgo)
-        on_fifth = held("on_fifth", [P, 4 * CHUNK], U32, FIFTH_AT)
-        gather("dst_w1", tab_w[1], dst_list, U32, 0, CHUNK, on_fifth)
-        gather("src_w1", tab_w[1], src_list, U32, 0, CHUNK, on_fifth, CHUNK)
-        gather("dst_w1", tab_w[1], dst_list, U32, CHUNK, 3 * CHUNK, on_fifth, 2 * CHUNK)
-        quantise_wt(1, 1, 4, LAST_AT)
+        gather("src_w1", tab_w[1], src_list, U32, 0, CHUNK)
+        gather("dst_w1", tab_w[1], dst_list, U32, 0, CHUNK)
+        quantise_wt(1, 0)
+        on_fifth = held("on_fifth", [P, 2 * CHUNK], U32, FIFTH_AT)
+        gather("dst_w1", tab_w[1], dst_list, U32, CHUNK, 3 * CHUNK, on_fifth)
+        quantise_wt(1, 1, 4)
         on_last = held("on_last", [P, 2 * CHUNK], U32, LAST_AT)
         gather("src_w1", tab_w[1], src_list, U32, CHUNK, 2 * CHUNK, on_last)
         gather("dst_w1", tab_w[1], dst_list, U32, 3 * CHUNK, J, on_last, CHUNK)
@@ -188,7 +189,7 @@ def tile_list_msg_relu_none_kernel(
                 for t in range(4):
                     for g in groups:
                         b, tile = g // 2, 2 * c + g % 2
-                        side, a = STEPS[b][i]
+                        side, a = (STEPS[b] if b or c else FIRST_LOW)[i]
                         cols = slice(t * P, (t + 1) * P)
                         if side == "dst":
                             lhs, lhs_sc = wt_w[a, b][:, cols].bitcast(FP8X4), wt_sc[a, b][:, cols]
@@ -223,15 +224,16 @@ def tile_list_msg_relu_none_kernel(
             y = banks[bank]
             width = chunks * CHUNK
             for u in range(chunks):
-                for b in (1, 0):
+                order = (0, 1) if (c, n) == (0, 0) else (1, 0)
+                for b in order:
                     nc.tensor.matmul_mx(
                         out=y[:, u * CHUNK : (u + 1) * CHUNK],
                         lhsT=wd_w[:, b, 2 * P * n : 2 * P * (n + 1)].bitcast(FP4X4),
                         lhsT_scale=wd_sc[:, b, P * n : P * (n + 1)],
                         rhs=h_w[c + u][:, b, :].bitcast(FP8X4),
                         rhs_scale=h_sc[c + u][:, b, :],
-                        start=(b == 1),
-                        stop=(b == 0),
+                        start=(b == order[0]),
+                        stop=(b == order[1]),
                     )
             msg = held("msg%d%d" % (c, n), [P, width], F32)
             nc.scalar.copy(msg[:], y[:, 0:width])
@@ -247,10 +249,12 @@ def tile_list_msg_relu_none_kernel(
             for i in range(2):
                 for c in range(2):
                     first_layer(c, (2 * b, 2 * b + 1), (i,))
-        first_layer(0, (0, 1), (2, 3))
+        first_layer(0, (0, 1), (2,))
+        first_layer(0, (2, 3), (2,))
+        first_layer(0, (0, 1), (3,))
         rectify(0, (0, 1))
         quantise_h(0, 0, 1)
-        first_layer(0, (2, 3), (2, 3))
+        first_layer(0, (2, 3), (3,))
         rectify(0, (2, 3))
         quantise_h(0, 1, 2)
         gather("src_w1", tab_w[1], src_list, U32, 2 * CHUNK, J, held("on_third", [P, 2 * CHUNK], U32, THIRD_AT))
@@ -258,20 +262,22 @@ def tile_list_msg_relu_none_kernel(
         first_layer(1, (0, 1), (2, 3))
         send(0, 1, 1)
         first_layer(1, (2, 3), (2, 3))
-        for c in range(1, CHUNKS):
+        for c in range(1, CHUNKS - 1):
             rectify(c, range(4))
             quantise_h(c, 0, 2)
             send(c - 1, 2, sum_banks[c][3])
-            if c + 1 < CHUNKS:
-                send(c - 1, 3, sum_banks[c][2])
-                for g in range(2):
-                    first_layer(c + 1, (g,), range(4))
-            for n in range(2):
-                send(c, n, sum_banks[c][n])
-            if c + 1 < CHUNKS:
-                for g in range(2, 4):
-                    first_layer(c + 1, (g,), range(4))
-        send(3, 2, sum_banks[3][2])
-        send(2, 3, sum_banks[3][1], 2)
-        for n, page in enumerate(placed):
-            nc.sync.dma_start(out[n * P : (n + 1) * P, :], page[:])
+            send(c - 1, 3, sum_banks[c][2])
+            for g in range(3):
+                first_layer(c + 1, (g,), range(4))
+            for n in (0, 1) if c == 1 else (3,):
+                send(c, n, sum_banks[c][n % 3])
+            first_layer(c + 1, (3,), range(4))
+        rectify(3, range(4))
+        quantise_h(3, 0, 2)
+        send(2, 2, sum_banks[3][3])
+        send(3, 3, sum_banks[3][0])
+        send(3, 2, sum_banks[3][1])
+        send(2, 0, sum_banks[2][1], 2)
+        send(2, 1, sum_banks[3][2], 2)
+        for n in (3, 2, 0, 1):
+            nc.sync.dma_start(out[n * P : (n + 1) * P, :], placed[n][:])

@@ -25,8 +25,8 @@ CHUNKS = J // CHUNK
 BANKS = 8
 ALIGN = 64
 WORD = 4
-FIRST_LOW = (("dst", 0), ("src", 0), ("src", 1), ("dst", 1))
-STEPS = ((("dst", 0), ("src", 0), ("dst", 1), ("src", 1)), (("src", 0), ("dst", 0), ("src", 1), ("dst", 1)))
+FIRST_LOW = (("src", 0), ("dst", 0), ("dst", 1), ("src", 1))
+LATER = (("src", 0), ("dst", 0), ("dst", 1), ("src", 1))
 RAW_BYTES = 4 * 4 * HALF
 FIRST_AT = 0
 SECOND_AT = RAW_BYTES
@@ -112,14 +112,16 @@ def tile_list_msg_relu_none_kernel(
             grouped = held("grouped%d%d" % (a, b), [P, 4, P, 4], BF16, offset)
             wt_w[a, b] = held("wt_w%d%d" % (a, b), [P, HALF], U32)
             wt_sc[a, b] = held("wt_sc%d%d" % (a, b), [P, HALF], U8)
-            width = P // len(raw[a, b])
-            for u, piece in enumerate(raw[a, b]):
-                dst = grouped[:, :, u * width : (u + 1) * width, :].rearrange("p t m i -> p m i t")
-                src = piece[:].rearrange("p i (m t) -> p m i t", t=4)
-                if u == 0:
-                    nc.scalar.activation(dst, src, COPY)
-                else:
+            m0 = 0
+            for src, on_vector in raw[a, b]:
+                width = src.shape[2] // 4
+                dst = grouped[:, :, m0 : m0 + width, :].rearrange("p t m i -> p m i t")
+                src = src.rearrange("p i (m t) -> p m i t", t=4)
+                if on_vector:
                     nc.vector.tensor_copy(dst, src)
+                else:
+                    nc.scalar.activation(dst, src, COPY)
+                m0 = m0 + width
             flat = grouped[:].rearrange("p t m i -> p (t m i)")
             width = HALF // parts
             for u in range(parts):
@@ -130,13 +132,15 @@ def tile_list_msg_relu_none_kernel(
                     in_=flat[:, 4 * u * width : 4 * (u + 1) * width],
                 )
 
-        raw = {(0, 0): [load_wt(0, 0, HALF, FIRST_AT)]}
         tab_w = [load_tab(0)]
-        ws_raw = held("ws_raw", [P, 2, R], U16)
-        nc.sync.dma_start(ws_raw[:].bitcast(I32), ws_words.rearrange("a p x -> p a x").bitcast(I32))
+        ws_raw = [held("ws_raw%d" % a, [P, R], U16, None if a else LAST_AT) for a in range(2)]
+        nc.sync.dma_start(ws_raw[0][:].bitcast(I32), ws_words[0].bitcast(I32))
         load_rows(ws_sc_raw, ws_scales)
-        raw[0, 1] = [load_wt(0, HALF, HALF, SECOND_AT)]
-        raw[1, 0] = [load_wt(1, 0, HALF, FIFTH_AT)]
+        first = load_wt(0, 0, R, FIRST_AT)
+        second = load_wt(1, 0, R, THIRD_AT)
+        raw = {(0, 0): [(first[:, :, 0:512], False)], (0, 1): [(first[:, :, 512:896], True), (first[:, :, 896:1024], False)], (1, 0): [(second[:, :, 0:128], True), (second[:, :, 128:512], False)], (1, 1): [(second[:, :, 512:1024], True)]}
+        nc.sync.dma_start(ws_raw[1][:].bitcast(I32), ws_words[1].bitcast(I32))
+        tab_w.append(load_tab(1))
 
         edge_sc = held("edge_sc", [P, 2 * J], U8)
         moved_sc = held("moved_sc", [P, 2 * J], U8)
@@ -146,39 +150,41 @@ def tile_list_msg_relu_none_kernel(
             picked["dst_sc1", t] = (moved_sc, t * P)
             picked["src_sc1", t] = (moved_sc, J + t * P)
 
-        gather("dst_w0", tab_w[0], dst_list, U32, 0, 2 * CHUNK)
-        gather("src_w0", tab_w[0], src_list, U32, 0, 2 * CHUNK)
-        quantise_wt(0, 0)
-        ws_w = held("ws_w", [P, 4, 4, P], U16)
-        nc.scalar.copy(ws_w[:], ws_raw[:].rearrange("p a (b m t) -> p (a b) t m", b=2, t=4))
-        ws_sc = held("ws_sc", [P, 4, 4, P], U8, FIRST_AT + WORD * 2 * CHUNK)
-        nc.vector.tensor_copy(ws_sc[:], ws_sc_raw[:].rearrange("p a (b m t) -> p (a b) t m", b=2, t=4))
-        gather("dst_w0", tab_w[0], dst_list, U32, 2 * CHUNK, J, held("on_first", [P, 2 * CHUNK], U32, FIRST_AT))
-        quantise_wt(0, 1)
-        gather("src_w0", tab_w[0], src_list, U32, 2 * CHUNK, J, held("on_second", [P, 2 * CHUNK], U32, SECOND_AT))
-        tab_w.append(load_tab(1))
         move_up(moved_sc[:], edge_sc[:])
-        raw[1, 1] = [load_wt(1, HALF, HALF // 2, THIRD_AT), load_wt(1, HALF + HALF // 2, HALF // 2, LAST_AT)]
         wd_sc = held("wd_sc", [P, 2, N], U8)
         load_rows(wd_sc, wd_scales)
         wd_w = held("wd_w", [P, 2, 2 * N], U8)
         nc.sync.dma_start(wd_w[:].bitcast(I32), wd_words.rearrange("a p x -> p a x").bitcast(I32))
         gain = held("gain", [P, J], F32)
         nc.sync.dma_start(gain[:], wgo)
-        gather("src_w1", tab_w[1], src_list, U32, 0, CHUNK)
-        gather("dst_w1", tab_w[1], dst_list, U32, 0, CHUNK)
+        gather("src_w0", tab_w[0], src_list, U32, 0, 2 * CHUNK)
+        gather("dst_w0", tab_w[0], dst_list, U32, 0, 2 * CHUNK)
+        ws_w = held("ws_w", [P, 4, 4, P], U16)
+        nc.scalar.copy(ws_w[:, 0:2], ws_raw[0][:].rearrange("p (b m t) -> p b t m", b=2, t=4))
+        ws_sc = held("ws_sc", [P, 4, 4, P], U8)
+        nc.vector.tensor_copy(ws_sc[:], ws_sc_raw[:].rearrange("p a (b m t) -> p (a b) t m", b=2, t=4))
+        gather("src_w0", tab_w[0], src_list, U32, 2 * CHUNK, J)
+        gather("dst_w0", tab_w[0], dst_list, U32, 2 * CHUNK, J, held("on_ws", [P, 2 * CHUNK], U32, LAST_AT))
+        quantise_wt(0, 0)
+        quantise_wt(0, 1)
+        quantise_wt(1, 1)
         quantise_wt(1, 0)
-        on_fifth = held("on_fifth", [P, 2 * CHUNK], U32, FIFTH_AT)
-        gather("dst_w1", tab_w[1], dst_list, U32, CHUNK, 3 * CHUNK, on_fifth)
-        quantise_wt(1, 1, 4)
-        on_last = held("on_last", [P, 2 * CHUNK], U32, LAST_AT)
-        gather("src_w1", tab_w[1], src_list, U32, CHUNK, 2 * CHUNK, on_last)
-        gather("dst_w1", tab_w[1], dst_list, U32, 3 * CHUNK, J, on_last, CHUNK)
+        nc.scalar.copy(ws_w[:, 2:4], ws_raw[1][:].rearrange("p (b m t) -> p b t m", b=2, t=4))
+        for tile in range(2):
+            gather("dst_w1", tab_w[1], dst_list, U32, tile * P, (tile + 1) * P)
+            gather("src_w1", tab_w[1], src_list, U32, tile * P, (tile + 1) * P)
+        on_second = held("on_second", [P, 4 * CHUNK], U32, THIRD_AT)
+        gather("dst_w1", tab_w[1], dst_list, U32, CHUNK, J, on_second)
 
-        h_in = [held("h_in%d" % c, [P, 2, 2, P, 4], BF16, None if c else THIRD_AT) for c in range(CHUNKS)]
+        h_in = [
+            [held("h_in%d%d" % (c, b), [P, 2, P, 4], BF16, None if c else FIFTH_AT + (1 + b) * RAW_BYTES) for b in range(2)]
+            if c == 0
+            else held("h_in%d" % c, [P, 2, 2, P, 4], BF16)
+            for c in range(CHUNKS)
+        ]
         h_w = [held("h_w%d" % c, [P, 2, CHUNK], U32) for c in range(CHUNKS)]
         h_sc = [held("h_sc%d" % c, [P, 2, CHUNK], U8) for c in range(CHUNKS)]
-        sum_banks = ((0, 1, 2, 3), (4, 5, 6, 7), (2, 3, 0, 1), (6, 7, 4, 5))
+        sum_banks = ((0, 1, 2, 3), (4, 5, 6, 7), (0, 1, 2, 3), (6, 7, 4, 5))
 
         def edge_cols(name, tile, row=0):
             got, at = picked[name, tile]
@@ -189,7 +195,7 @@ def tile_list_msg_relu_none_kernel(
                 for t in range(4):
                     for g in groups:
                         b, tile = g // 2, 2 * c + g % 2
-                        side, a = (STEPS[b] if b or c else FIRST_LOW)[i]
+                        side, a = (LATER if c else FIRST_LOW)[i]
                         cols = slice(t * P, (t + 1) * P)
                         if side == "dst":
                             lhs, lhs_sc = wt_w[a, b][:, cols].bitcast(FP8X4), wt_sc[a, b][:, cols]
@@ -210,21 +216,23 @@ def tile_list_msg_relu_none_kernel(
         def rectify(c, groups):
             for g in groups:
                 nc.scalar.activation(
-                    h_in[c][:, g // 2, g % 2], banks[sum_banks[c][g]][:].rearrange("p (t j) -> p j t", t=4), RELU
+                    h_in[c][g // 2][:, g % 2] if c == 0 else h_in[c][:, g // 2, g % 2], banks[sum_banks[c][g]][:].rearrange("p (t j) -> p j t", t=4), RELU
                 )
 
         def quantise_h(c, b0, b1):
             nc.vector.quantize_mx(
                 out=h_w[c][:, b0:b1, :].rearrange("p b j -> p (b j)").bitcast(FP8X4),
                 scales=h_sc[c][:, b0:b1, :].rearrange("p b j -> p (b j)"),
-                in_=h_in[c][:, b0:b1].rearrange("p b e j t -> p (b e j t)"),
+                in_=h_in[c][b0][:].rearrange("p e j t -> p (e j t)")
+                if c == 0
+                else h_in[c][:, b0:b1].rearrange("p b e j t -> p (b e j t)"),
             )
 
         def send(c, n, bank, chunks=1):
             y = banks[bank]
             width = chunks * CHUNK
             for u in range(chunks):
-                order = (0, 1) if (c, n) == (0, 0) else (1, 0)
+                order = (1, 0)
                 for b in order:
                     nc.tensor.matmul_mx(
                         out=y[:, u * CHUNK : (u + 1) * CHUNK],
@@ -245,23 +253,25 @@ def tile_list_msg_relu_none_kernel(
                 MULT,
             )
 
-        for b in range(2):
+        for c in range(2):
             for i in range(2):
-                for c in range(2):
+                for b in range(2):
                     first_layer(c, (2 * b, 2 * b + 1), (i,))
-        first_layer(0, (0, 1), (2,))
-        first_layer(0, (2, 3), (2,))
-        first_layer(0, (0, 1), (3,))
-        rectify(0, (0, 1))
-        quantise_h(0, 0, 1)
-        first_layer(0, (2, 3), (3,))
-        rectify(0, (2, 3))
+        for g in (2, 3, 0, 1):
+            first_layer(0, (g,), (2, 3))
+            rectify(0, (g,))
         quantise_h(0, 1, 2)
-        gather("src_w1", tab_w[1], src_list, U32, 2 * CHUNK, J, held("on_third", [P, 2 * CHUNK], U32, THIRD_AT))
-        send(0, 0, 0)
-        first_layer(1, (0, 1), (2, 3))
-        send(0, 1, 1)
-        first_layer(1, (2, 3), (2, 3))
+        on_high = held("on_high", [P, CHUNK], U32, FIFTH_AT + 2 * RAW_BYTES)
+        gather("src_w1", tab_w[1], src_list, U32, 3 * CHUNK, J, on_high)
+        quantise_h(0, 0, 1)
+        on_third = held("on_third", [P, 2 * CHUNK], U32, FIFTH_AT + RAW_BYTES)
+        gather("src_w1", tab_w[1], src_list, U32, CHUNK, 2 * CHUNK, on_third)
+        gather("src_w1", tab_w[1], src_list, U32, 2 * CHUNK, 3 * CHUNK, on_third, CHUNK)
+        send(0, 0, 2)
+        send(0, 1, 3)
+        first_layer(1, range(4), (2,))
+        for g in range(4):
+            first_layer(1, (g,), (3,))
         for c in range(1, CHUNKS - 1):
             rectify(c, range(4))
             quantise_h(c, 0, 2)

@@ -27,6 +27,8 @@ ALIGN = 64
 WORD = 4
 FIRST_LOW = (("src", 0), ("dst", 0), ("dst", 1), ("src", 1))
 LATER = (("src", 0), ("dst", 0), ("dst", 1), ("src", 1))
+NARROW = 2
+SUM_BANKS = ((0, 1, 2, 3), (4, 5, 6, 7), (0, 1, 2, 3), (6, 7, 4, 5))
 RAW_BYTES = 4 * 4 * HALF
 FIRST_AT = 0
 SECOND_AT = RAW_BYTES
@@ -177,55 +179,60 @@ def tile_list_msg_relu_none_kernel(
         gather("dst_w1", tab_w[1], dst_list, U32, CHUNK, J, on_second)
 
         h_in = [
-            [held("h_in%d%d" % (c, b), [P, 2, P, 4], BF16, None if c else FIFTH_AT + (1 + b) * RAW_BYTES) for b in range(2)]
+            [held("h_in%d%d" % (c, b), [P, CHUNK, 4], BF16, None if c else FIFTH_AT + (1 + b) * RAW_BYTES) for b in range(2)]
             if c == 0
-            else held("h_in%d" % c, [P, 2, 2, P, 4], BF16)
+            else held("h_in%d" % c, [P, 2, CHUNK, 4], BF16)
             for c in range(CHUNKS)
         ]
         h_w = [held("h_w%d" % c, [P, 2, CHUNK], U32) for c in range(CHUNKS)]
         h_sc = [held("h_sc%d" % c, [P, 2, CHUNK], U8) for c in range(CHUNKS)]
-        sum_banks = ((0, 1, 2, 3), (4, 5, 6, 7), (0, 1, 2, 3), (6, 7, 4, 5))
 
-        def edge_cols(name, tile, row=0):
+        def edge_cols(name, tile, width):
             got, at = picked[name, tile]
-            return got[row:P, at : at + P]
+            return got[:, at : at + width]
 
         def first_layer(c, groups, steps):
+            width = P if c < NARROW else CHUNK
+            slices = HALF // width
             for i in steps:
-                for t in range(4):
+                for e in range(slices):
                     for g in groups:
-                        b, tile = g // 2, 2 * c + g % 2
+                        b = g // 2
                         side, a = (LATER if c else FIRST_LOW)[i]
+                        t = e if c < NARROW else 2 * (g % 2) + e
+                        tile = 2 * c + (g % 2 if c < NARROW else 0)
                         cols = slice(t * P, (t + 1) * P)
                         if side == "dst":
                             lhs, lhs_sc = wt_w[a, b][:, cols].bitcast(FP8X4), wt_sc[a, b][:, cols]
-                            rhs_sc = edge_cols("dst_sc%d" % a, tile)
                         else:
                             lhs, lhs_sc = ws_w[:, 2 * a + b, t, :].bitcast(FP4X4), ws_sc[:, 2 * a + b, t, :]
-                            rhs_sc = edge_cols("src_sc%d" % a, tile)
                         nc.tensor.matmul_mx(
-                            out=banks[sum_banks[c][g]][:, cols],
+                            out=banks[SUM_BANKS[c][g]][:, e * width : (e + 1) * width],
                             lhsT=lhs,
                             lhsT_scale=lhs_sc,
-                            rhs=edge_cols("%s_w%d" % (side, a), tile).bitcast(FP8X4),
-                            rhs_scale=rhs_sc,
-                            start=(i == 0 and t == 0),
-                            stop=(i == 3 and t == 3),
+                            rhs=edge_cols("%s_w%d" % (side, a), tile, width).bitcast(FP8X4),
+                            rhs_scale=edge_cols("%s_sc%d" % (side, a), tile, width),
+                            start=(i == 0 and e == 0),
+                            stop=(i == 3 and e == slices - 1),
                         )
 
         def rectify(c, groups):
             for g in groups:
-                nc.scalar.activation(
-                    h_in[c][g // 2][:, g % 2] if c == 0 else h_in[c][:, g // 2, g % 2], banks[sum_banks[c][g]][:].rearrange("p (t j) -> p j t", t=4), RELU
-                )
+                half = h_in[c][g // 2][:] if c == 0 else h_in[c][:, g // 2]
+                if c < NARROW:
+                    dst = half[:, P * (g % 2) : P * (g % 2 + 1), :]
+                else:
+                    dst = half[:, :, 2 * (g % 2) : 2 * (g % 2 + 1)]
+                sums = banks[SUM_BANKS[c][g]][:].rearrange("p (t j) -> p j t", t=4 if c < NARROW else 2)
+                nc.scalar.activation(dst, sums, RELU)
 
         def quantise_h(c, b0, b1):
             nc.vector.quantize_mx(
                 out=h_w[c][:, b0:b1, :].rearrange("p b j -> p (b j)").bitcast(FP8X4),
                 scales=h_sc[c][:, b0:b1, :].rearrange("p b j -> p (b j)"),
-                in_=h_in[c][b0][:].rearrange("p e j t -> p (e j t)")
+                in_=h_in[c][b0][:].rearrange("p j t -> p (j t)")
                 if c == 0
-                else h_in[c][:, b0:b1].rearrange("p b e j t -> p (b e j t)"),
+                else h_in[c][:, b0:b1].rearrange("p b j t -> p (b j t)"),
             )
 
         def send(c, n, bank, chunks=1):
@@ -275,19 +282,19 @@ def tile_list_msg_relu_none_kernel(
         for c in range(1, CHUNKS - 1):
             rectify(c, range(4))
             quantise_h(c, 0, 2)
-            send(c - 1, 2, sum_banks[c][3])
-            send(c - 1, 3, sum_banks[c][2])
+            send(c - 1, 2, SUM_BANKS[c][3])
+            send(c - 1, 3, SUM_BANKS[c][2])
             for g in range(3):
                 first_layer(c + 1, (g,), range(4))
             for n in (0, 1) if c == 1 else (3,):
-                send(c, n, sum_banks[c][n % 3])
+                send(c, n, SUM_BANKS[c][n % 3])
             first_layer(c + 1, (3,), range(4))
         rectify(3, range(4))
         quantise_h(3, 0, 2)
-        send(2, 2, sum_banks[3][3])
-        send(3, 3, sum_banks[3][0])
-        send(3, 2, sum_banks[3][1])
-        send(2, 0, sum_banks[2][1], 2)
-        send(2, 1, sum_banks[3][2], 2)
+        send(2, 2, SUM_BANKS[3][3])
+        send(3, 3, SUM_BANKS[3][0])
+        send(3, 2, SUM_BANKS[3][1])
+        send(2, 0, SUM_BANKS[2][1], 2)
+        send(2, 1, SUM_BANKS[3][2], 2)
         for n in (3, 2, 0, 1):
             nc.sync.dma_start(out[n * P : (n + 1) * P, :], placed[n][:])

@@ -28,7 +28,7 @@ WORD = 4
 FIRST_LOW = (("src", 0), ("dst", 0), ("dst", 1), ("src", 1))
 LATER = (("src", 0), ("dst", 0), ("dst", 1), ("src", 1))
 NARROW = 2
-SUM_BANKS = ((0, 1, 2, 3), (4, 5, 6, 7), (0, 1, 2, 3), (6, 7, 4, 5))
+SUM_BANKS = ((0, 1, 2, 3), (4, 5, 6, 7), (0, 1, 2, 3), (5, 6, 4, 7))
 RAW_BYTES = 4 * 4 * HALF
 FIRST_AT = 0
 SECOND_AT = RAW_BYTES
@@ -279,22 +279,20 @@ def tile_list_msg_relu_none_kernel(
         first_layer(1, range(4), (2,))
         for g in range(4):
             first_layer(1, (g,), (3,))
-        for c in range(1, CHUNKS - 1):
+        for c in range(1, CHUNKS):
             rectify(c, range(4))
             quantise_h(c, 0, 2)
-            send(c - 1, 2, SUM_BANKS[c][3])
-            send(c - 1, 3, SUM_BANKS[c][2])
-            for g in range(3):
-                first_layer(c + 1, (g,), range(4))
-            for n in (0, 1) if c == 1 else (3,):
-                send(c, n, SUM_BANKS[c][n % 3])
-            first_layer(c + 1, (3,), range(4))
-        rectify(3, range(4))
-        quantise_h(3, 0, 2)
-        send(2, 2, SUM_BANKS[3][3])
+            send(c - 1, 3, SUM_BANKS[c][1])
+            send(c - 1, 2, SUM_BANKS[c][2])
+            if c == 1:
+                send(c, 0, SUM_BANKS[c][0])
+                send(c, 1, SUM_BANKS[c][3])
+            if c + 1 < CHUNKS:
+                for g in range(4):
+                    first_layer(c + 1, (g,), range(4))
         send(3, 3, SUM_BANKS[3][0])
-        send(3, 2, SUM_BANKS[3][1])
-        send(2, 0, SUM_BANKS[2][1], 2)
+        send(3, 2, SUM_BANKS[3][3])
+        send(2, 0, SUM_BANKS[3][1], 2)
         send(2, 1, SUM_BANKS[3][2], 2)
         for n in (3, 2, 0, 1):
             nc.sync.dma_start(out[n * P : (n + 1) * P, :], placed[n][:])

@@ -25,8 +25,8 @@ CHUNKS = J // CHUNK
 BANKS = 8
 ALIGN = 64
 WORD = 4
-FIRST_LOW = (("src", 0), ("dst", 0), ("dst", 1), ("src", 1))
-LATER = (("src", 0), ("dst", 0), ("dst", 1), ("src", 1))
+FIRST_LOW = (("dst", 0), ("src", 0), ("dst", 1), ("src", 1))
+LATER = (("dst", 0), ("src", 0), ("dst", 1), ("src", 1))
 NARROW = 2
 SUM_BANKS = ((0, 1, 2, 3), (4, 5, 6, 7), (0, 1, 2, 3), (5, 6, 4, 7))
 RAW_BYTES = 4 * 4 * HALF
@@ -134,13 +134,14 @@ def tile_list_msg_relu_none_kernel(
                     in_=flat[:, 4 * u * width : 4 * (u + 1) * width],
                 )
 
+        first = load_wt(0, 0, HALF, FIRST_AT)
         tab_w = [load_tab(0)]
-        ws_raw = [held("ws_raw%d" % a, [P, R], U16, None if a else LAST_AT) for a in range(2)]
+        upper = load_wt(0, HALF, HALF, SECOND_AT)
+        ws_raw = [held("ws_raw%d" % a, [P, R], U16) for a in range(2)]
         nc.sync.dma_start(ws_raw[0][:].bitcast(I32), ws_words[0].bitcast(I32))
         load_rows(ws_sc_raw, ws_scales)
-        first = load_wt(0, 0, R, FIRST_AT)
         second = load_wt(1, 0, R, THIRD_AT)
-        raw = {(0, 0): [(first[:, :, 0:512], False)], (0, 1): [(first[:, :, 512:896], True), (first[:, :, 896:1024], False)], (1, 0): [(second[:, :, 0:128], True), (second[:, :, 128:512], False)], (1, 1): [(second[:, :, 512:1024], True)]}
+        raw = {(0, 0): [(first[:], False)], (0, 1): [(upper[:], False)], (1, 0): [(second[:, :, 0:128], True), (second[:, :, 128:512], False)], (1, 1): [(second[:, :, 512:1024], True)]}
         nc.sync.dma_start(ws_raw[1][:].bitcast(I32), ws_words[1].bitcast(I32))
         tab_w.append(load_tab(1))
 
@@ -159,16 +160,16 @@ def tile_list_msg_relu_none_kernel(
         nc.sync.dma_start(wd_w[:].bitcast(I32), wd_words.rearrange("a p x -> p a x").bitcast(I32))
         gain = held("gain", [P, J], F32)
         nc.sync.dma_start(gain[:], wgo)
-        gather("src_w0", tab_w[0], src_list, U32, 0, 2 * CHUNK)
         gather("dst_w0", tab_w[0], dst_list, U32, 0, 2 * CHUNK)
+        gather("src_w0", tab_w[0], src_list, U32, 0, 2 * CHUNK)
+        quantise_wt(0, 0)
+        quantise_wt(0, 1)
         ws_w = held("ws_w", [P, 4, 4, P], U16)
         nc.scalar.copy(ws_w[:, 0:2], ws_raw[0][:].rearrange("p (b m t) -> p b t m", b=2, t=4))
         ws_sc = held("ws_sc", [P, 4, 4, P], U8)
         nc.vector.tensor_copy(ws_sc[:], ws_sc_raw[:].rearrange("p a (b m t) -> p (a b) t m", b=2, t=4))
-        gather("src_w0", tab_w[0], src_list, U32, 2 * CHUNK, J)
-        gather("dst_w0", tab_w[0], dst_list, U32, 2 * CHUNK, J, held("on_ws", [P, 2 * CHUNK], U32, LAST_AT))
-        quantise_wt(0, 0)
-        quantise_wt(0, 1)
+        gather("dst_w0", tab_w[0], dst_list, U32, 2 * CHUNK, J, held("on_first", [P, 2 * CHUNK], U32, FIRST_AT))
+        gather("src_w0", tab_w[0], src_list, U32, 2 * CHUNK, J, held("on_upper", [P, 2 * CHUNK], U32, SECOND_AT))
         quantise_wt(1, 1)
         quantise_wt(1, 0)
         nc.scalar.copy(ws_w[:, 2:4], ws_raw[1][:].rearrange("p (b m t) -> p b t m", b=2, t=4))

@@ -110,10 +110,10 @@ def tile_list_msg_relu_none_kernel(
 
         wt_w, wt_sc = {}, {}
 
-        def quantise_wt(a, b, parts=1, offset=None):
+        def quantise_wt(a, b, parts=1, offset=None, between=None):
             grouped = held("grouped%d%d" % (a, b), [P, 4, P, 4], BF16, offset)
             wt_w[a, b] = held("wt_w%d%d" % (a, b), [P, HALF], U32)
-            wt_sc[a, b] = held("wt_sc%d%d" % (a, b), [P, HALF], U8)
+            wt_sc[a, b] = held("wt_sc%d%d" % (a, b), [P, HALF], U8, LAST_AT if (a, b) == (1, 0) else None)
             m0 = 0
             for src, on_vector in raw[a, b]:
                 width = src.shape[2] // 4
@@ -124,6 +124,8 @@ def tile_list_msg_relu_none_kernel(
                 else:
                     nc.scalar.activation(dst, src, COPY)
                 m0 = m0 + width
+            if between:
+                between()
             flat = grouped[:].rearrange("p t m i -> p (t m i)")
             width = HALF // parts
             for u in range(parts):
@@ -136,13 +138,13 @@ def tile_list_msg_relu_none_kernel(
 
         first = load_wt(0, 0, HALF, FIRST_AT)
         tab_w = [load_tab(0)]
-        upper = load_wt(0, HALF, HALF, SECOND_AT)
-        ws_raw = [held("ws_raw%d" % a, [P, R], U16) for a in range(2)]
+        ws_raw = [held("ws_raw0", [P, R], U16)] + [held("ws_raw1%d" % b, [P, HALF], U16, None if b else LAST_AT) for b in range(2)]
         nc.sync.dma_start(ws_raw[0][:].bitcast(I32), ws_words[0].bitcast(I32))
         load_rows(ws_sc_raw, ws_scales)
+        upper = load_wt(0, HALF, HALF, SECOND_AT)
+        nc.sync.dma_start(ws_raw[2][:].bitcast(I32), ws_words[1][:, R : 2 * R].bitcast(I32))
         second = load_wt(1, 0, R, THIRD_AT)
-        raw = {(0, 0): [(first[:], False)], (0, 1): [(upper[:], False)], (1, 0): [(second[:, :, 0:128], True), (second[:, :, 128:512], False)], (1, 1): [(second[:, :, 512:1024], True)]}
-        nc.sync.dma_start(ws_raw[1][:].bitcast(I32), ws_words[1].bitcast(I32))
+        raw = {(0, 0): [(first[:], False)], (0, 1): [(upper[:], False)], (1, 0): [(second[:, :, 0:128], True), (second[:, :, 128:512], False)], (1, 1): [(second[:, :, 512:896], True), (second[:, :, 896:1024], False)]}
         tab_w.append(load_tab(1))
 
         edge_sc = held("edge_sc", [P, 2 * J], U8)
@@ -153,11 +155,12 @@ def tile_list_msg_relu_none_kernel(
             picked["dst_sc1", t] = (moved_sc, t * P)
             picked["src_sc1", t] = (moved_sc, J + t * P)
 
+        nc.sync.dma_start(ws_raw[1][:].bitcast(I32), ws_words[1][:, 0:R].bitcast(I32))
         move_up(moved_sc[:], edge_sc[:])
         wd_sc = held("wd_sc", [P, 2, N], U8)
-        load_rows(wd_sc, wd_scales)
         wd_w = held("wd_w", [P, 2, 2 * N], U8)
         nc.sync.dma_start(wd_w[:].bitcast(I32), wd_words.rearrange("a p x -> p a x").bitcast(I32))
+        load_rows(wd_sc, wd_scales)
         gain = held("gain", [P, J], F32)
         nc.sync.dma_start(gain[:], wgo)
         gather("dst_w0", tab_w[0], dst_list, U32, 0, 2 * CHUNK)
@@ -168,16 +171,19 @@ def tile_list_msg_relu_none_kernel(
         nc.scalar.copy(ws_w[:, 0:2], ws_raw[0][:].rearrange("p (b m t) -> p b t m", b=2, t=4))
         ws_sc = held("ws_sc", [P, 4, 4, P], U8)
         nc.vector.tensor_copy(ws_sc[:], ws_sc_raw[:].rearrange("p a (b m t) -> p (a b) t m", b=2, t=4))
-        gather("dst_w0", tab_w[0], dst_list, U32, 2 * CHUNK, J, held("on_first", [P, 2 * CHUNK], U32, FIRST_AT))
-        gather("src_w0", tab_w[0], src_list, U32, 2 * CHUNK, J, held("on_upper", [P, 2 * CHUNK], U32, SECOND_AT))
+        on_first = held("on_first", [P, J], U32, FIRST_AT)
+        gather("dst_w0", tab_w[0], dst_list, U32, 2 * CHUNK, J, on_first)
+        gather("src_w0", tab_w[0], src_list, U32, 2 * CHUNK, J, on_first, 2 * CHUNK)
+        nc.scalar.copy(ws_w[:, 3], ws_raw[2][:].rearrange("p (m t) -> p t m", t=4))
         quantise_wt(1, 1)
-        quantise_wt(1, 0)
-        nc.scalar.copy(ws_w[:, 2:4], ws_raw[1][:].rearrange("p (b m t) -> p b t m", b=2, t=4))
+        quantise_wt(1, 0, between=lambda: nc.scalar.copy(ws_w[:, 2], ws_raw[1][:].rearrange("p (m t) -> p t m", t=4)))
         for tile in range(2):
             gather("dst_w1", tab_w[1], dst_list, U32, tile * P, (tile + 1) * P)
             gather("src_w1", tab_w[1], src_list, U32, tile * P, (tile + 1) * P)
-        on_second = held("on_second", [P, 4 * CHUNK], U32, THIRD_AT)
-        gather("dst_w1", tab_w[1], dst_list, U32, CHUNK, J, on_second)
+        on_second = held("on_second", [P, 4 * CHUNK], U32, LAST_AT + HALF)
+        gather("dst_w1", tab_w[1], dst_list, U32, CHUNK, 2 * CHUNK, on_second)
+        gather("dst_w1", tab_w[1], dst_list, U32, 2 * CHUNK, J, on_second, CHUNK)
+        gather("src_w1", tab_w[1], src_list, U32, 3 * CHUNK, J, on_second, 3 * CHUNK)
 
         h_in = [
             [held("h_in%d%d" % (c, b), [P, CHUNK, 4], BF16, None if c else FIFTH_AT + (1 + b) * RAW_BYTES) for b in range(2)]
@@ -240,7 +246,7 @@ def tile_list_msg_relu_none_kernel(
             y = banks[bank]
             width = chunks * CHUNK
             for u in range(chunks):
-                order = (1, 0)
+                order = (0, 1)
                 for b in order:
                     nc.tensor.matmul_mx(
                         out=y[:, u * CHUNK : (u + 1) * CHUNK],
@@ -261,16 +267,14 @@ def tile_list_msg_relu_none_kernel(
                 MULT,
             )
 
-        for c in range(2):
+        for b in range(2):
             for i in range(2):
-                for b in range(2):
+                for c in range(2):
                     first_layer(c, (2 * b, 2 * b + 1), (i,))
         for g in (2, 3, 0, 1):
             first_layer(0, (g,), (2, 3))
             rectify(0, (g,))
         quantise_h(0, 1, 2)
-        on_high = held("on_high", [P, CHUNK], U32, FIFTH_AT + 2 * RAW_BYTES)
-        gather("src_w1", tab_w[1], src_list, U32, 3 * CHUNK, J, on_high)
         quantise_h(0, 0, 1)
         on_third = held("on_third", [P, 2 * CHUNK], U32, FIFTH_AT + RAW_BYTES)
         gather("src_w1", tab_w[1], src_list, U32, CHUNK, 2 * CHUNK, on_third)

@@ -13,7 +13,6 @@ U16 = mybir.dt.uint16
 U8 = mybir.dt.uint8
 FP8X4 = mybir.dt.float8_e4m3fn_x4
 FP4X4 = mybir.dt.float4_e2m1fn_x4
-COPY = mybir.ActivationFunctionType.Copy
 RELU = mybir.ActivationFunctionType.Relu
 MULT = mybir.AluOpType.mult
 
@@ -117,12 +116,12 @@ def tile_list_msg_relu_none_kernel(
             m0 = 0
             for src, on_vector in raw[a, b]:
                 width = src.shape[2] // 4
-                dst = grouped[:, :, m0 : m0 + width, :].rearrange("p t m i -> p m i t")
-                src = src.rearrange("p i (m t) -> p m i t", t=4)
+                dst = grouped[:, :, m0 : m0 + width, :].rearrange("p t m (h e) -> p m h t e", e=2)
+                src = src.rearrange("p (h e) (m t) -> p m h t e", e=2, t=4)
                 if on_vector:
                     nc.vector.tensor_copy(dst, src)
                 else:
-                    nc.scalar.activation(dst, src, COPY)
+                    nc.scalar.copy(dst, src)
                 m0 = m0 + width
             if between:
                 between()

from contextlib import ExitStack

import concourse.mybir as mybir

K, R, N, T, J = 1024, 1024, 512, 2048, 1024
FLOPS = 2 * (2 * K * R * J + R * N * J)

F32 = mybir.dt.float32
BF16 = mybir.dt.bfloat16
I32 = mybir.dt.int32
U32 = mybir.dt.uint32
U16 = mybir.dt.uint16
U8 = mybir.dt.uint8
FP8X4 = mybir.dt.float8_e4m3fn_x4
FP4X4 = mybir.dt.float4_e2m1fn_x4
RELU = mybir.ActivationFunctionType.Relu
MULT = mybir.AluOpType.mult

P = 128
HALF = 512
GROUP = 16
CHUNK = 256
CHUNKS = J // CHUNK
BANKS = 8
ALIGN = 64
WORD = 4
FIRST_LOW = (("dst", 0), ("src", 0), ("dst", 1), ("src", 1))
LATER = (("dst", 0), ("src", 0), ("dst", 1), ("src", 1))
NARROW = 2
SUM_BANKS = ((0, 1, 2, 3), (4, 5, 6, 7), (0, 1, 2, 3), (5, 6, 4, 7))
RAW_BYTES = 4 * 4 * HALF
FIRST_AT = 0
SECOND_AT = RAW_BYTES
LAST_AT = 2 * RAW_BYTES
THIRD_AT = 3 * RAW_BYTES
FOURTH_AT = 4 * RAW_BYTES
FIFTH_AT = 5 * RAW_BYTES


def tile_list_msg_relu_none_kernel(
    tc, tab_words, tab_scales, ws_words, ws_scales, wt, wd_words, wd_scales, wgo, offs, offs2, out
):
    nc = tc.nc
    with ExitStack() as ctx:
        lists = ctx.enter_context(tc.tile_pool(name="lists", bufs=1))
        keep = ctx.enter_context(tc.tile_pool(name="keep", bufs=1))
        shared = ctx.enter_context(tc.tile_pool(name="shared", bufs=1))
        psum = ctx.enter_context(tc.psum_pool(name="psum", bufs=1))

        def held(name, shape, dtype, offset=None):
            if offset is None:
                return keep.tile(shape, dtype, name=name, align_bytes=ALIGN)
            return shared.tile(shape, dtype, name=name, align_bytes=ALIGN, offset=offset)

        banks = [psum.tile([P, HALF], F32, name="bank%d" % i) for i in range(BANKS)]

        tab_sc = held("tab_sc", [P, T], U8)
        nc.gpsimd.memset(tab_sc[:].bitcast(I32), 0)
        ws_sc_raw = held("ws_sc_raw", [P, 2, R], U8)
        nc.gpsimd.memset(ws_sc_raw[:].rearrange("p a r -> p (a r)").bitcast(I32), 0)

        placed = [held("placed%d" % n, [P, T], F32) for n in range(N // P)]
        for page in placed:
            nc.gpsimd.memset(page[:], 0.0)

        def load_tab(a):
            words = held("tab_w%d" % a, [P, T], U32)
            nc.sync.dma_start(words[:].bitcast(I32), tab_words[a].rearrange("p t i -> p (t i)").bitcast(I32))
            return words

        def load_wt(a, c0, width, offset=None):
            piece = held("wt_raw%d_%d" % (a, c0), [P, 4, width], F32, offset)
            rows = wt[a * HALF : (a + 1) * HALF, c0 : c0 + width]
            nc.sync.dma_start(piece[:], rows.rearrange("(p i) c -> p i c", i=4))
            return piece

        def load_rows(planes, rows):
            for r in range(4):
                nc.sync.dma_start(
                    planes[r:P:32, :, :].bitcast(I32), rows[:, r:16:4, :].rearrange("a q n -> q a n").bitcast(I32)
                )

        def load_both(planes, rows):
            for r in range(4):
                nc.sync.dma_start(
                    planes[r:P:16, :].bitcast(I32), rows[:, r:16:4, :].rearrange("a q n -> q a n").bitcast(I32)
                )

        def move_up(dst, src):
            for r in range(4):
                nc.sync.dma_start(dst[r:P:32, :].bitcast(I32), src[16 + r : P : 32, :].bitcast(I32))

        src_list = lists.tile([P, J // GROUP], U16, name="src_list")
        dst_list = lists.tile([P, J // GROUP], U16, name="dst_list")
        nc.sync.dma_start(dst_list[:], offs2)
        load_both(tab_sc, tab_scales)
        nc.sync.dma_start(src_list[:], offs)
        picked = {}

        def gather(name, window, edge_list, dtype, j0, j1, got=None, at=0):
            if got is None:
                got = held("%s_%d" % (name, j0), [P, j1 - j0], dtype)
            nc.vector.tensor_copy(
                got[:, at : at + j1 - j0], window[:].indirect(edge_list[:, j0 // GROUP : j1 // GROUP])
            )
            for t in range(j0 // P, j1 // P):
                picked[name, t] = (got, at + t * P - j0)
            return got

        wt_w, wt_sc = {}, {}

        def quantise_wt(a, b, parts=1, offset=None, between=None):
            grouped = held("grouped%d%d" % (a, b), [P, 4, P, 4], BF16, offset)
            wt_w[a, b] = held("wt_w%d%d" % (a, b), [P, HALF], U32)
            wt_sc[a, b] = held("wt_sc%d%d" % (a, b), [P, HALF], U8, LAST_AT if (a, b) == (1, 0) else None)
            m0 = 0
            for src, on_vector in raw[a, b]:
                width = src.shape[2] // 4
                dst = grouped[:, :, m0 : m0 + width, :].rearrange("p t m (h e) -> p m h t e", e=2)
                src = src.rearrange("p (h e) (m t) -> p m h t e", e=2, t=4)
                if on_vector:
                    nc.vector.tensor_copy(dst, src)
                else:
                    nc.scalar.copy(dst, src)
                m0 = m0 + width
            if between:
                between()
            flat = grouped[:].rearrange("p t m i -> p (t m i)")
            width = HALF // parts
            for u in range(parts):
                cols = slice(u * width, (u + 1) * width)
                nc.vector.quantize_mx(
                    out=wt_w[a, b][:, cols].bitcast(FP8X4),
                    scales=wt_sc[a, b][:, cols],
                    in_=flat[:, 4 * u * width : 4 * (u + 1) * width],
                )

        first = load_wt(0, 0, HALF, FIRST_AT)
        tab_w = [load_tab(0)]
        ws_raw = [held("ws_raw0", [P, R], U16)] + [held("ws_raw1%d" % b, [P, HALF], U16, None if b else LAST_AT) for b in range(2)]
        nc.sync.dma_start(ws_raw[0][:].bitcast(I32), ws_words[0].bitcast(I32))
        load_rows(ws_sc_raw, ws_scales)
        upper = load_wt(0, HALF, HALF, SECOND_AT)
        nc.sync.dma_start(ws_raw[2][:].bitcast(I32), ws_words[1][:, R : 2 * R].bitcast(I32))
        second = load_wt(1, 0, R, THIRD_AT)
        raw = {(0, 0): [(first[:], False)], (0, 1): [(upper[:], False)], (1, 0): [(second[:, :, 0:128], True), (second[:, :, 128:512], False)], (1, 1): [(second[:, :, 512:896], True), (second[:, :, 896:1024], False)]}
        tab_w.append(load_tab(1))

        edge_sc = held("edge_sc", [P, 2 * J], U8)
        moved_sc = held("moved_sc", [P, 2 * J], U8)
        gather("dst_sc0", tab_sc, dst_list, U8, 0, J, edge_sc)
        gather("src_sc0", tab_sc, src_list, U8, 0, J, edge_sc, J)
        for t in range(J // P):
            picked["dst_sc1", t] = (moved_sc, t * P)
            picked["src_sc1", t] = (moved_sc, J + t * P)

        nc.sync.dma_start(ws_raw[1][:].bitcast(I32), ws_words[1][:, 0:R].bitcast(I32))
        move_up(moved_sc[:], edge_sc[:])
        wd_sc = held("wd_sc", [P, 2, N], U8)
        wd_w = held("wd_w", [P, 2, 2 * N], U8)
        nc.sync.dma_start(wd_w[:].bitcast(I32), wd_words.rearrange("a p x -> p a x").bitcast(I32))
        load_rows(wd_sc, wd_scales)
        gain = held("gain", [P, J], F32)
        nc.sync.dma_start(gain[:], wgo)
        gather("dst_w0", tab_w[0], dst_list, U32, 0, 2 * CHUNK)
        gather("src_w0", tab_w[0], src_list, U32, 0, 2 * CHUNK)
        quantise_wt(0, 0)
        quantise_wt(0, 1)
        ws_w = held("ws_w", [P, 4, 4, P], U16)
        nc.scalar.copy(ws_w[:, 0:2], ws_raw[0][:].rearrange("p (b m t) -> p b t m", b=2, t=4))
        ws_sc = held("ws_sc", [P, 4, 4, P], U8)
        nc.vector.tensor_copy(ws_sc[:], ws_sc_raw[:].rearrange("p a (b m t) -> p (a b) t m", b=2, t=4))
        on_first = held("on_first", [P, J], U32, FIRST_AT)
        gather("dst_w0", tab_w[0], dst_list, U32, 2 * CHUNK, J, on_first)
        gather("src_w0", tab_w[0], src_list, U32, 2 * CHUNK, J, on_first, 2 * CHUNK)
        nc.scalar.copy(ws_w[:, 3], ws_raw[2][:].rearrange("p (m t) -> p t m", t=4))
        quantise_wt(1, 1)
        quantise_wt(1, 0, between=lambda: nc.scalar.copy(ws_w[:, 2], ws_raw[1][:].rearrange("p (m t) -> p t m", t=4)))
        for tile in range(2):
            gather("dst_w1", tab_w[1], dst_list, U32, tile * P, (tile + 1) * P)
            gather("src_w1", tab_w[1], src_list, U32, tile * P, (tile + 1) * P)
        on_second = held("on_second", [P, 4 * CHUNK], U32, LAST_AT + HALF)
        gather("dst_w1", tab_w[1], dst_list, U32, CHUNK, 2 * CHUNK, on_second)
        gather("dst_w1", tab_w[1], dst_list, U32, 2 * CHUNK, J, on_second, CHUNK)
        gather("src_w1", tab_w[1], src_list, U32, 3 * CHUNK, J, on_second, 3 * CHUNK)

        h_in = [
            [held("h_in%d%d" % (c, b), [P, CHUNK, 4], BF16, None if c else FIFTH_AT + (1 + b) * RAW_BYTES) for b in range(2)]
            if c == 0
            else held("h_in%d" % c, [P, 2, CHUNK, 4], BF16)
            for c in range(CHUNKS)
        ]
        h_w = [held("h_w%d" % c, [P, 2, CHUNK], U32) for c in range(CHUNKS)]
        h_sc = [held("h_sc%d" % c, [P, 2, CHUNK], U8) for c in range(CHUNKS)]

        def edge_cols(name, tile, width):
            got, at = picked[name, tile]
            return got[:, at : at + width]

        def first_layer(c, groups, steps):
            width = P if c < NARROW else CHUNK
            slices = HALF // width
            for i in steps:
                for e in range(slices):
                    for g in groups:
                        b = g // 2
                        side, a = (LATER if c else FIRST_LOW)[i]
                        t = e if c < NARROW else 2 * (g % 2) + e
                        tile = 2 * c + (g % 2 if c < NARROW else 0)
                        cols = slice(t * P, (t + 1) * P)
                        if side == "dst":
                            lhs, lhs_sc = wt_w[a, b][:, cols].bitcast(FP8X4), wt_sc[a, b][:, cols]
                        else:
                            lhs, lhs_sc = ws_w[:, 2 * a + b, t, :].bitcast(FP4X4), ws_sc[:, 2 * a + b, t, :]
                        nc.tensor.matmul_mx(
                            out=banks[SUM_BANKS[c][g]][:, e * width : (e + 1) * width],
                            lhsT=lhs,
                            lhsT_scale=lhs_sc,
                            rhs=edge_cols("%s_w%d" % (side, a), tile, width).bitcast(FP8X4),
                            rhs_scale=edge_cols("%s_sc%d" % (side, a), tile, width),
                            start=(i == 0 and e == 0),
                            stop=(i == 3 and e == slices - 1),
                        )

        def rectify(c, groups):
            for g in groups:
                half = h_in[c][g // 2][:] if c == 0 else h_in[c][:, g // 2]
                if c < NARROW:
                    dst = half[:, P * (g % 2) : P * (g % 2 + 1), :]
                else:
                    dst = half[:, :, 2 * (g % 2) : 2 * (g % 2 + 1)]
                sums = banks[SUM_BANKS[c][g]][:].rearrange("p (t j) -> p j t", t=4 if c < NARROW else 2)
                nc.scalar.activation(dst, sums, RELU)

        def quantise_h(c, b0, b1):
            nc.vector.quantize_mx(
                out=h_w[c][:, b0:b1, :].rearrange("p b j -> p (b j)").bitcast(FP8X4),
                scales=h_sc[c][:, b0:b1, :].rearrange("p b j -> p (b j)"),
                in_=h_in[c][b0][:].rearrange("p j t -> p (j t)")
                if c == 0
                else h_in[c][:, b0:b1].rearrange("p b j t -> p (b j t)"),
            )

        def send(c, n, bank, chunks=1):
            y = banks[bank]
            width = chunks * CHUNK
            for u in range(chunks):
                order = (0, 1)
                for b in order:
                    nc.tensor.matmul_mx(
                        out=y[:, u * CHUNK : (u + 1) * CHUNK],
                        lhsT=wd_w[:, b, 2 * P * n : 2 * P * (n + 1)].bitcast(FP4X4),
                        lhsT_scale=wd_sc[:, b, P * n : P * (n + 1)],
                        rhs=h_w[c + u][:, b, :].bitcast(FP8X4),
                        rhs_scale=h_sc[c + u][:, b, :],
                        start=(b == order[0]),
                        stop=(b == order[1]),
                    )
            msg = held("msg%d%d" % (c, n), [P, width], F32)
            nc.scalar.copy(msg[:], y[:, 0:width])
            j0 = c * CHUNK
            nc.vector.tensor_tensor(
                placed[n][:].indirect(dst_list[:, j0 // GROUP : (j0 + width) // GROUP]),
                msg[:],
                gain[:, j0 : j0 + width],
                MULT,
            )

        for b in range(2):
            for i in range(2):
                for c in range(2):
                    first_layer(c, (2 * b, 2 * b + 1), (i,))
        for g in (2, 3, 0, 1):
            first_layer(0, (g,), (2, 3))
            rectify(0, (g,))
        quantise_h(0, 1, 2)
        quantise_h(0, 0, 1)
        on_third = held("on_third", [P, 2 * CHUNK], U32, FIFTH_AT + RAW_BYTES)
        gather("src_w1", tab_w[1], src_list, U32, CHUNK, 2 * CHUNK, on_third)
        gather("src_w1", tab_w[1], src_list, U32, 2 * CHUNK, 3 * CHUNK, on_third, CHUNK)
        send(0, 0, 2)
        send(0, 1, 3)
        first_layer(1, range(4), (2,))
        for g in range(4):
            first_layer(1, (g,), (3,))
        for c in range(1, CHUNKS):
            rectify(c, range(4))
            quantise_h(c, 0, 2)
            send(c - 1, 3, SUM_BANKS[c][1])
            send(c - 1, 2, SUM_BANKS[c][2])
            if c == 1:
                send(c, 0, SUM_BANKS[c][0])
                send(c, 1, SUM_BANKS[c][3])
            if c + 1 < CHUNKS:
                for g in range(4):
                    first_layer(c + 1, (g,), range(4))
        send(3, 3, SUM_BANKS[3][0])
        send(3, 2, SUM_BANKS[3][3])
        send(2, 0, SUM_BANKS[3][1], 2)
        send(2, 1, SUM_BANKS[3][2], 2)
        for n in (3, 2, 0, 1):
            nc.sync.dma_start(out[n * P : (n + 1) * P, :], placed[n][:])
